import numpy as np, ml_dtypes
CORES = [23,119,17,113]
N = 4
import mx_ref
BF = ml_dtypes.bfloat16
def gentries(a):
    return np.ascontiguousarray(a.reshape(8, 16, -1).transpose(0, 2, 1)).reshape(8, -1)
def gtable(e):
    e = np.asarray(e); return np.ascontiguousarray(e.reshape(8, -1, 16).transpose(0, 2, 1)).reshape(128, -1).astype(np.int32)
def gcols(t, e):
    v = np.concatenate([t.reshape(8, 16, -1, 4), np.zeros((8, 16, 1, 4), BF)], axis=2)
    return np.ascontiguousarray(np.stack([v[g][:, e[g]] for g in range(8)])).reshape(128, -1)
def tile(rs):
    return np.stack(rs, axis=2).reshape(128, -1).astype(BF)
def cut(t, i, w=512):
    return t[:, w * i:w * i + w]
def pick(q, e):
    c = np.concatenate([q[0].reshape(128, -1, 4), np.zeros((128, 1, 4), np.uint8)], axis=1); s = np.concatenate([q[1], np.ones((16, 1), np.uint8)], axis=1)
    return (np.ascontiguousarray(c[:, e].reshape(128, -1)), np.ascontiguousarray(s[:, e]))
def join(*qs):
    return (np.concatenate([q[0] for q in qs], axis=1), np.concatenate([q[1] for q in qs], axis=1))
def put(q, e, v):
    c, s = q[0].reshape(128, -1, 4).copy(), q[1].copy(); c[:, e] = v[0].reshape(128, -1, 4); s[:, e] = v[1]
    return (c.reshape(128, -1), s)
def pk(c, s):
    return (np.ascontiguousarray(c), mx_ref.live(s))
def emit(q):
    return q[0], q[1]
def packed(v, rng):
    q = [mx_ref.quantize(np.ascontiguousarray(v[r])) for r in range(N)]
    return np.stack([a for a, b in q]), np.stack([mx_ref.plane(b, rng) for a, b in q])
def values_of_codes():
    e, c = np.zeros((128, 128, 4), np.float32), np.zeros((128, 2, 4), np.uint8)
    e[np.arange(128), np.arange(128), 0] = 1
    c[:127, :, 0] = np.arange(256).reshape(2, 128).T[:127]
    return mx_ref.matmul(mx_ref.quantize(e.reshape(128, 512).astype(BF)), (c.reshape(128, 8), np.full((16, 2), 127, np.uint8))).T.reshape(-1).astype(np.float64)
CODE_VALUE, SCALE_VALUE = values_of_codes(), 2.0 ** (np.arange(256) - 127.0)
def decode(q):
    return (CODE_VALUE[q[0]].reshape(16, 8, -1, 4) * SCALE_VALUE[q[1]][:, None, :, None] + 0.0).reshape(128, -1).astype(np.float32)
def f(rng, *shape):
    return mx_ref.flush((rng.standard_normal(shape, dtype=np.float32) * np.exp2(rng.integers(-2, 3, shape[:-1] + (1,)))).astype(BF))
def wide(rng, *shape, cols=0):
    v = rng.standard_normal(shape, dtype=np.float32) * np.exp2(rng.integers(-12, 13, shape)).astype(np.float32)
    if cols: v *= np.repeat(np.exp2(rng.integers(-cols, cols + 1, shape[:-2] + (1, shape[-1] // 4))) * (rng.random(shape[:-2] + (1, shape[-1] // 4)) > 0.0625), 4, axis=-1).astype(np.float32)
    return mx_ref.flush(v.astype(BF))
C, K, R = 384, 192, 3
def living(z):
    return np.sort(np.argsort(-(z[::16] + np.float32(0.0)), axis=1, kind="stable")[:, :K], axis=1)
def ancestors(p, e, alive):
    to = np.where(alive, np.arange(C), p)
    for k in range(9): to = np.take_along_axis(to, to, axis=1)
    a = np.take_along_axis(to, np.take_along_axis(p, e, axis=1), axis=1)
    return np.where(np.take_along_axis(alive, a, axis=1), a, e)
def cleared(v):
    v = v.astype(np.float32)
    v[np.abs(v) < np.float32(2.0 ** -16)] = 0
    return v.astype(BF)
def pointers(rng):
    w = 2 ** rng.integers(1, 10, (N, 8, 1))
    back = rng.integers(1, w + 1, (N, 8, C))
    back[rng.random((N, 8, C)) < 0.03125] = 0
    e = np.maximum(np.arange(C) - back, 0)
    return np.stack([gtable(e[r]) for r in range(N)])
def numbers_of(rng):
    return {"x": cleared(f(rng, N, 128, 4 * C)), "ptr": pointers(rng), "u": np.array(f(rng, N, 128, 512))}
def weights(rng, w):
    c, p = packed(w, rng)
    return {"wc": c, "ws": p}
def still(rng, gs=(), hs=()):
    w = np.zeros((N, 128, 4, 128, 4), np.float32)
    i = np.arange(128)
    for b in range(4): w[:, i, b, i, b] = 32
    for g in gs:
        w[:, 16 * g, 0, 16 * g, 0] = 128
        w[:, 16 * g + 2, 0, 16 * g + 2, 0] = 0
    for g in hs: w[:, 16 * g + 4, 0, 16 * g + 4, 0] = 36
    return weights(rng, w.reshape(N, 128, 2048).astype(BF))
def signs(rng):
    return np.stack([rng.permutation(8) % 2 * 2.0 - 1.0 for r in range(N)]).astype(np.float32)
def setup_inputs(rng):
    return {**numbers_of(rng), **weights(rng, f(rng, N, 128, 2048))}
def setup_inputs_ties(rng):
    d = numbers_of(rng)
    n = rng.permutation(N)
    x = d["x"].reshape(N, 8, 16, C, 4)
    for r in range(N):
        for g in range(8):
            k = np.zeros(C, int) if r == n[0] else rng.permutation(C) % 3
            a = x[r, g, :8, :3].copy()
            a[:, 2] = 0
            x[r, g, :8] = a[:, k]
    x[n[1]] = 0
    u = d["u"].reshape(N, 8, 16, 8, 16, 4)
    b = np.zeros((N, 8, 16, 8, 4), BF)
    for g in range(8): b[:, g, :8, g] = u[:, g, :8, g, 0]
    u[:, :, :, :, 0] = b
    w = f(rng, N, 128, 2048).astype(np.float32).reshape(N, 8, 16, 4, 8, 16, 4)
    w[:, :, 8:, :, :, :8] = 0
    for g in range(8):
        for h in range(8):
            if g != h: w[:, g, :, :, h, :8] = 0
    w[:, :, :, :, :, :8] *= 4
    return {"x": x.reshape(N, 128, 4 * C), "ptr": d["ptr"], "u": u.reshape(N, 128, 512), **weights(rng, w.reshape(N, 128, 2048).astype(BF))}
def setup_inputs_near(rng):
    d = numbers_of(rng)
    x = d["x"].astype(np.float32).reshape(N, 8, 16, C, 4)
    s = (np.arange(C) // 2 + rng.integers(0, C // 4, (N, 8, 1))) % (C // 2)
    g = ((s[..., None] >> np.arange(8)) & 1) * np.exp2(np.arange(8) - 23.0)
    v = np.stack([rng.permutation(8) for r in range(N)])
    k = (v % 2 * 2.0 - 1.0).astype(np.float32)
    size = np.where(v < 4, 1.0, 2.0 ** -30).astype(np.float32)
    x[:, :, 0] = 0
    x[:, :, 0, :, 0] = 1
    for r in rng.permutation(N)[:N // 2]:
        for h in range(8):
            x[r, h, 0, rng.choice(np.flatnonzero(s[r, h] == C // 2 - 1)), 0] = k[r, h] * 2.0 ** 30
            x[r, h, 0, rng.choice(np.flatnonzero(s[r, h] == 0)), 0] = k[r, h] * -2.0 ** 30
    x[:, :, 8] = g[..., :4]
    x[:, :, 9] = g[..., 4:]
    x[:, :, 10:] = rng.integers(4, 8, (N, 8, 6, C, 4)) * rng.choice([-1.0, 1.0], (N, 8, 6, C, 4)) * 2.0 ** -20
    u = d["u"].reshape(N, 128, 128, 4)
    u[:, :, ::16] = 0
    for h in range(0, 128, 16):
        c = size[:, h // 16]
        u[:, h, h, 0] = (k[:, h // 16] * c).astype(BF)
        u[:, h + 8:h + 10, h] = c[:, None, None].astype(BF)
    return {"x": x.reshape(N, 128, 4 * C).astype(BF), "ptr": d["ptr"], "u": u.reshape(N, 128, 512), **still(rng)}
def setup_inputs_huge(rng):
    d = numbers_of(rng)
    x = 2.0 ** 30 * (0.6 + 0.4 * rng.random((N, 128, C, 4)))
    c = np.ones((N, C))
    for r in rng.permutation(N)[:N // 4]: c[r, rng.permutation(C) % 3 == 0] = -1
    x *= c[:, None, :, None]
    u = d["u"].reshape(N, 128, 128, 4)
    a = 2.0 ** 30 * (1 - 0.25 * rng.random((N, 128, 8, 4))) * signs(rng)[:, None, :, None]
    u[:, :, ::16] = a.astype(np.float32).astype(BF)
    return {"x": x.astype(np.float32).reshape(N, 128, 4 * C).astype(BF), "ptr": d["ptr"], "u": u.reshape(N, 128, 512), **still(rng)}
def setup_inputs_deep(rng):
    d = numbers_of(rng)
    x = d["x"].reshape(N, 8, 16, C, 4)
    u = d["u"].reshape(N, 8, 16, 8, 16, 4)
    u[:, :, :, :, 0] = 0
    kind = rng.permutation([0, 0, 1, 1, 2, 3, 3, 4])
    e = np.stack([gentries(d["ptr"][r]) for r in range(N)])
    e[:, kind != 2] = np.maximum(np.arange(C) - 1, 0)
    e[:, kind == 4] = np.arange(C)
    step = SCALE_VALUE[mx_ref.quantize(np.full((128, 16), 28.0, np.float32).astype(BF))[1][0, 0]] * 2.0 ** -9
    small = (np.where(np.arange(C) < K + K // 2, 3, 5) * step).astype(np.float32).astype(BF)
    for g in range(8):
        alive = np.arange(C) > K if kind[g] == 0 else np.arange(C) >= K
        a = np.where(alive, 4.0, -4.0).astype(np.float32)
        if kind[g] == 0: a[0] = 8
        if kind[g] == 4: a[K:K + K // 2] = 12
        o = 8 if kind[g] == 4 else 0
        for r in range(N):
            b = np.where(alive, (16.0, 8.0, 0.0, 8.0 - 8.0 * (r % 2), 8.0)[kind[g]], 0.0).astype(np.float32)
            x[r, g, o + r % 2, :, 0] = a.astype(BF)
            x[r, g, o + 1 - r % 2, :, 0] = b.astype(BF)
            u[r, g, o + r % 2, g, 0, 0] = 1
            if kind[g] == 3:
                x[r, g, 2, :, 0] = 0
                if r % 2 == 0:
                    x[r, g, 0, K, 0] = 3
                    x[r, g, 2, K, 0] = 64
                    u[r, g, 2, g, 0, 0] = 1
            if kind[g] == 4:
                x[r, g, :8] = 0
                x[r, g, 3, :, 0] = small
                x[r, g, 4, :, 0] = 28
                u[r, g, 3, g, 0, 0] = 1
    return {"x": x.reshape(N, 128, 4 * C), "ptr": np.stack([gtable(e[r]) for r in range(N)]), "u": u.reshape(N, 128, 512), **still(rng, np.flatnonzero(kind == 3), np.flatnonzero(kind == 4))}
def setup_inputs_spread(rng):
    d = setup_inputs(rng)
    d["x"] = cleared(wide(rng, N, 128, 4 * C, cols=6))
    return d
def check_inputs(d):
    b = []
    for k in ("x", "u"):
        a = np.abs(d[k].astype(np.float32))
        if not (np.isfinite(a).all() and ((a == 0) | (a >= 2.0 ** -30) & (a <= 2.0 ** 30)).all()): b.append("a value of " + k)
    for p in d["ptr"]:
        e = gentries(p)
        if ((e < 0) | (e > np.arange(C))).any():
            b.append("an entry of ptr")
            break
    return b
def reference(x, ptr, u, wc, ws):
    qu = [mx_ref.quantize(u[r]) for r in range(N)]
    lay = [pk(wc[r], ws[r]) for r in range(N)]
    now = [x[r] for r in range(N)]
    point = [gentries(ptr[r]) for r in range(N)]
    for t in range(R):
        blend, sent = [], []
        for r in range(N):
            e = living(mx_ref.matmul(qu[r], mx_ref.quantize(now[r])))
            number = np.full((8, C), -1)
            np.put_along_axis(number, e, np.arange(K)[None, :], axis=1)
            a = ancestors(point[r], e, number >= 0)
            s = ((gcols(now[r], e).astype(np.float32) + gcols(now[r], a).astype(np.float32)) * np.float32(0.5)).astype(BF)
            q = mx_ref.quantize(s)
            h = tile([np.maximum(mx_ref.matmul(pick(lay[r], np.arange(128 * b, 128 * b + 128)), q), np.float32(0.0)) * np.float32(0.03125) for b in range(4)])
            blend.append(s)
            sent.append(mx_ref.quantize(h))
            point[r] = np.concatenate([np.take_along_axis(number, a, axis=1), np.tile(np.arange(K), (8, 1))], axis=1)
        came = decode(join(*sent)).astype(BF)
        for r in range(N): now[r] = np.concatenate([blend[r], cut(came, (r - 1) % N, 4 * K)], axis=1)
    y, pl = np.zeros((N, 128, C), np.float32), np.zeros((N, 8, C), np.float32)
    oc, osc = np.zeros((N, 128, 4 * C), np.uint8), np.zeros((N, 16, C), np.uint8)
    for r in range(N):
        q = mx_ref.quantize(now[r])
        y[r] = mx_ref.matmul(qu[r], q)
        pl[r] = point[r]
        oc[r], osc[r] = emit(q)
    return {"y": y, "pl": pl, "oc": oc, "osc": osc}

@@ -1,0 +1,630 @@
+import numpy as np
+from concourse.bass import DstId, RemoteDMATransfer
+from concourse.mybir import dt, AluOpType, ActivationFunctionType
+
+C, K, R = 384, 192, 3
+F32, BF, F16, I32, U16, U8, X4 = "float32", "bfloat16", "float16", "int32", "uint16", "uint8", "float8_e4m3fn_x4"
+
+SCRATCH = {}
+
+
+def _decl(name, n, d, where="sbuf"):
+    SCRATCH[name] = (where, [128, n], d)
+
+
+for _t in range(R + 1):
+    _decl("X%d" % _t, 4 * C, BF)
+    _decl("QX%d" % _t, C, X4)
+    _decl("SX%d" % _t, C, U8)
+for _h in range(2):
+    for _n, _w, _d in [("MK", K, F32), ("HD", K, F32), ("NEQ", K, BF), ("NQS", K, BF), ("CMP", 12 * K, BF),
+                       ("JK", 12 * K, BF), ("RK", 12 * 96, BF), ("AL", 12, F32), ("AG", 12, F32), ("TA", 12, F32),
+                       ("TB", 12, F32), ("OFF", 12, U16), ("AA", C, BF)]:
+        _decl(_n + str(_h), _w, _d)
+    _decl("PV%d" % _h, 512, F32, "psum")
+    _decl("PS%d" % _h, 512, F32, "psum")
+for _b in range(4):
+    _decl("D%d" % _b, 512, F32, "psum")
+for _n, _w, _d in [
+    ("H", R * 1024, BF), ("QH", R * 256, X4), ("SH", R * 256, U8), ("LC", R * K, X4), ("LS", R * 256, U8),
+    ("U", 512, BF), ("QU", 128, X4), ("SU", 128, U8), ("QR", 128, X4), ("SR", 128, U8),
+    ("WC", 512, X4), ("WS", 512, U8), ("ONES", 512, BF), ("EB", 2048, BF), ("QE", 512, X4), ("SE", 512, U8),
+    ("PTR", 24, I32), ("PC", 1, I32), ("AI", 1, I32), ("QI", 1, I32), ("I16", 12, I32), ("UL", 8, U16),
+    ("COL", 16, F32), ("IOTA", K, F32), ("J16", K, BF), ("J4", 16, BF), ("C64", 64, F32), ("C64H", 64, F32),
+    ("NB", 12, F32), ("NE", 12, F32), ("REPG", 4, F32), ("REP", 4, U16), ("IOC", C, BF),
+    ("CM0", K, BF), ("CMIN", K, BF), ("R16", K, BF), ("KEEP", K, BF), ("T1", 96, BF), ("A16", 24, U16),
+    ("HOLDA", C, BF), ("HOLDB", K, BF), ("HOLD4", K, BF), ("NEG", K, BF),
+    ("SC", C, F32), ("SREV", K, F32), ("RS", K, BF), ("ALV", C, BF), ("PN", K, BF), ("DC", C, BF), ("P", C, BF),
+    ("JKE", 12 * 208, BF), ("ES", 12 * 104, F32), ("F64", 64, F32), ("L64", 64, U16), ("EL", 12, U16),
+    ("PE", K, BF), ("PEL", 12, U16), ("Q1", K, BF), ("QL", 12, U16), ("Y", K, BF), ("H4", K, BF), ("L4", 48, U16),
+    ("VH", 4 * K, BF), ("VH2", 4 * K, BF), ("TT", 7 * C, BF), ("PR", C, BF), ("PP", C, BF), ("UU", C, BF),
+    ("JL", 8 * 24, U16), ("HSA", C, F16), ("HSB", K, BF), ("PL", K, F32), ("YB", C, F32),
+]:
+    _decl(_n, _w, _d)
+
+NDMA = 24
+SEMAPHORES = ["cv", "cs", "cp", "cg", "sent"] + ["arr%d" % _t for _t in range(R)] + ["d%d" % _k for _k in range(NDMA)]
+
+NS = {(0, 0): 5, (0, 1): 5, (1, 0): 4, (1, 1): 5, (2, 0): 4, (2, 1): 5}
+SPL = {0: 12, 1: 4, 2: 4}
+SPA = {0: 12, 1: 0, 2: 0}
+VPL = {0: 1, 1: 0, 2: 0}
+EV = {0: 4, 1: 3, 2: 3}
+CP = {"relu": "svssvsvs", "dec": "ssvs"}
+PARTS = [(0, 128, 128), (128, K, 256)]
+
+SETS = [(1.04, 70, 1.55, 3.8, 200, 1300, 500, 900), (0.87, 40, 1.2, 2.2, 150, 1000, 300, 600),
+        (1.2, 120, 1.9, 5.0, 260, 1800, 800, 1300), (1.0, 110, 1.2, 3.0, 180, 1200, 300, 1200),
+        (1.04, 40, 1.95, 4.5, 200, 1500, 800, 700)]
+T_DMA, ROUNDS, STEPS, HEAT = 2000.0, 16, 16000, 0.0012
+
+
+def build(T, topo, core, par):
+    A, F = AluOpType, ActivationFunctionType
+    CYC, _lat, GATH, SCAT, T_MM, T_REM, T_ISS, T_BYT = par
+    rank = T.rank_of(core)
+    nxt = T.cores[(rank + 1) % len(T.cores)]
+    prv = T.cores[(rank - 1) % len(T.cores)]
+    ops = []
+
+    def v(name, a=0, b=None, s=1):
+        return (name, a, SCRATCH[name][1][1] if b is None else b, s)
+
+    def col(name, j):
+        return (name, j, j + 1, 1)
+
+    def ap(w):
+        if isinstance(w, tuple) and w[0] == "ind":
+            return ap(w[1]).indirect(ap(w[2]))
+        if isinstance(w, tuple):
+            return T[w[0]][:, w[1]:w[2]] if w[3] == 1 else T[w[0]][:, w[1]:w[2]:w[3]]
+        return w
+
+    def ind(win, off):
+        return ("ind", win, off)
+
+    def flat(ws):
+        r = []
+        for w in ws:
+            if isinstance(w, tuple):
+                r += [w[1], w[2]] if w[0] == "ind" else [w]
+        return r
+
+    def cnt(w):
+        return 16 * cnt(w[2]) if w[0] == "ind" else len(range(w[1], w[2], w[3]))
+
+    def two(w):
+        return SCRATCH[w[0]][2] in (BF, U16, F16)
+
+    def add(eng, fn, rd, wr, dur, kind="c", lat=0.0, after=()):
+        ops.append({"e": eng, "fn": fn, "rd": flat(rd), "wr": flat(wr), "dur": dur, "kind": kind, "lat": lat,
+                    "after": list(after), "k": len(ops), "soft": []})
+        return len(ops) - 1
+
+    def chain(ks):
+        for x, y in zip(ks, ks[1:]):
+            ops[y]["soft"].append(x)
+
+    def vdur(out, ins, base=1.0, fast=True):
+        if out[0] == "ind":
+            return 50 + SCAT * CYC * cnt(out)
+        if ins[0][0] == "ind":
+            return 50 + GATH * CYC * cnt(out)
+        h = 0.5 if fast and all(two(w) for w in [out] + ins) else base
+        return CYC * max(64, h * cnt(out))
+
+    def copy(out, in_):
+        if out[0] == "ind":
+            return add("v", lambda q: q.tensor_copy(ap(out), ap(in_)), [in_, out[2]], [out[1]], vdur(out, [in_]))
+        return add("v", lambda q: q.tensor_copy(ap(out), ap(in_)), [in_], [out], vdur(out, [in_]))
+
+    def ts(out, in0, s1, op0, s2=None, op1=None):
+        if op1 is None:
+            fn = lambda q: q.tensor_scalar(ap(out), ap(in0), ap(s1), None, op0)
+        else:
+            fn = lambda q: q.tensor_scalar(ap(out), ap(in0), ap(s1), ap(s2), op0, op1)
+        return add("v", fn, [in0, s1, s2], [out], vdur(out, [in0]))
+
+    def tt(out, in0, in1, op):
+        ps = any(w[0] != "ind" and SCRATCH[w[0]][0] == "psum" for w in (in0, in1))
+        return add("v", lambda q: q.tensor_tensor(ap(out), ap(in0), ap(in1), op), [in0, in1], [out],
+                   vdur(out, [in0, in1], 1.0 if ps else 2.0, False))
+
+    def scan(out, d0, d1, init, op0, op1):
+        return add("v", lambda q: q.tensor_tensor_scan(ap(out), ap(d0), ap(d1), ap(init), op0, op1), [d0, d1, init],
+                   [out], vdur(out, [d0, d1]))
+
+    def act(out, in_, func, bias=None, scale=None, acc=None):
+        kw = {}
+        if bias is not None:
+            kw["bias"] = ap(bias)
+        if scale is not None:
+            kw["scale"] = scale
+        if acc is not None:
+            kw["accum_out"] = ap(acc)
+        d = 65 + GATH * CYC * cnt(out) if in_[0] == "ind" else CYC * max(64, cnt(out)) + 30 + (25 if acc else 0)
+        return add("s", lambda q: q.activation(ap(out), ap(in_), func, **kw), [in_, bias], [out, acc], d)
+
+    def gather(eng, out, win, off):
+        return act(out, ind(win, off), F.Copy) if eng == "s" else copy(out, ind(win, off))
+
+    def quant(qc, qs, in_):
+        return add("v", lambda q: q.quantize_mx(ap(qc), ap(qs), ap(in_)), [in_], [qc, qs],
+                   CYC / 0.83 * (12 + 0.22 * cnt(in_)))
+
+    def mm(bank, lc, ls, rc, rs):
+        out = v(bank, 0, cnt(rc))
+        return add("p", lambda q: q.matmul_mx(ap(out), ap(lc), ap(ls), ap(rc), ap(rs), True, True), [lc, ls, rc, rs],
+                   [out], T_MM * (cnt(rc) + 16) / 208.0)
+
+    def iota(out, pattern, base, cm=0):
+        if SCRATCH[out[0]][2] == I32:
+            fn = lambda q: q.iota(ap(out), pattern, base, cm)
+        else:
+            fn = lambda q: q.iota(ap(out), pattern, base, cm, allow_small_or_imprecise_dtypes=True)
+        return add("g", fn, [], [out], 160 + 2 * CYC * cnt(out))
+
+    def dma(eng, out, in_, rd, wr, nbytes, after=()):
+        return add(eng, lambda q: q.dma_start(out, in_), rd, wr, 100.0, "dma", T_DMA + nbytes / 200.0, after)
+
+    def u8(w):
+        return ap(w).bitcast(dt.uint8)
+
+    dma("s", ap(v("U")), T.u[:], [], [v("U")], 131072)
+    dma("s", ap(v("PTR")), T.ptr[:], [], [v("PTR")], 12288)
+    xa = dma("y", ap(v("X0", 0, 4 * K)), T.x[:, 0:4 * K], [], [v("X0", 0, 4 * K)], 196608)
+    xb = dma("y", ap(v("X0", 4 * K)), T.x[:, 4 * K:4 * C], [], [v("X0", 4 * K)], 393216)
+    dma("y", u8(v("WC")), T.wc[:], [], [v("WC")], 262144, after=[xa, xb])
+    dma("y", ap(v("WS")), T.ws[:], [], [v("WS")], 65536, after=[xa, xb])
+
+    iota(v("PC"), [[0, 1]], 0, 1)
+    iota(v("I16"), [[16, 12]], 0)
+    iota(v("J16"), [[0, 12], [1, 16]], 0)
+    iota(v("IOTA"), [[1, K]], 0)
+    iota(v("J4"), [[0, 4], [1, 4]], 0)
+    iota(v("IOC"), [[1, C]], -K)
+    iota(v("NEG"), [[-1, K]], -1)
+    iota(v("PP", K, C), [[1, K]], 1)
+    iota(v("NE"), [[16, 12]], 16)
+    iota(v("ES"), [[0, 12 * 104]], 0)
+    for h in range(2):
+        iota(col("AG%d" % h, 11), [[0, 1]], 0)
+    for t in range(R):
+        iota(v("X%d" % (t + 1), 4 * K, 1024), [[0, 256]], 0)
+        iota(v("H", 1024 * t + 4 * K, 1024 * t + 1024), [[0, 256]], 0)
+    iota(v("C64"), [[1, 4], [64, 16]], 416)
+    iota(v("ONES"), [[0, 512]], 1)
+    for b in range(4):
+        o = v("EB", 512 * b, 512 * b + 512)
+        add("g", lambda q, o=o, b=b: q.affine_select(ap(o), ap(v("ONES")), [[-1, 512]], A.is_equal, 0.0, b, 4),
+            [v("ONES")], [o], 200 + 2 * CYC * 512)
+    quant(v("QE"), v("SE"), v("EB"))
+    a0, a1, q0, q1, fa, fb, f4, ah, f5, f6, f7 = [col("COL", j) for j in range(11)]
+    ts(v("AI"), v("PC"), 15, A.bitwise_and)
+    ts(v("QI"), v("AI"), 2, A.arith_shift_right)
+    copy(a0, v("AI"))
+    copy(q0, v("QI"))
+    ts(a1, a0, 1.0, A.add)
+    ts(q1, q0, 1.0, A.add)
+    ts(ah, a0, 0.5, A.add)
+    ts(f7, a0, 15.0, A.is_lt, float(C), A.mult)
+    ts(fa, f7, float(K), A.add)
+    ts(fb, f7, 0.5, A.mult, -1.0, A.add)
+    ts(f5, q0, 3.0, A.is_lt, float(K), A.mult)
+    ts(f6, a0, 0.25, A.mult, q0, A.subtract)
+    ts(f4, f5, f6, A.add, -1.0, A.add)
+    copy(v("UL"), v("I16", 0, 8))
+    ts(v("NB"), v("I16"), ah, A.add)
+    act(v("C64H"), v("C64"), F.Copy, scale=0.5)
+    ts(v("CM0"), v("J16"), a0, A.is_equal, 0.5, A.subtract)
+    ts(v("CMIN"), v("CM0"), 2.0 ** 97, A.mult)
+    ts(v("R16"), v("J16"), 0.5, A.subtract, 2.0 ** 97, A.mult)
+    ts(v("KEEP"), v("J16"), 1.0, A.min)
+    ts(v("A16"), v("J16", 0, 24), 0.0, A.mult, a0, A.add)
+    ts(v("REPG"), v("A16", 0, 4), 11.0, A.min, 104.0, A.mult)
+    ts(v("REP"), v("REPG"), 103.0, A.add)
+    ts(v("T1", 0, 16), v("J16", 0, 16), a0, A.is_equal, 1024.0, A.mult)
+    ts(v("T1", 16, 32), v("J16", 0, 16), a1, A.is_equal, -float(C), A.mult)
+    tt(v("T1", 32, 48), v("T1", 0, 16), v("T1", 16, 32), A.add)
+    act(v("HOLDA"), ind(v("T1", 32, 48), v("A16")), F.Copy)
+    act(v("HOLDB"), v("HOLDA", 0, K), F.Copy, scale=0.5)
+    ts(v("T1", 48, 64), v("J4"), q0, A.is_equal, 512.0, A.mult)
+    ts(v("T1", 64, 80), v("J4"), q1, A.is_equal, -float(K), A.mult)
+    tt(v("T1", 80, 96), v("T1", 48, 64), v("T1", 64, 80), A.add)
+    act(v("HOLD4"), ind(v("T1", 80, 96), v("A16", 0, 12)), F.Copy)
+    dma("y", T.pl[:, K:C], T["IOTA"][0:128:16, 0:K], [v("IOTA")], [], 6144)
+
+    quant(v("QU"), v("SU"), v("U"))
+    add("v", lambda q: q.tensor_copy(ap(v("QR")).bitcast(dt.uint32), ap(v("QU")).bitcast(dt.uint32).indirect(ap(v("UL")))),
+        [v("QU"), v("UL")], [v("QR")], 50 + GATH * CYC * 128)
+    act(v("SR"), ind(v("SU"), v("UL")), F.Copy)
+
+    def half(t, h):
+        return v("QX%d" % t, K * h, K * h + K), v("SX%d" % t, K * h, K * h + K), v("X%d" % t, 4 * K * h, 4 * K * h + 4 * K)
+
+    def ranks(t, h):
+        qc, qs, _x = half(t, h)
+        s = str(h)
+        pv = v("PV" + s, 0, K)
+        mm("PV" + s, v("QR"), v("SR"), qc, qs)
+        mm("PS" + s, v("QR"), v("SR"), qc, qs)
+        sc = v("SC", K * h, K * h + K)
+        act(sc, v("PS" + s, 0, K), F.Copy)
+        tt(v("MK" + s), pv, v("CMIN"), A.min)
+        scan(v("HD" + s), v("R16"), v("MK" + s), 0.0, A.min, A.max)
+        tt(v("NEQ" + s), pv, v("HD" + s), A.not_equal)
+        scan(v("NQS" + s), v("KEEP"), v("NEQ" + s), 0.0, A.mult, A.add)
+        b0 = 12 - NS[(t, h)]
+        cv, cs = [], []
+        for b in range(b0 + 1):
+            if b < b0:
+                w, n, o = col("HD" + s, 16 * b + 15), 16 * b + 16, K * b
+                cv.append(ts(v("CMP" + s, o, o + n), v("PV" + s, 0, n), w, A.is_ge))
+                if n < K:
+                    cv.append(ts(v("CMP" + s, o + n, o + K), v("PV" + s, n, K), w, A.is_gt))
+            if b > 0:
+                o = K * b - K
+                cv.append(scan(v("RK" + s, 96 * b - 96, 96 * b), v("CMP" + s, o, o + 96), v("CMP" + s, o + 96, o + K),
+                               col("NQS" + s, 16 * b - 1), A.add, A.add))
+        for b in range(b0, 13):
+            if b < 12:
+                cs.append(act(v("CMP" + s, K * b, K * b + K), sc, F.Sign, bias=col("HD" + s, 16 * b + 15), scale=-1.0))
+            if b > b0:
+                n, o = 16 * b, K * b - K
+                cs.append(act(v("JK" + s, o, o + n), v("CMP" + s, o, o + n), F.Relu, acc=col("AL" + s, b - 1)))
+                if n < K:
+                    cs.append(act(v("JK" + s, o + n, o + K), v("CMP" + s, o + n, o + K), F.Relu, scale=-1.0,
+                                  acc=col("AG" + s, b - 1)))
+        chain(cv)
+        chain(cs)
+        if b0 < 12:
+            tt(v("TA" + s, b0, 12), v("NQS" + s, 16 * b0 + 15, K, 16), v("NE", b0, 12), A.add)
+            tt(v("TB" + s, b0, 12), v("AG" + s, b0, 12), v("AL" + s, b0, 12), A.subtract)
+            tt(v("RK" + s, 96 * b0 + 95, 12 * 96, 96), v("TA" + s, b0, 12), v("TB" + s, b0, 12), A.add)
+        rk = v("RK" + s, 95, 12 * 96, 96)
+        if h == 0:
+            ts(v("OFF0"), rk, -1.0, A.mult, float(K - 1 + 16), A.add)
+            copy(ind(v("SREV"), v("OFF0")), sc)
+            gather("s", v("RS"), v("IOTA"), v("OFF0"))
+        else:
+            ts(v("OFF1"), rk, -16.0, A.add)
+
+    def jl(t, k):
+        return v("JL", 24 * k, 24 * k + (24 if t == 0 else 12))
+
+    def to_list(t, out, rep):
+        if t == 0:
+            scan(v("HSA", 0, cnt(rep)), v("HOLDA", 0, cnt(rep)), rep, 0.0, A.add, A.min)
+            ts(out, v("HSA", 15, cnt(rep), 16), fa, A.add)
+        else:
+            scan(v("HSB"), v("HOLDB"), rep, 0.0, A.add, A.min)
+            ts(out, v("HSB", 15, K, 16), fb, A.add)
+
+    def split(out, win, off, ns):
+        c = cnt(off) - ns
+        if c > 0:
+            gather("v", v(out[0], out[1], out[1] + 16 * c), win, v(off[0], off[1], off[1] + c))
+        if ns > 0:
+            gather("s", v(out[0], out[1] + 16 * c, out[2]), win, v(off[0], off[1] + c, off[2]))
+
+    quant(*half(0, 0))
+    quant(*half(0, 1))
+    copy(jl(0, 7), v("PTR"))
+    gather("s", v("PR"), v("IOC"), jl(0, 7))
+    ranks(0, 0)
+    rid, pid, _e = topo.addr(nxt)
+    mask = topo.mask(core, nxt)
+    eng = topo.engines(core, nxt)
+    halves = [sum(1 << e for e in eng[:len(eng) // 2]), sum(1 << e for e in eng[len(eng) // 2:])]
+    for t in range(R):
+        X, Xn = "X%d" % t, "X%d" % (t + 1)
+        ranks(t, 1)
+        aln, als, pn_last = v("ALV", K, C), v("ALV", 0, K), col("PN", K - 1)
+        tt(aln, ind(v("SREV"), v("OFF1")), v("SC", K, C), A.is_lt)
+        scan(v("PN"), aln, aln, 0.0, A.add, A.max)
+        ts(als, v("RS"), pn_last, A.is_ge)
+        ts(v("P", K, C), v("PN"), pn_last, A.subtract, float(K), A.add)
+        scan(v("P", 0, K), als, als, 0.0, A.add, A.max)
+        ts(v("DC", 0, K), v("RS"), pn_last, A.is_lt, -1000.0, A.mult)
+        n = C if t == 0 else K
+        own = v("IOC") if t == 0 else v("PP", K, C)
+        if t == 0:
+            ts(v("DC", K, C), aln, 1.0, A.subtract, 1000.0, A.mult)
+        scan(v("AA0", 0, n), v("P", 0, n), v("DC", 0, n), 0.0, A.max, A.add)
+        scan(v("UU", 0, n), own, v("DC", 0, n), -1000.0, A.max, A.add)
+        tt(v("TT", 0, n), ind(own, jl(t, 7)), v("UU", 0, n), A.max)
+        tt(v("TT", C, C + n), ind(v("TT", 0, n), jl(t, 7)), v("UU", 0, n), A.max)
+        for k in range(1, 7):
+            cur = v("TT", C * k, C * k + n)
+            to_list(t, jl(t, k), cur)
+            if k < 6:
+                split(v("TT", C * k + C, C * k + C + n), cur, jl(t, k), SPL[t])
+        split(v("AA1", 0, n), v("AA0", 0, n), jl(t, 6), SPA[t])
+        split(v("AA0", 0, n), v("AA1", 0, n), jl(t, 6), SPA[t])
+        cs = []
+        for b in range(12):
+            o = 208 * b
+            if b < EV[t]:
+                ts(v("JKE", o, o + 208), v("P", 16 * b, 16 * b + 208), col("NB", b), A.is_le, 2.0, A.mult)
+                scan(v("ES", 104 * b, 104 * b + 104), v("JKE", o, o + 104), v("JKE", o + 104, o + 208), -208.0, A.add, A.add)
+            else:
+                cs.append(act(v("JKE", o, o + 208), v("P", 16 * b, 16 * b + 208), F.Sign, bias=col("NB", b), scale=-1.0,
+                              acc=col("ES", 104 * b + 103)))
+        chain(cs)
+        tt(v("F64"), ind(v("ES"), v("REP")), v("C64H"), A.add)
+        ts(v("EL"), v("F64", 0, 12), 0.5, A.mult)
+        ts(v("L64"), v("F64"), 2.0, A.mult)
+        gather("s", v("PE"), v("PR") if t == 0 else v("PP"), v("EL"))
+        to_list(t, v("PEL"), v("PE"))
+        gather("s", v("Q1"), v("TT", 6 * C, 6 * C + n), v("PEL"))
+        to_list(t, v("QL"), v("Q1"))
+        tt(v("Y"), ind(v("AA0", 0, n), v("QL")), v("NEG"), A.max)
+        cs = []
+        for j in range(4):
+            src = ind(v(X), v("L64", 16 * j, 16 * j + 12))
+            if j >= 4 - VPL[t]:
+                ts(v("VH", j, 4 * K, 4), src, 0.5, A.mult)
+            else:
+                cs.append(act(v("VH", j, 4 * K, 4), src, F.Copy, scale=0.5))
+            copy(v("VH2", j, 4 * K, 4), v("VH", j, 4 * K, 4))
+        chain(cs)
+        p1 = v("PP", 0, K)
+        act(p1, v("Y"), F.Abs)
+        scan(v("H4"), v("HOLD4"), p1, 0.0, A.add, A.min)
+        ts(v("L4"), v("H4", 3, K, 4), f4, A.add, 4.0, A.mult)
+        arr = T.sem["arr%d" % t]
+        for i, (c0, c1, c2) in enumerate(PARTS):
+            tt(v(Xn, 4 * c0, 4 * c1), ind(v("VH"), v("L4", c0 // 4, c1 // 4)), v("VH2", 4 * c0, 4 * c1), A.add)
+            qc, qs = v("QX%d" % (t + 1), c0, c2), v("SX%d" % (t + 1), c0, c2)
+            quant(qc, qs, v(Xn, 4 * c0, 4 * c2))
+            h0, g0, l0 = 1024 * t, 256 * t, K * t
+            for b in range(4):
+                bank = "D%d" % b if i == 0 else ("PV1", "PS1", "PV0", "PS0")[b]
+                mm(bank, v("WC", 128 * b, 128 * b + 128), v("WS", 128 * b, 128 * b + 128), qc, qs)
+                o = v("H", h0 + 4 * c0 + b, h0 + 4 * c1, 4)
+                if CP["relu"][4 * i + b] == "s":
+                    act(o, v(bank, 0, c1 - c0), F.Relu, scale=0.03125)
+                else:
+                    ts(o, v(bank, 0, c1 - c0), 0.0, A.max, 0.03125, A.mult)
+            quant(v("QH", g0 + c0, g0 + c2), v("SH", g0 + c0, g0 + c2), v("H", h0 + 4 * c0, h0 + 4 * c2))
+            qh, lc = v("QH", g0 + c0, g0 + c1), v("LC", l0 + c0, l0 + c1)
+            if i == 0:
+                s1 = add("g", lambda q, lc=lc, qh=qh, arr=arr:
+                         q.remote_dma(u8(lc), u8(qh), arr, T.sem["sent"], pid, rid, mask), [qh], [], T_ISS, "rem")
+            else:
+                sh, ls = v("SH", g0, g0 + 256), v("LS", g0, g0 + 256)
+                s2 = add("g", lambda q, lc=lc, qh=qh, ls=ls, sh=sh, arr=arr: q.remote_dma_fused(
+                    [RemoteDMATransfer(dst_ids=[DstId(rid=rid, pnc=pid)], dma_engine_mask=m, remote_sem=arr, src=a, dst=b)
+                     for m, a, b in ((halves[0], u8(qh), u8(lc)), (halves[1], ap(sh), ap(ls)))], local_sem=T.sem["sent"]),
+                    [qh, sh], [], T_ISS, "rem", after=[s1])
+        lc, ls = v("LC", K * t, K * t + K), v("LS", 256 * t, 256 * t + K)
+        add("r", ("arr%d" % t, 2 * len(topo.engines(prv, core))), [], [lc, ls], T_BYT * 0.55, "arr", T_REM, after=[s1, s2])
+        if t + 1 < R:
+            to_list(t + 1, jl(t + 1, 7), p1)
+            ranks(t + 1, 0)
+        else:
+            ts(v("PL"), p1, -1.0, A.add)
+            dma("y", T.pl[:, 0:K], T["PL"][0:128:16, 0:K], [v("PL")], [], 6144)
+        for b in range(4):
+            mm("D%d" % b, v("QE", 128 * b, 128 * b + 128), v("SE", 128 * b, 128 * b + 128), lc, ls)
+            o = v(Xn, 4 * K + b, 4 * C, 4)
+            if CP["dec"][b] == "s":
+                act(o, v("D%d" % b, 0, K), F.Copy)
+            else:
+                copy(o, v("D%d" % b, 0, K))
+        quant(*half(t + 1, 1))
+
+    for h in range(2):
+        qc, qs, _x = half(R, h)
+        mm("PV%d" % h, v("QU"), v("SU"), qc, qs)
+        yb = v("YB", K * h, K * h + K)
+        copy(yb, v("PV%d" % h, 0, K))
+        dma("y", T.oc[:, 4 * K * h:4 * K * h + 4 * K], u8(qc), [qc], [], 98304)
+        for k in range(4):
+            dma("y" if (h == 0 or k < 2) else "s", T.osc[4 * k:4 * k + 4, K * h:K * h + K],
+                T["SX%d" % R][32 * k:32 * k + 4, K * h:K * h + K], [qs], [], 768)
+        dma("y" if h == 0 else "s", T.y[:, K * h:K * h + K], ap(yb), [yb], [], 98304)
+    return ops, 2 * R * len(eng)
+
+
+def depend(ops):
+    seen, anc = {}, []
+    for o in ops:
+        dep = set(o["after"])
+        for isw, ws in ((False, o["rd"]), (True, o["wr"])):
+            for w in ws:
+                psum = SCRATCH[w[0]][0] == "psum"
+                m = np.zeros(SCRATCH[w[0]][1][1], bool)
+                m[w[1]:w[2]:w[3]] = True
+                for (k, pw, pm, pe) in seen.get(w[0], []):
+                    if k != o["k"] and ((psum and pe != o["e"]) or ((isw or pw) and bool((m & pm).any()))):
+                        dep.add(k)
+                seen.setdefault(w[0], []).append((o["k"], isw, m, o["e"]))
+        o["dep"] = sorted(dep)
+        near, m = [], 0
+        for d in reversed(o["dep"]):
+            if not (m >> d) & 1:
+                near.append(d)
+                m |= anc[d] | (1 << d)
+        anc.append(m)
+        o["near"] = near
+
+
+def by_key(key, pre, seq):
+    k2 = list(key)
+    for k in seq:
+        for d, _w in pre[k]:
+            if k2[k] <= k2[d]:
+                k2[k] = k2[d] + 1e-3
+    return [int(k) for k in np.argsort(k2, kind="stable")]
+
+
+def lay(ops, idx, pre, back):
+    st, en, busy = [0.0] * len(ops), [0.0] * len(ops), {}
+    for k in idx:
+        o = ops[k]
+        t0 = max([en[d] + w for d, w in pre[k]] + [0.0]) + (o["lat"] if back else 0.0)
+        iv = busy.setdefault(o["e"], [])
+        pos = len(iv)
+        for j, (s, e) in enumerate(iv):
+            if t0 + o["dur"] <= s:
+                pos = j
+                break
+            t0 = max(t0, e)
+        iv.insert(pos, (t0, t0 + o["dur"]))
+        st[k], en[k] = t0, t0 + o["dur"] + (0.0 if back else o["lat"])
+    return st, en
+
+
+def span(seq, near, eng, cost):
+    dur, lat, w = cost
+    en, free = [0.0] * len(dur), {}
+    for k in seq:
+        t = free.get(eng[k], 0.0)
+        for j in near[k]:
+            if en[j] + w > t:
+                t = en[j] + w
+        free[eng[k]] = t + dur[k]
+        en[k] = t + dur[k] + lat[k]
+    return max(en)
+
+
+def tight(seq, near, eng, cost):
+    dur, lat, w = cost
+    en, free, why, last = [0.0] * len(dur), {}, [None] * len(dur), {}
+    for k in seq:
+        e = eng[k]
+        t, y = free.get(e, 0.0), (last.get(e), True)
+        for j in near[k]:
+            if en[j] + w > t:
+                t, y = en[j] + w, (j, False)
+        free[e], en[k], why[k], last[e] = t + dur[k], t + dur[k] + lat[k], y, k
+    k, pairs = en.index(max(en)), []
+    while k is not None:
+        j, same = why[k]
+        if same and j is not None and j not in near[k]:
+            pairs.append((j, k))
+        k = j
+    return pairs
+
+
+def order(ops, costs):
+    n = len(ops)
+    lat = costs[0][2]
+    pre = [[(d, lat) for d in o["near"]] + [(d, 0.0) for d in o["soft"]] for o in ops]
+    suc = [[] for o in ops]
+    up = [0.0] * n
+    for o in reversed(ops):
+        up[o["k"]] += o["dur"] + o["lat"]
+        for d, w in pre[o["k"]]:
+            up[d] = max(up[d], up[o["k"]] + w)
+            suc[d].append((o["k"], w))
+    fwd, bwd = list(range(n)), list(range(n - 1, -1, -1))
+    st, en = lay(ops, by_key([-u for u in up], pre, fwd), pre, False)
+    best = (max(en), st)
+    rng = np.random.default_rng(0)
+    for it in range(ROUNDS):
+        nz = rng.normal(0.0, 200.0 if it % 2 else 1e-6, n)
+        _s, eb = lay(ops, by_key([-en[k] + nz[k] for k in range(n)], suc, bwd), suc, True)
+        st, en = lay(ops, by_key([-eb[k] for k in range(n)], pre, fwd), pre, False)
+        if max(en) < best[0]:
+            best = (max(en), st)
+    near, eng = [o["near"] for o in ops], [o["e"] for o in ops]
+    hard = [[(d, 0.0) for d in o["near"]] for o in ops]
+    seq = by_key(best[1], hard, fwd)
+    base = [span(seq, near, eng, c) for c in costs]
+    wts = [2.0] + [1.0] * (len(costs) - 1)
+
+    def score(q):
+        return sum(w * span(q, near, eng, c) / b for w, c, b in zip(wts, costs, base)) / sum(wts)
+
+    cur = top = score(seq)
+    now, pairs, key = seq, None, None
+    for it in range(STEPS):
+        if pairs is None:
+            pairs = [tight(now, near, eng, c) for c in costs]
+            key = [0.0] * n
+            for j, k in enumerate(now):
+                key[k] = float(j)
+        pr = pairs[int(rng.integers(0, len(costs)))]
+        if not pr:
+            continue
+        a, b = pr[int(rng.integers(0, len(pr)))]
+        k2 = list(key)
+        far = float(rng.integers(0, 2)) * float(rng.exponential(8.0))
+        if rng.random() < 0.5:
+            k2[b] = key[a] - 0.5 - far
+        else:
+            k2[a] = key[b] + 0.5 + far
+        q = by_key(k2, hard, fwd)
+        e = score(q)
+        if e < cur or rng.random() < np.exp((cur - e) / (HEAT * (1.0 - it / STEPS) + 1e-6)):
+            cur, now, pairs = e, q, None
+            if e < top:
+                top, seq = e, q
+    return seq
+
+
+_ORDER = {}
+
+
+def plan(T, topo, core):
+    ops, nsent = build(T, topo, core, SETS[0])
+    depend(ops)
+    if "seq" not in _ORDER:
+        costs = []
+        for par in SETS:
+            o2 = build(T, topo, core, par)[0]
+            costs.append(([o["dur"] for o in o2], [o["lat"] for o in o2], par[1]))
+        _ORDER["seq"], _ORDER["costs"] = order(ops, costs), costs
+    return ops, nsent, _ORDER["seq"]
+
+
+def rank_program(g, core, T, topo):
+    if T.rank_of(core) is None:
+        return
+    ops, nsent, seq = plan(T, topo, core)
+    queue = {"v": g.vector, "s": g.scalar, "p": g.tensor, "g": g, "y": g.sync}
+    csem = {"v": "cv", "s": "cs", "p": "cp", "g": "cg"}
+    count = {}
+    known = {e: {} for e in queue}
+    pos = {k: j for j, k in enumerate(seq)}
+    ndma = 0
+    for k in seq:
+        o = ops[k]
+        e = o["e"]
+        if o["kind"] == "arr":
+            o["sig"], o["clock"] = o["fn"], {}
+            count[o["fn"][0]] = o["fn"][1]
+            continue
+        q, kn = queue[e], known[e]
+        need = {}
+        for d in o["dep"]:
+            s, n = ops[d]["sig"]
+            need[s] = max(need.get(s, 0), n)
+        for d in sorted(o["dep"], key=lambda j: -pos[j]):
+            s, n = ops[d]["sig"]
+            if kn.get(s, 0) < n:
+                q.wait_ge(T.sem[s], need[s])
+                kn[s] = need[s]
+            for s2, n2 in ops[d]["clock"].items():
+                kn[s2] = max(kn.get(s2, 0), n2)
+        ins = o["fn"](q)
+        o["clock"] = dict(kn)
+        if o["kind"] == "rem":
+            o["sig"] = ("sent", 0)
+        elif o["kind"] == "dma":
+            s = "d%d" % ndma
+            ndma += 1
+            ins.then_inc(T.sem[s], 16)
+            o["sig"] = (s, 16)
+            count[s] = 16
+        else:
+            s = csem[e]
+            count[s] = count.get(s, 0) + 1
+            ins.then_inc(T.sem[s], 1)
+            o["sig"] = (s, count[s])
+    g.wait_ge(T.sem["sent"], nsent)
+    for s, n in count.items():
+        if max(known[e].get(s, 0) for e in queue) < n:
+            g.sync.wait_ge(T.sem[s], n)

@@ -19,7 +19,7 @@ for _t in range(R + 1):
 for _h in range(2):
     for _n, _w, _d in [("MK", K, F32), ("HD", K, F32), ("NEQ", K, BF), ("NQS", K, BF), ("CMP", 12 * K, BF),
                        ("JK", 12 * K, BF), ("RK", 12 * 96, BF), ("AL", 12, F32), ("AG", 12, F32), ("TA", 12, F32),
-                       ("TB", 12, F32), ("OFF", 12, U16), ("AA", C, BF)]:
+                       ("OFF", 12, U16), ("AA", C, BF)]:
         _decl(_n + str(_h), _w, _d)
     _decl("PV%d" % _h, 512, F32, "psum")
     _decl("PS%d" % _h, 512, F32, "psum")
@@ -34,29 +34,27 @@ for _n, _w, _d in [
     ("NB", 12, F32), ("NE", 12, F32), ("REPG", 4, F32), ("REP", 4, U16), ("IOC", C, BF),
     ("CM0", K, BF), ("CMIN", K, BF), ("R16", K, BF), ("KEEP", K, BF), ("T1", 96, BF), ("A16", 24, U16),
     ("HOLDA", C, BF), ("HOLDB", K, BF), ("HOLD4", K, BF), ("NEG", K, BF),
-    ("SC", C, F32), ("SREV", K, F32), ("RS", K, BF), ("ALV", C, BF), ("PN", K, BF), ("DC", C, BF), ("P", C, BF),
+    ("SC", C, F32), ("SREV", K, F32), ("RS", K, BF), ("ALV", C, BF), ("PN", K, BF), ("P", C, BF),
     ("JKE", 12 * 208, BF), ("ES", 12 * 104, F32), ("F64", 64, F32), ("L64", 64, U16), ("EL", 12, U16),
     ("PE", K, BF), ("PEL", 12, U16), ("Q1", K, BF), ("QL", 12, U16), ("Y", K, BF), ("H4", K, BF), ("L4", 48, U16),
-    ("VH", 4 * K, BF), ("VH2", 4 * K, BF), ("TT", 7 * C, BF), ("PR", C, BF), ("PP", C, BF), ("UU", C, BF),
-    ("JL", 8 * 24, U16), ("HSA", C, F16), ("HSB", K, BF), ("PL", K, F32), ("YB", C, F32),
+    ("VH", 4 * K, BF), ("VH2", 4 * K, BF), ("TT", 7 * C, BF), ("PR", C, BF), ("PP", C, BF),
+    ("JL", 9 * 24, U16), ("JR", 8 * C, BF), ("PJ", C, BF), ("Y1", K, BF), ("DA", C, F16), ("DB", C + 2, F16),
+    ("HSA", 4 * C, F16), ("HSB", 4 * K, BF), ("PL", K, F32), ("YB", C, F32),
 ]:
     _decl(_n, _w, _d)
 
 NDMA = 24
 SEMAPHORES = ["cv", "cs", "cp", "cg", "sent"] + ["arr%d" % _t for _t in range(R)] + ["d%d" % _k for _k in range(NDMA)]
 
-NS = {(0, 0): 5, (0, 1): 5, (1, 0): 4, (1, 1): 5, (2, 0): 4, (2, 1): 5}
-SPL = {0: 12, 1: 4, 2: 4}
-SPA = {0: 12, 1: 0, 2: 0}
-VPL = {0: 1, 1: 0, 2: 0}
-EV = {0: 4, 1: 3, 2: 3}
+NS = {(0, 0): 5, (0, 1): 4, (1, 0): 4, (1, 1): 4, (2, 0): 4, (2, 1): 4}
+EV = {0: 0, 1: 1, 2: 1}
 CP = {"relu": "svssvsvs", "dec": "ssvs"}
 PARTS = [(0, 128, 128), (128, K, 256)]
 
-SETS = [(1.04, 70, 1.55, 3.8, 200, 1300, 500, 900), (0.87, 40, 1.2, 2.2, 150, 1000, 300, 600),
-        (1.2, 120, 1.9, 5.0, 260, 1800, 800, 1300), (1.0, 110, 1.2, 3.0, 180, 1200, 300, 1200),
-        (1.04, 40, 1.95, 4.5, 200, 1500, 800, 700)]
-T_DMA, ROUNDS, STEPS, HEAT = 2000.0, 16, 16000, 0.0012
+SETS = [(0.83, 200, 1.55, 3.8, 150, 1500, 600, 900), (0.83, 120, 1.55, 3.8, 150, 3500, 800, 900),
+        (1.2, 200, 1.9, 5.0, 260, 1800, 800, 1300), (1.0, 150, 1.2, 2.5, 180, 2200, 500, 1200),
+        (0.9, 250, 1.3, 4.5, 200, 1500, 400, 700)]
+T_DMA, ROUNDS, STEPS, HEAT = 2000.0, 16, 20000, 0.0012
 
 
 def build(T, topo, core, par):
@@ -145,8 +143,8 @@ def build(T, topo, core, par):
         d = 65 + GATH * CYC * cnt(out) if in_[0] == "ind" else CYC * max(64, cnt(out)) + 30 + (25 if acc else 0)
         return add("s", lambda q: q.activation(ap(out), ap(in_), func, **kw), [in_, bias], [out, acc], d)
 
-    def gather(eng, out, win, off):
-        return act(out, ind(win, off), F.Copy) if eng == "s" else copy(out, ind(win, off))
+    def gather(out, win, off):
+        return act(out, ind(win, off), F.Copy)
 
     def quant(qc, qs, in_):
         return add("v", lambda q: q.quantize_mx(ap(qc), ap(qs), ap(in_)), [in_], [qc, qs],
@@ -207,6 +205,7 @@ def build(T, topo, core, par):
     ts(a1, a0, 1.0, A.add)
     ts(q1, q0, 1.0, A.add)
     ts(ah, a0, 0.5, A.add)
+    ts(col("DB", 0), a0, 0.0, A.mult)
     ts(f7, a0, 15.0, A.is_lt, float(C), A.mult)
     ts(fa, f7, float(K), A.add)
     ts(fb, f7, 0.5, A.mult, -1.0, A.add)
@@ -226,18 +225,18 @@ def build(T, topo, core, par):
     ts(v("T1", 0, 16), v("J16", 0, 16), a0, A.is_equal, 1024.0, A.mult)
     ts(v("T1", 16, 32), v("J16", 0, 16), a1, A.is_equal, -float(C), A.mult)
     tt(v("T1", 32, 48), v("T1", 0, 16), v("T1", 16, 32), A.add)
-    act(v("HOLDA"), ind(v("T1", 32, 48), v("A16")), F.Copy)
+    gather(v("HOLDA"), v("T1", 32, 48), v("A16"))
     act(v("HOLDB"), v("HOLDA", 0, K), F.Copy, scale=0.5)
     ts(v("T1", 48, 64), v("J4"), q0, A.is_equal, 512.0, A.mult)
     ts(v("T1", 64, 80), v("J4"), q1, A.is_equal, -float(K), A.mult)
     tt(v("T1", 80, 96), v("T1", 48, 64), v("T1", 64, 80), A.add)
-    act(v("HOLD4"), ind(v("T1", 80, 96), v("A16", 0, 12)), F.Copy)
+    gather(v("HOLD4"), v("T1", 80, 96), v("A16", 0, 12))
     dma("y", T.pl[:, K:C], T["IOTA"][0:128:16, 0:K], [v("IOTA")], [], 6144)
 
     quant(v("QU"), v("SU"), v("U"))
     add("v", lambda q: q.tensor_copy(ap(v("QR")).bitcast(dt.uint32), ap(v("QU")).bitcast(dt.uint32).indirect(ap(v("UL")))),
         [v("QU"), v("UL")], [v("QR")], 50 + GATH * CYC * 128)
-    act(v("SR"), ind(v("SU"), v("UL")), F.Copy)
+    gather(v("SR"), v("SU"), v("UL"))
 
     def half(t, h):
         return v("QX%d" % t, K * h, K * h + K), v("SX%d" % t, K * h, K * h + K), v("X%d" % t, 4 * K * h, 4 * K * h + 4 * K)
@@ -277,40 +276,49 @@ def build(T, topo, core, par):
                                   acc=col("AG" + s, b - 1)))
         chain(cv)
         chain(cs)
-        if b0 < 12:
-            tt(v("TA" + s, b0, 12), v("NQS" + s, 16 * b0 + 15, K, 16), v("NE", b0, 12), A.add)
-            tt(v("TB" + s, b0, 12), v("AG" + s, b0, 12), v("AL" + s, b0, 12), A.subtract)
-            tt(v("RK" + s, 96 * b0 + 95, 12 * 96, 96), v("TA" + s, b0, 12), v("TB" + s, b0, 12), A.add)
+        tt(v("TA" + s, b0, 12), v("NQS" + s, 16 * b0 + 15, K, 16), v("NE", b0, 12), A.add)
+        for b in range(b0, 12):
+            scan(col("RK" + s, 96 * b + 95), col("AG" + s, b), col("AL" + s, b), col("TA" + s, b), A.add, A.subtract)
         rk = v("RK" + s, 95, 12 * 96, 96)
         if h == 0:
             ts(v("OFF0"), rk, -1.0, A.mult, float(K - 1 + 16), A.add)
             copy(ind(v("SREV"), v("OFF0")), sc)
-            gather("s", v("RS"), v("IOTA"), v("OFF0"))
+            gather(v("RS"), v("IOTA"), v("OFF0"))
         else:
             ts(v("OFF1"), rk, -16.0, A.add)
 
     def jl(t, k):
         return v("JL", 24 * k, 24 * k + (24 if t == 0 else 12))
 
-    def to_list(t, out, rep):
-        if t == 0:
-            scan(v("HSA", 0, cnt(rep)), v("HOLDA", 0, cnt(rep)), rep, 0.0, A.add, A.min)
-            ts(out, v("HSA", 15, cnt(rep), 16), fa, A.add)
-        else:
-            scan(v("HSB"), v("HOLDB"), rep, 0.0, A.add, A.min)
-            ts(out, v("HSB", 15, K, 16), fb, A.add)
+    turn = [0]
 
-    def split(out, win, off, ns):
-        c = cnt(off) - ns
-        if c > 0:
-            gather("v", v(out[0], out[1], out[1] + 16 * c), win, v(off[0], off[1], off[1] + c))
-        if ns > 0:
-            gather("s", v(out[0], out[1] + 16 * c, out[2]), win, v(off[0], off[1] + c, off[2]))
+    def to_list(t, out, rep):
+        turn[0] = (turn[0] + 1) % 4
+        n = cnt(rep)
+        if t == 0:
+            o = C * turn[0]
+            scan(v("HSA", o, o + n), v("HOLDA", 0, n), rep, 0.0, A.add, A.min)
+            ts(out, v("HSA", o + 15, o + n, 16), fa, A.add)
+        else:
+            o = K * turn[0]
+            scan(v("HSB", o, o + n), v("HOLDB"), rep, 0.0, A.add, A.min)
+            ts(out, v("HSB", o + 15, o + n, 16), fb, A.add)
+
+    def tables(t):
+        n = C if t == 0 else K
+        cur = v("PR") if t == 0 else v("PP", 0, K)
+        for k in range(1, 9):
+            new = v("PJ", K, C) if (k == 8 and t > 0) else v("JR", C * (k - 1), C * (k - 1) + n)
+            gather(new, cur, jl(t, max(k - 2, 0)))
+            to_list(t, jl(t, k), new)
+            cur = new
+        gather(v("PJ", 0, n), cur, jl(t, 0))
 
     quant(*half(0, 0))
     quant(*half(0, 1))
-    copy(jl(0, 7), v("PTR"))
-    gather("s", v("PR"), v("IOC"), jl(0, 7))
+    copy(jl(0, 0), v("PTR"))
+    gather(v("PR"), v("IOC"), jl(0, 0))
+    tables(0)
     ranks(0, 0)
     rid, pid, _e = topo.addr(nxt)
     mask = topo.mask(core, nxt)
@@ -325,22 +333,21 @@ def build(T, topo, core, par):
         ts(als, v("RS"), pn_last, A.is_ge)
         ts(v("P", K, C), v("PN"), pn_last, A.subtract, float(K), A.add)
         scan(v("P", 0, K), als, als, 0.0, A.add, A.max)
-        ts(v("DC", 0, K), v("RS"), pn_last, A.is_lt, -1000.0, A.mult)
         n = C if t == 0 else K
-        own = v("IOC") if t == 0 else v("PP", K, C)
+        ts(v("DA", 0, K), v("RS"), pn_last, A.is_ge, 1001.0, A.mult)
+        ts(v("DB", 1, K + 1), v("RS"), pn_last, A.is_ge, 1000.0, A.mult)
         if t == 0:
-            ts(v("DC", K, C), aln, 1.0, A.subtract, 1000.0, A.mult)
-        scan(v("AA0", 0, n), v("P", 0, n), v("DC", 0, n), 0.0, A.max, A.add)
-        scan(v("UU", 0, n), own, v("DC", 0, n), -1000.0, A.max, A.add)
-        tt(v("TT", 0, n), ind(own, jl(t, 7)), v("UU", 0, n), A.max)
-        tt(v("TT", C, C + n), ind(v("TT", 0, n), jl(t, 7)), v("UU", 0, n), A.max)
-        for k in range(1, 7):
-            cur = v("TT", C * k, C * k + n)
-            to_list(t, jl(t, k), cur)
-            if k < 6:
-                split(v("TT", C * k + C, C * k + C + n), cur, jl(t, k), SPL[t])
-        split(v("AA1", 0, n), v("AA0", 0, n), jl(t, 6), SPA[t])
-        split(v("AA0", 0, n), v("AA1", 0, n), jl(t, 6), SPA[t])
+            ts(v("DA", K, C), aln, 1001.0, A.mult)
+            ts(v("DB", K + 1, C + 1), aln, 1000.0, A.mult)
+        for h in range(2):
+            scan(v("AA%d" % h, 0, n), v("DA", 0, n), v("DB", 0, n), -1000.0, A.add, A.subtract)
+        small, large = v("AA0", 0, n), v("AA1", 0, n)
+        for k in range(10):
+            new = v("TT", C * (k % 7), C * (k % 7) + n)
+            tt(new, ind(large, jl(t, max(k - 1, 0))), small, A.max)
+            small, large = large, new
+            if k == 7:
+                a55 = new
         cs = []
         for b in range(12):
             o = 208 * b
@@ -354,18 +361,15 @@ def build(T, topo, core, par):
         tt(v("F64"), ind(v("ES"), v("REP")), v("C64H"), A.add)
         ts(v("EL"), v("F64", 0, 12), 0.5, A.mult)
         ts(v("L64"), v("F64"), 2.0, A.mult)
-        gather("s", v("PE"), v("PR") if t == 0 else v("PP"), v("EL"))
+        gather(v("PE"), v("PR") if t == 0 else v("PP"), v("EL"))
         to_list(t, v("PEL"), v("PE"))
-        gather("s", v("Q1"), v("TT", 6 * C, 6 * C + n), v("PEL"))
+        gather(v("Q1"), v("PJ"), v("EL"))
         to_list(t, v("QL"), v("Q1"))
-        tt(v("Y"), ind(v("AA0", 0, n), v("QL")), v("NEG"), A.max)
+        tt(v("Y1"), ind(a55, v("PEL")), v("NEG"), A.max)
+        tt(v("Y"), ind(large, v("QL")), v("Y1"), A.max)
         cs = []
         for j in range(4):
-            src = ind(v(X), v("L64", 16 * j, 16 * j + 12))
-            if j >= 4 - VPL[t]:
-                ts(v("VH", j, 4 * K, 4), src, 0.5, A.mult)
-            else:
-                cs.append(act(v("VH", j, 4 * K, 4), src, F.Copy, scale=0.5))
+            cs.append(act(v("VH", j, 4 * K, 4), ind(v(X), v("L64", 16 * j, 16 * j + 12)), F.Copy, scale=0.5))
             copy(v("VH2", j, 4 * K, 4), v("VH", j, 4 * K, 4))
         chain(cs)
         p1 = v("PP", 0, K)
@@ -400,7 +404,8 @@ def build(T, topo, core, par):
         lc, ls = v("LC", K * t, K * t + K), v("LS", 256 * t, 256 * t + K)
         add("r", ("arr%d" % t, 2 * len(topo.engines(prv, core))), [], [lc, ls], T_BYT * 0.55, "arr", T_REM, after=[s1, s2])
         if t + 1 < R:
-            to_list(t + 1, jl(t + 1, 7), p1)
+            to_list(t + 1, jl(t + 1, 0), p1)
+            tables(t + 1)
             ranks(t + 1, 0)
         else:
             ts(v("PL"), p1, -1.0, A.add)

@@ -1,9 +1,16 @@
 import numpy as np
 from concourse.bass import DstId, RemoteDMATransfer
-from concourse.mybir import dt, AluOpType, ActivationFunctionType
+from concourse.mybir import dt, AluOpType, ActivationFunctionType, AxisListType
 
 C, K, R = 384, 192, 3
 F32, BF, F16, I32, U16, U8, X4 = "float32", "bfloat16", "float16", "int32", "uint16", "uint8", "float8_e4m3fn_x4"
+
+FIB = [1, 2, 3, 5, 8, 13, 21, 34, 55, 89]
+ZS = [(0, 208), (0, 240), (0, 304), (32, C)]
+E = 1.0 / 512
+W = 200
+B = 208
+NB = 12 * 17
 
 SCRATCH = {}
 
@@ -17,9 +24,9 @@ for _t in range(R + 1):
     _decl("QX%d" % _t, C, X4)
     _decl("SX%d" % _t, C, U8)
 for _h in range(2):
-    for _n, _w, _d in [("MK", K, F32), ("HD", K, F32), ("NEQ", K, BF), ("NQS", K, BF), ("CMP", 12 * K, BF),
-                       ("JK", 12 * K, BF), ("RK", 12 * 96, BF), ("AL", 12, F32), ("AG", 12, F32), ("TA", 12, F32),
-                       ("OFF", 12, U16), ("AA", C, BF)]:
+    for _n, _w, _d in [("MK", K, F32), ("HD", K, F32), ("NEQ", 2 * K, BF), ("CMP", 12 * W, BF),
+                       ("JK", 12 * W, BF), ("RK", 12 * 96, BF), ("AL", 24, F32), ("SC", K, F32),
+                       ("OFF", 12, U16), ("ALV", K + 2, BF), ("DB", K + 2, F16), ("CM", K + 96, BF)]:
         _decl(_n + str(_h), _w, _d)
     _decl("PV%d" % _h, 512, F32, "psum")
     _decl("PS%d" % _h, 512, F32, "psum")
@@ -29,32 +36,34 @@ for _n, _w, _d in [
     ("H", R * 1024, BF), ("QH", R * 256, X4), ("SH", R * 256, U8), ("LC", R * K, X4), ("LS", R * 256, U8),
     ("U", 512, BF), ("QU", 128, X4), ("SU", 128, U8), ("QR", 128, X4), ("SR", 128, U8),
     ("WC", 512, X4), ("WS", 512, U8), ("ONES", 512, BF), ("EB", 2048, BF), ("QE", 512, X4), ("SE", 512, U8),
-    ("PTR", 24, I32), ("PC", 1, I32), ("AI", 1, I32), ("QI", 1, I32), ("I16", 12, I32), ("UL", 8, U16),
-    ("COL", 16, F32), ("IOTA", K, F32), ("J16", K, BF), ("J4", 16, BF), ("C64", 64, F32), ("C64H", 64, F32),
-    ("NB", 12, F32), ("NE", 12, F32), ("REPG", 4, F32), ("REP", 4, U16), ("IOC", C, BF),
-    ("CM0", K, BF), ("CMIN", K, BF), ("R16", K, BF), ("KEEP", K, BF), ("T1", 96, BF), ("A16", 24, U16),
-    ("HOLDA", C, BF), ("HOLDB", K, BF), ("HOLD4", K, BF), ("NEG", K, BF),
-    ("SC", C, F32), ("SREV", K, F32), ("RS", K, BF), ("ALV", C, BF), ("PN", K, BF), ("P", C, BF),
-    ("JKE", 12 * 208, BF), ("ES", 12 * 104, F32), ("F64", 64, F32), ("L64", 64, U16), ("EL", 12, U16),
-    ("PE", K, BF), ("PEL", 12, U16), ("Q1", K, BF), ("QL", 12, U16), ("Y", K, BF), ("H4", K, BF), ("L4", 48, U16),
-    ("VH", 4 * K, BF), ("VH2", 4 * K, BF), ("TT", 7 * C, BF), ("PR", C, BF), ("PP", C, BF),
-    ("JL", 9 * 24, U16), ("JR", 8 * C, BF), ("PJ", C, BF), ("Y1", K, BF), ("DA", C, F16), ("DB", C + 2, F16),
-    ("HSA", 4 * C, F16), ("HSB", 4 * K, BF), ("PL", K, F32), ("YB", C, F32),
+    ("PTR", 24, I32), ("PI", 16, I32), ("UL", 8, U16),
+    ("COL", 40, F32), ("IOTA", K, F32), ("J16", K + 16, BF), ("NGB", 12, F32), ("IOC", C + K, BF),
+    ("CMIN", 2 * K, BF), ("R16", 2 * K, BF), ("T1", 96, BF), ("A16", 24, U16),
+    ("HOLD", 2 * C + 2 * K + B, BF), ("IOS", C + K, BF), ("TAB", 24, F32),
+    ("SREV", K, F32), ("RS", B, BF), ("SM", 256, F32), ("PIV", 12, F32), ("G16", 16, F32),
+    ("J48", 48, F32), ("OL", 6, U16), ("PB", C, BF), ("FP", C + 2, BF), ("DF", C, BF), ("VV", C, BF), ("PN", K, BF),
+    ("L64", 64, U16), ("EL", 16, U16), ("H4", K, BF), ("L4", 48, U16),
+    ("VH", 4 * K, BF), ("VH2", 4 * K, BF), ("TR", len(FIB) * C, BF), ("ZR", 2 * C, BF), ("AP", C, BF),
+    ("PR", C, BF), ("PP", C, BF), ("PE", K, BF), ("PEL", 12, U16), ("J1", 60, U16), ("JL", len(FIB) * 24, U16),
+    ("DA", C, F16), ("HSA", 3 * C, F16), ("HSB", 6 * K, BF), ("PL", K, F32), ("YB", C, F32),
+    ("KF", 9 * B, F32), ("KL", 3 * 14, U16), ("M0", 3 * K, BF), ("JR", 3 * K, BF), ("MR", 6 * K, BF), ("TB", 224, BF),
+    ("TP", 416, BF), ("PS", 2 * B, F32), ("BK", 10 * B, BF),
 ]:
     _decl(_n, _w, _d)
 
 NDMA = 24
 SEMAPHORES = ["cv", "cs", "cp", "cg", "sent"] + ["arr%d" % _t for _t in range(R)] + ["d%d" % _k for _k in range(NDMA)]
 
-NS = {(0, 0): 5, (0, 1): 4, (1, 0): 4, (1, 1): 4, (2, 0): 4, (2, 1): 4}
-EV = {0: 0, 1: 1, 2: 1}
-CP = {"relu": "svssvsvs", "dec": "ssvs"}
+NS = {(0, 0): (0, 4), (0, 1): (0, 5), (1, 0): (0, 5), (1, 1): (0, 5), (2, 0): (0, 5), (2, 1): (0, 5)}
+CP = {"relu": "svssvsvs", "dec": "ssvs", "jump": "ssssvvvvs", "vh": "ssss", "vh2": "ggvv", "twin": "sss"}
+LOW = 128
 PARTS = [(0, 128, 128), (128, K, 256)]
 
 SETS = [(0.83, 200, 1.55, 3.8, 150, 1500, 600, 900), (0.83, 120, 1.55, 3.8, 150, 3500, 800, 900),
         (1.2, 200, 1.9, 5.0, 260, 1800, 800, 1300), (1.0, 150, 1.2, 2.5, 180, 2200, 500, 1200),
         (0.9, 250, 1.3, 4.5, 200, 1500, 400, 700)]
-T_DMA, ROUNDS, STEPS, HEAT = 2000.0, 16, 20000, 0.0012
+WEIGHT = [2.0, 1.0, 1.0, 1.0, 1.0]
+T_DMA, ROUNDS, STEPS, HEAT = 2000.0, 6, 40000, 0.0003
 
 
 def build(T, topo, core, par):
@@ -70,6 +79,9 @@ def build(T, topo, core, par):
 
     def col(name, j):
         return (name, j, j + 1, 1)
+
+    def sub(w, a, b, s=1):
+        return (w[0], w[1] + a, w[1] + b, s)
 
     def ap(w):
         if isinstance(w, tuple) and w[0] == "ind":
@@ -116,6 +128,12 @@ def build(T, topo, core, par):
             return add("v", lambda q: q.tensor_copy(ap(out), ap(in_)), [in_, out[2]], [out[1]], vdur(out, [in_]))
         return add("v", lambda q: q.tensor_copy(ap(out), ap(in_)), [in_], [out], vdur(out, [in_]))
 
+    def turn32(out, in_):
+        return add("v", lambda q: q.transpose(ap(out), ap(in_)), [in_], [out], vdur(out, [in_]))
+
+    def fill(out, c):
+        return add("v", lambda q: q.memset(ap(out), c), [], [out], CYC * max(64, cnt(out)))
+
     def ts(out, in0, s1, op0, s2=None, op1=None):
         if op1 is None:
             fn = lambda q: q.tensor_scalar(ap(out), ap(in0), ap(s1), None, op0)
@@ -132,6 +150,10 @@ def build(T, topo, core, par):
         return add("v", lambda q: q.tensor_tensor_scan(ap(out), ap(d0), ap(d1), ap(init), op0, op1), [d0, d1, init],
                    [out], vdur(out, [d0, d1]))
 
+    def reduce(out, in_, op):
+        return add("v", lambda q: q.tensor_reduce(ap(out), ap(in_), AxisListType.X, op), [in_], [out],
+                   CYC * max(64, cnt(in_)))
+
     def act(out, in_, func, bias=None, scale=None, acc=None):
         kw = {}
         if bias is not None:
@@ -140,11 +162,14 @@ def build(T, topo, core, par):
             kw["scale"] = scale
         if acc is not None:
             kw["accum_out"] = ap(acc)
-        d = 65 + GATH * CYC * cnt(out) if in_[0] == "ind" else CYC * max(64, cnt(out)) + 30 + (25 if acc else 0)
+        d = (65 + GATH * CYC * cnt(out) if in_[0] == "ind" else CYC * max(64, cnt(out)) + 30) + (25 if acc else 0)
         return add("s", lambda q: q.activation(ap(out), ap(in_), func, **kw), [in_, bias], [out, acc], d)
 
     def gather(out, win, off):
         return act(out, ind(win, off), F.Copy)
+
+    def take(e, out, win, off):
+        return gather(out, win, off) if e == "s" else copy(out, ind(win, off))
 
     def quant(qc, qs, in_):
         return add("v", lambda q: q.quantize_mx(ap(qc), ap(qs), ap(in_)), [in_], [qc, qs],
@@ -162,6 +187,15 @@ def build(T, topo, core, par):
             fn = lambda q: q.iota(ap(out), pattern, base, cm, allow_small_or_imprecise_dtypes=True)
         return add("g", fn, [], [out], 160 + 2 * CYC * cnt(out))
 
+    def select(out, in_, pattern, op, c, base, cm=0):
+        return add("g", lambda q: q.affine_select(ap(out), ap(in_), pattern, op, c, base, cm), [in_], [out],
+                   200 + 2 * CYC * cnt(out))
+
+    def twin(e, out, in_):
+        if e == "g":
+            return select(out, in_, [[0, cnt(out)]], A.is_ge, 0.0, 0)
+        return act(out, in_, F.Copy) if e == "s" else copy(out, in_)
+
     def dma(eng, out, in_, rd, wr, nbytes, after=()):
         return add(eng, lambda q: q.dma_start(out, in_), rd, wr, 100.0, "dma", T_DMA + nbytes / 200.0, after)
 
@@ -175,63 +209,114 @@ def build(T, topo, core, par):
     dma("y", u8(v("WC")), T.wc[:], [], [v("WC")], 262144, after=[xa, xb])
     dma("y", ap(v("WS")), T.ws[:], [], [v("WS")], 65536, after=[xa, xb])
 
-    iota(v("PC"), [[0, 1]], 0, 1)
-    iota(v("I16"), [[16, 12]], 0)
-    iota(v("J16"), [[0, 12], [1, 16]], 0)
+    pc, ai, qi, gi, i16 = col("PI", 0), col("PI", 1), col("PI", 2), col("PI", 3), v("PI", 8, 16)
+    j16, j4 = v("J16", 0, K), v("J16", K, K + 16)
+    ioc, negi = v("IOC", 0, C), v("IOC", C, C + K)
+    ios, iop = v("IOS", 0, C), v("IOS", C, C + K)
+    cmin, cm0, r16, keep = v("CMIN", 0, K), v("CMIN", K, 2 * K), v("R16", 0, K), v("R16", K, 2 * K)
+    holda, holdc, holdd = v("HOLD", 0, C), v("HOLD", C, 2 * C), v("HOLD", 2 * C, 2 * C + K)
+    hold4, holde = v("HOLD", 2 * C + K, 2 * C + 2 * K), v("HOLD", 2 * C + 2 * K)
+    iota(pc, [[0, 1]], 0, 1)
+    iota(i16, [[16, 8]], 0)
+    iota(j16, [[0, 12], [1, 16]], 0)
     iota(v("IOTA"), [[1, K]], 0)
-    iota(v("J4"), [[0, 4], [1, 4]], 0)
-    iota(v("IOC"), [[1, C]], -K)
-    iota(v("NEG"), [[-1, K]], -1)
-    iota(v("PP", K, C), [[1, K]], 1)
-    iota(v("NE"), [[16, 12]], 16)
-    iota(v("ES"), [[0, 12 * 104]], 0)
+    iota(j4, [[0, 4], [1, 4]], 0)
+    iota(ioc, [[1, C]], -K)
+    iota(negi, [[-1, K]], -1)
+    iota(v("NGB"), [[-16, 12]], -16)
+    t01, t16, tbig = v("TAB", 0, 2), v("TAB", 8, 10), v("TAB", 16, 18)
+    iota(t01, [[1, 2]], 0)
+    iota(t16, [[-16, 2]], 0)
     for h in range(2):
-        iota(col("AG%d" % h, 11), [[0, 1]], 0)
+        iota(col("ALV%d" % h, 0), [[0, 1]], 0)
     for t in range(R):
         iota(v("X%d" % (t + 1), 4 * K, 1024), [[0, 256]], 0)
         iota(v("H", 1024 * t + 4 * K, 1024 * t + 1024), [[0, 256]], 0)
-    iota(v("C64"), [[1, 4], [64, 16]], 416)
     iota(v("ONES"), [[0, 512]], 1)
     for b in range(4):
-        o = v("EB", 512 * b, 512 * b + 512)
-        add("g", lambda q, o=o, b=b: q.affine_select(ap(o), ap(v("ONES")), [[-1, 512]], A.is_equal, 0.0, b, 4),
-            [v("ONES")], [o], 200 + 2 * CYC * 512)
+        select(v("EB", 512 * b, 512 * b + 512), v("ONES"), [[-1, 512]], A.is_equal, 0.0, b, 4)
     quant(v("QE"), v("SE"), v("EB"))
-    a0, a1, q0, q1, fa, fb, f4, ah, f5, f6, f7 = [col("COL", j) for j in range(11)]
-    ts(v("AI"), v("PC"), 15, A.bitwise_and)
-    ts(v("QI"), v("AI"), 2, A.arith_shift_right)
-    copy(a0, v("AI"))
-    copy(q0, v("QI"))
+    (a0, a1, q0, q1, fe, f4, f5, f6, f7, f8, ns1, nb16, thr0, thr, cf, cfk, gam,
+     piv2, ns2, cst, pnc, cf2, up0, n1, n2, n1h, fc, fd) = [col("COL", j) for j in range(28)]
+    ts(ai, pc, 15, A.bitwise_and)
+    ts(qi, ai, 2, A.arith_shift_right)
+    ts(gi, pc, 4, A.arith_shift_right, 1, A.bitwise_and)
+    copy(a0, ai)
+    copy(q0, qi)
+    copy(gam, gi)
     ts(a1, a0, 1.0, A.add)
     ts(q1, q0, 1.0, A.add)
-    ts(ah, a0, 0.5, A.add)
-    ts(col("DB", 0), a0, 0.0, A.mult)
     ts(f7, a0, 15.0, A.is_lt, float(C), A.mult)
-    ts(fa, f7, float(K), A.add)
-    ts(fb, f7, 0.5, A.mult, -1.0, A.add)
-    ts(f5, q0, 3.0, A.is_lt, float(K), A.mult)
+    ts(fc, f7, float(K), A.add, E, A.mult)
+    ts(fd, f7, 0.5 * E, A.mult, -E, A.add)
+    ts(fe, f7, 2.0, A.mult)
+    ts(f5, q0, 3.0, A.is_lt, K * E, A.mult)
     ts(f6, a0, 0.25, A.mult, q0, A.subtract)
-    ts(f4, f5, f6, A.add, -1.0, A.add)
-    copy(v("UL"), v("I16", 0, 8))
-    ts(v("NB"), v("I16"), ah, A.add)
-    act(v("C64H"), v("C64"), F.Copy, scale=0.5)
-    ts(v("CM0"), v("J16"), a0, A.is_equal, 0.5, A.subtract)
-    ts(v("CMIN"), v("CM0"), 2.0 ** 97, A.mult)
-    ts(v("R16"), v("J16"), 0.5, A.subtract, 2.0 ** 97, A.mult)
-    ts(v("KEEP"), v("J16"), 1.0, A.min)
+    ts(f8, f6, -1.0, A.add, E, A.mult)
+    ts(f4, f8, f5, A.add)
+    ts(ns1, a0, -16.0, A.mult, -15.0, A.add)
+    ts(nb16, a0, -0.0625, A.mult)
+    ts(thr0, a0, 16.0, A.mult, 15.5, A.add)
+    ts(thr, thr0, K - 0.5, A.min)
+    ts(cf, a0, -1.0, A.mult, 2071.5, A.add)
+    ts(cfk, cf, float(K), A.add)
+    copy(col("FP", 0), cf)
+    for h in range(2):
+        fill(col("DB%d" % h, 0), -E)
+    act(ios, ioc, F.Copy, scale=E)
+    act(iop, negi, F.Copy, scale=-E)
+    act(v("PP", K, C), negi, F.Copy, scale=-E)
+    ts(tbig, t01, 0.5, A.subtract, 2.0 ** 97, A.mult)
+    fill(v("SM", K, 256), 2.0 ** 96)
+    copy(v("UL"), i16)
+    ts(cm0, j16, a0, A.is_equal, 0.5, A.subtract)
+    ts(cmin, cm0, 2.0 ** 97, A.mult)
+    ts(r16, j16, 0.5, A.subtract, 2.0 ** 97, A.mult)
+    ts(keep, j16, 1.0, A.min)
     ts(v("A16"), v("J16", 0, 24), 0.0, A.mult, a0, A.add)
-    ts(v("REPG"), v("A16", 0, 4), 11.0, A.min, 104.0, A.mult)
-    ts(v("REP"), v("REPG"), 103.0, A.add)
     ts(v("T1", 0, 16), v("J16", 0, 16), a0, A.is_equal, 1024.0, A.mult)
     ts(v("T1", 16, 32), v("J16", 0, 16), a1, A.is_equal, -float(C), A.mult)
     tt(v("T1", 32, 48), v("T1", 0, 16), v("T1", 16, 32), A.add)
-    gather(v("HOLDA"), v("T1", 32, 48), v("A16"))
-    act(v("HOLDB"), v("HOLDA", 0, K), F.Copy, scale=0.5)
-    ts(v("T1", 48, 64), v("J4"), q0, A.is_equal, 512.0, A.mult)
-    ts(v("T1", 64, 80), v("J4"), q1, A.is_equal, -float(K), A.mult)
+    gather(holda, v("T1", 32, 48), v("A16"))
+    act(holdc, holda, F.Copy, scale=E)
+    act(holdd, sub(holda, 0, K), F.Copy, scale=0.5 * E)
+    act(holde, sub(holda, 0, B), F.Copy, scale=2.0)
+    ts(v("T1", 48, 64), j4, q0, A.is_equal, 1.0, A.mult)
+    ts(v("T1", 64, 80), j4, q1, A.is_equal, -K * E, A.mult)
     tt(v("T1", 80, 96), v("T1", 48, 64), v("T1", 64, 80), A.add)
-    gather(v("HOLD4"), v("T1", 80, 96), v("A16", 0, 12))
+    gather(hold4, v("T1", 80, 96), v("A16", 0, 12))
     dma("y", T.pl[:, K:C], T["IOTA"][0:128:16, 0:K], [v("IOTA")], [], 6144)
+    kf = [v("KF", B * j, B * j + B) for j in range(9)]
+    bk = [v("BK", B * j, B * j + B) for j in range(10)]
+    st1, st2, reset = kf[6], kf[7], bk[0]
+    in17 = [[0, 12], [1, 17]]
+    iota(v("KF", 0, 3 * B), [[0, 3 * B]], 0)
+    for j in (3, 5, 8):
+        iota(sub(kf[j], NB, B), [[0, B - NB]], 0)
+    iota(reset, [[0, B]], 0)
+    iota(v("TB"), [[0, 224]], 0)
+    iota(v("RS", K, K + 2), [[-257, 2]], 256)
+    iota(sub(kf[3], 0, NB), [[16, 12], [1, 17]], 0)
+    iota(sub(kf[4], 0, NB), [[16, 12], [1, 17]], -1)
+    iota(sub(kf[5], 0, NB), [[0, 6], [1, 2], [0, 17]], 0)
+    iota(sub(kf[8], 0, NB), [[1008, 12], [-1, 17]], 1023)
+    iota(sub(st2, 0, 12), [[2, 12]], 2)
+    select(sub(kf[8], 0, NB), sub(kf[8], 0, NB), in17, A.not_equal, 100.0 / E, -16)
+    select(sub(reset, 0, NB), sub(reset, 0, NB), in17, A.not_equal, -100.0, 0)
+    select(sub(kf[0], 0, NB), sub(kf[3], 0, NB), in17, A.not_equal, float(K), -16)
+    select(sub(kf[1], 0, NB), sub(kf[4], 0, NB), in17, A.not_equal, float(K + 1), 0)
+    act(st1, kf[8], F.Copy, scale=E)
+    ts(kf[5], kf[5], gam, A.not_equal, float(B), A.mult)
+    tt(kf[2], kf[5], kf[3], A.add)
+    kl = [v("KL", 14 * j, 14 * j + 13) for j in range(3)]
+    for j in range(3):
+        scan(kf[3 + j], holde, kf[j], 0.0, A.add, A.min)
+        ts(kl[j], sub(kf[3 + j], 15, B, 16), fe, A.add)
+    m0, m1, mb = [v("M0", K * j, K * j + K) for j in range(3)]
+    iota(mb, [[2, 12], [0, 16]], 2)
+    act(m1, cm0, F.Relu, scale=64.0)
+    tt(m0, m1, mb, A.min)
+    act(m1, m0, F.Copy)
 
     quant(v("QU"), v("SU"), v("U"))
     add("v", lambda q: q.tensor_copy(ap(v("QR")).bitcast(dt.uint32), ap(v("QU")).bitcast(dt.uint32).indirect(ap(v("UL")))),
@@ -241,84 +326,155 @@ def build(T, topo, core, par):
     def half(t, h):
         return v("QX%d" % t, K * h, K * h + K), v("SX%d" % t, K * h, K * h + K), v("X%d" % t, 4 * K * h, 4 * K * h + 4 * K)
 
-    def ranks(t, h):
+    def scores(t, h):
         qc, qs, _x = half(t, h)
+        mm("PV%d" % h, v("QR"), v("SR"), qc, qs)
+        mm("PS%d" % h, v("QR"), v("SR"), qc, qs)
+
+    def ranks(t, h):
         s = str(h)
-        pv = v("PV" + s, 0, K)
-        mm("PV" + s, v("QR"), v("SR"), qc, qs)
-        mm("PS" + s, v("QR"), v("SR"), qc, qs)
-        sc = v("SC", K * h, K * h + K)
-        act(sc, v("PS" + s, 0, K), F.Copy)
-        tt(v("MK" + s), pv, v("CMIN"), A.min)
-        scan(v("HD" + s), v("R16"), v("MK" + s), 0.0, A.min, A.max)
-        tt(v("NEQ" + s), pv, v("HD" + s), A.not_equal)
-        scan(v("NQS" + s), v("KEEP"), v("NEQ" + s), 0.0, A.mult, A.add)
-        b0 = 12 - NS[(t, h)]
+        pv, ps = v("PV" + s, 0, K), v("PS" + s, 0, K)
+        neq, nqs = v("NEQ" + s, 0, K), v("NEQ" + s, K, 2 * K)
+        tt(v("MK" + s), pv, cmin, A.min)
+        scan(v("HD" + s), r16, v("MK" + s), 0.0, A.min, A.max)
+        tt(neq, pv, v("HD" + s), A.not_equal)
+        scan(nqs, keep, neq, 0.0, A.mult, A.add)
+        b0, b1 = NS[(t, h)]
         cv, cs = [], []
-        for b in range(b0 + 1):
-            if b < b0:
-                w, n, o = col("HD" + s, 16 * b + 15), 16 * b + 16, K * b
+        mine = list(range(b0)) + list(range(b1, 12))
+        for j in range(len(mine) + 1):
+            if j < len(mine):
+                b = mine[j]
+                w, n, o = col("HD" + s, 16 * b + 15), 16 * b + 16, W * b
                 cv.append(ts(v("CMP" + s, o, o + n), v("PV" + s, 0, n), w, A.is_ge))
                 if n < K:
                     cv.append(ts(v("CMP" + s, o + n, o + K), v("PV" + s, n, K), w, A.is_gt))
-            if b > 0:
-                o = K * b - K
-                cv.append(scan(v("RK" + s, 96 * b - 96, 96 * b), v("CMP" + s, o, o + 96), v("CMP" + s, o + 96, o + K),
-                               col("NQS" + s, 16 * b - 1), A.add, A.add))
-        for b in range(b0, 13):
-            if b < 12:
-                cs.append(act(v("CMP" + s, K * b, K * b + K), sc, F.Sign, bias=col("HD" + s, 16 * b + 15), scale=-1.0))
+            if j > 0:
+                b = mine[j - 1]
+                o = W * b
+                cv.append(scan(v("RK" + s, 96 * b, 96 * b + 96), v("CMP" + s, o, o + 96), v("CMP" + s, o + 96, o + K),
+                               sub(nqs, 16 * b + 15, 16 * b + 16), A.add, A.add))
+        tt(v("CMP" + s, K + W * b0, W * b1, W), v("NGB", b0, b1), sub(nqs, 16 * b0 + 15, 16 * b1, 16), A.subtract)
+        for b in range(b0, b1 + 1):
+            if b < b1:
+                cs.append(act(v("CMP" + s, W * b, W * b + K), ps, F.Sign, bias=col("HD" + s, 16 * b + 15), scale=-1.0))
             if b > b0:
-                n, o = 16 * b, K * b - K
+                n, o = 16 * b, W * b - W
                 cs.append(act(v("JK" + s, o, o + n), v("CMP" + s, o, o + n), F.Relu, acc=col("AL" + s, b - 1)))
-                if n < K:
-                    cs.append(act(v("JK" + s, o + n, o + K), v("CMP" + s, o + n, o + K), F.Relu, scale=-1.0,
-                                  acc=col("AG" + s, b - 1)))
+                cs.append(act(v("JK" + s, o + n, o + K + 1), v("CMP" + s, o + n, o + K + 1), F.Relu, scale=-1.0,
+                              acc=col("AL" + s, 11 + b)))
         chain(cv)
         chain(cs)
-        tt(v("TA" + s, b0, 12), v("NQS" + s, 16 * b0 + 15, K, 16), v("NE", b0, 12), A.add)
-        for b in range(b0, 12):
-            scan(col("RK" + s, 96 * b + 95), col("AG" + s, b), col("AL" + s, b), col("TA" + s, b), A.add, A.subtract)
-        rk = v("RK" + s, 95, 12 * 96, 96)
+        tt(v("RK" + s, 96 * b0 + 95, 96 * b1, 96), v("AL" + s, 12 + b0, 12 + b1), v("AL" + s, b0, b1), A.subtract)
+        rk, off = v("RK" + s, 95, 12 * 96, 96), v("OFF" + s)
+        if h == 0 or t == 0:
+            act(v("SC" + s), ps, F.Copy)
         if h == 0:
-            ts(v("OFF0"), rk, -1.0, A.mult, float(K - 1 + 16), A.add)
-            copy(ind(v("SREV"), v("OFF0")), sc)
-            gather(v("RS"), v("IOTA"), v("OFF0"))
+            ts(off, rk, -1.0, A.mult, float(K - 1 + 16), A.add)
+            copy(ind(v("SREV"), off), v("SC0"))
+            gather(v("RS", 0, K), v("IOTA"), off)
+            if t > 0:
+                scan(v("PIV"), sub(cmin, 0, 12), v("SREV", 15, K, 16), 0.0, A.max, A.min)
+                scan(v("SM", 0, K), cmin, v("SREV"), 0.0, A.max, A.min)
+                gather(bk[1], v("RS", 0, K + 2), kl[0])
+                gather(bk[2], v("RS", 0, K + 2), kl[1])
         else:
-            ts(v("OFF1"), rk, -16.0, A.add)
+            ts(off, rk, -16.0, A.add)
 
-    def jl(t, k):
-        return v("JL", 24 * k, 24 * k + (24 if t == 0 else 12))
+    def search():
+        pv = v("PV1", 0, K)
+        for lv, (pivot, start) in enumerate(((col("PIV", 11), ns1), (piv2, ns2))):
+            cm, ol = "CM%d" % lv, col("OL", 2 * lv)
+            ts(v(cm, 0, K), pv, pivot, A.is_gt)
+            scan(v(cm, K, K + 96), v(cm, 0, 96), v(cm, 96, K), start, A.add, A.add)
+            ts(ol, col(cm, K + 95), 1.0, A.min)
+            if lv == 0:
+                tt(v("G16"), ind(tbig, ol), v("SM", 15, 256, 16), A.max)
+                reduce(piv2, v("G16"), A.min)
+                act(v("J48", 0, 16), ind(t16, ol), F.Identity, bias=nb16, acc=ns2)
+                act(v("J48", 16, 32), ind(t01, ol), F.Identity, acc=cst)
+            else:
+                act(v("J48", 32, 48), ind(t01, ol), F.Identity, bias=cst, acc=pnc)
 
     turn = [0]
 
     def to_list(t, out, rep):
-        turn[0] = (turn[0] + 1) % 4
+        turn[0] = (turn[0] + 1) % 6
         n = cnt(rep)
-        if t == 0:
-            o = C * turn[0]
-            scan(v("HSA", o, o + n), v("HOLDA", 0, n), rep, 0.0, A.add, A.min)
-            ts(out, v("HSA", o + 15, o + n, 16), fa, A.add)
-        else:
-            o = K * turn[0]
-            scan(v("HSB", o, o + n), v("HOLDB"), rep, 0.0, A.add, A.min)
-            ts(out, v("HSB", o + 15, o + n, 16), fb, A.add)
+        buf, o, hold, f = ("HSA", C * (turn[0] % 3), holdc, fc) if t == 0 else ("HSB", K * turn[0], holdd, fd)
+        scan(v(buf, o, o + n), sub(hold, 0, n), rep, 0.0, A.add, A.min)
+        ts(out, v(buf, o + 15, o + n, 16), f, A.add, 1.0 / E, A.mult)
 
-    def tables(t):
-        n = C if t == 0 else K
-        cur = v("PR") if t == 0 else v("PP", 0, K)
-        for k in range(1, 9):
-            new = v("PJ", K, C) if (k == 8 and t > 0) else v("JR", C * (k - 1), C * (k - 1) + n)
-            gather(new, cur, jl(t, max(k - 2, 0)))
-            to_list(t, jl(t, k), new)
-            cur = new
-        gather(v("PJ", 0, n), cur, jl(t, 0))
+    def climb():
+        def both(out, win, k, c0, c1):
+            for e, a, b in (("v", c0, LOW), ("s", LOW, c1)):
+                take(e, sub(out, a, b), sub(win, 0, b), v("JL", 24 * k + a // 16, 24 * k + b // 16))
+
+        tr = [v("TR", C * k, C * k + C) for k in range(len(FIB))]
+        z = [v("ZR", 0, C), v("ZR", C, 2 * C)]
+        tt(tr[0], ind(ios, v("J1", 0, 24)), v("AP"), A.max)
+        tt(tr[1], ind(tr[0], v("J1", 0, 24)), v("AP"), A.max)
+        n = len(FIB)
+        for k in range(n + 2):
+            if 2 <= k < n:
+                both(tr[k], tr[k - 1], k - 2, 0, C)
+            i = k - (n + 2 - len(ZS))
+            if i >= 0:
+                both(z[1 - i % 2], z[i % 2], k - 2, *ZS[i])
+            if k < n:
+                to_list(0, v("JL", 24 * k, 24 * k + 24), tr[k])
+        return z[0]
+
+    def blocks(p1):
+        j = {d: v("J1", 12 * i, 12 * i + 12) for i, d in enumerate((1, 2, 4, 8))}
+        p = {1: p1, 2: v("JR", 0, K), 4: v("JR", K, 2 * K), 8: v("JR", 2 * K, 3 * K)}
+        to_list(1, j[1], p1)
+        for d in (2, 4, 8):
+            gather(p[d], p[d // 2], j[d // 2])
+            to_list(1, j[d], p[d])
+        m = {1: (m0, m1), 16: (v("TB", 16, 16 + K), None)}
+        for i, d in enumerate((2, 4, 8, 16)):
+            if d < 16:
+                m[d] = (v("MR", 2 * K * i, 2 * K * i + K), v("MR", 2 * K * i + K, 2 * K * i + 2 * K))
+            tt(m[d][0], ind(m[d // 2][0], j[d // 2]), m[d // 2][1], A.max)
+            if d < 16:
+                twin(CP["twin"][i], m[d][1], m[d][0])
+        turn32(v("TP", 0, K), m[16][0])
+        turn32(v("TP", K, 416), v("TB"))
+        gather(bk[4], v("PP"), kl[0])
+        gather(bk[5], v("TP"), kl[2])
+        tt(v("PS", 0, B), ind(v("TP"), kl[2]), bk[4], A.subtract)
+        scan(v("PS", B, B + NB), sub(reset, 0, NB), v("PS", 0, NB), -4.0, A.add, A.max)
+        scan(sub(bk[3], 0, NB), sub(bk[5], 0, NB), sub(st1, 0, NB), 0.0, A.max, A.subtract)
+        tt(sub(bk[3], 16, NB, 17), sub(st2, 0, 12), v("PS", B + 15, B + NB, 17), A.subtract)
+
+    def jump(pn):
+        n0, n1_, dl, near = [sub(bk[j], 0, NB) for j in (6, 7, 8, 9)]
+        ts(n0, sub(bk[2], 0, NB), pn, A.is_ge, 2.0, A.add)
+        ts(n1_, sub(bk[1], 0, NB), pn, A.is_ge, 2.0, A.add)
+        scan(dl, n0, n1_, 0.0, A.max, A.subtract)
+        scan(near, dl, sub(bk[3], 0, NB), -4.0, A.add, A.max)
+        l = {d: v("JL", 12 * i, 12 * i + 12) for i, d in enumerate((1, 2, 3, 5))}
+        r = {1: v("TR", 0, K), 2: v("TR", K, 2 * K), 3: v("TR", 0, K), 5: v("TR", 2 * K, 3 * K)}
+        z = [v("ZR", 0, K), v("ZR", C, C + K)]
+        e = CP["jump"]
+        ts(l[1], sub(near, 16, NB, 17), 1.0 / E, A.mult, -1.0, A.add)
+        take(e[0], r[1], iop, l[1])
+        take(e[1], r[2], r[1], l[1])
+        to_list(1, l[2], r[2])
+        take(e[2], sub(r[3], 0, 160), r[2], sub(l[1], 0, 10))
+        to_list(1, sub(l[3], 2, 7), sub(r[3], 32, 112))
+        take(e[3], sub(r[5], 64, K), r[3], sub(l[2], 4, 12))
+        to_list(1, sub(l[5], 4, 12), sub(r[5], 64, K))
+        for i, (d, c0, c1) in enumerate(((1, 0, 1), (1, 0, 2), (2, 0, 4), (3, 2, 7), (5, 4, 12))):
+            take(e[4 + i], sub(z[1 - i % 2], 16 * c0, 16 * c1), z[i % 2], sub(l[d], c0, c1))
+        return z[1]
 
     quant(*half(0, 0))
     quant(*half(0, 1))
-    copy(jl(0, 0), v("PTR"))
-    gather(v("PR"), v("IOC"), jl(0, 0))
-    tables(0)
+    copy(v("J1", 0, 24), v("PTR"))
+    gather(v("PR"), ios, v("J1", 0, 24))
+    scores(0, 0)
     ranks(0, 0)
     rid, pid, _e = topo.addr(nxt)
     mask = topo.mask(core, nxt)
@@ -326,56 +482,64 @@ def build(T, topo, core, par):
     halves = [sum(1 << e for e in eng[:len(eng) // 2]), sum(1 << e for e in eng[len(eng) // 2:])]
     for t in range(R):
         X, Xn = "X%d" % t, "X%d" % (t + 1)
-        ranks(t, 1)
-        aln, als, pn_last = v("ALV", K, C), v("ALV", 0, K), col("PN", K - 1)
-        tt(aln, ind(v("SREV"), v("OFF1")), v("SC", K, C), A.is_lt)
-        scan(v("PN"), aln, aln, 0.0, A.add, A.max)
-        ts(als, v("RS"), pn_last, A.is_ge)
-        ts(v("P", K, C), v("PN"), pn_last, A.subtract, float(K), A.add)
-        scan(v("P", 0, K), als, als, 0.0, A.add, A.max)
-        n = C if t == 0 else K
-        ts(v("DA", 0, K), v("RS"), pn_last, A.is_ge, 1001.0, A.mult)
-        ts(v("DB", 1, K + 1), v("RS"), pn_last, A.is_ge, 1000.0, A.mult)
+        scores(t, 1)
+        al = [v("ALV%d" % h, 1, K + 1) for h in range(2)]
         if t == 0:
-            ts(v("DA", K, C), aln, 1001.0, A.mult)
-            ts(v("DB", K + 1, C + 1), aln, 1000.0, A.mult)
+            ranks(t, 1)
+            tt(al[1], ind(v("SREV"), v("OFF1")), v("SC1"), A.is_lt)
+            scan(v("PN"), al[1], al[1], 0.0, A.add, A.max)
+            pn = col("PN", K - 1)
+        else:
+            search()
+            ranks(t, 1)
+            pn = pnc
+            ts(al[1], ind(v("IOTA"), v("OFF1")), pn, A.is_lt)
+        rs = v("RS", 0, K)
+        ts(al[0], rs, pn, A.is_ge)
+        ts(v("DA", 0, K), rs, pn, A.is_ge, 1.0 - E, A.mult)
+        for k in range(2):
+            scan(v("ZR", C * k, C * k + K), v("ALV0", 0, K), v("DA", 0, K), 1.0, A.add, A.subtract)
+        if t == 0:
+            ts(v("DB0", 1, K + 1), rs, pn, A.is_ge, E, A.subtract)
+            ts(v("DB1", 1, K + 1), al[1], E, A.subtract)
+            ts(v("DA", K, C), al[1], 1.0 - E, A.mult)
+            ts(up0, pn, -E, A.mult, K * E + 1.0, A.add)
+            scan(v("AP", 0, K), al[0], v("DB0", 0, K), -1.0 - (K + 1) * E, A.add, A.subtract)
+            scan(v("AP", K, C), al[1], v("DB1", 0, K), -1.0 - E, A.add, A.subtract)
+            for k in range(2):
+                scan(v("ZR", C * k + K, C * k + C), v("ALV1", 0, K), v("DA", K, C), up0, A.add, A.subtract)
+            found = climb()
+        else:
+            found = jump(pn)
+        scan(v("PB", 0, K), al[0], al[0], 0.0, A.add, A.max)
+        scan(v("PB", K, C), al[1], al[1], col("PB", K - 1), A.add, A.max)
+        ts(cf2, pn, -1.0, A.mult, cfk, A.add)
         for h in range(2):
-            scan(v("AA%d" % h, 0, n), v("DA", 0, n), v("DB", 0, n), -1000.0, A.add, A.subtract)
-        small, large = v("AA0", 0, n), v("AA1", 0, n)
-        for k in range(10):
-            new = v("TT", C * (k % 7), C * (k % 7) + n)
-            tt(new, ind(large, jl(t, max(k - 1, 0))), small, A.max)
-            small, large = large, new
-            if k == 7:
-                a55 = new
-        cs = []
-        for b in range(12):
-            o = 208 * b
-            if b < EV[t]:
-                ts(v("JKE", o, o + 208), v("P", 16 * b, 16 * b + 208), col("NB", b), A.is_le, 2.0, A.mult)
-                scan(v("ES", 104 * b, 104 * b + 104), v("JKE", o, o + 104), v("JKE", o + 104, o + 208), -208.0, A.add, A.add)
-            else:
-                cs.append(act(v("JKE", o, o + 208), v("P", 16 * b, 16 * b + 208), F.Sign, bias=col("NB", b), scale=-1.0,
-                              acc=col("ES", 104 * b + 103)))
-        chain(cs)
-        tt(v("F64"), ind(v("ES"), v("REP")), v("C64H"), A.add)
-        ts(v("EL"), v("F64", 0, 12), 0.5, A.mult)
-        ts(v("L64"), v("F64"), 2.0, A.mult)
-        gather(v("PE"), v("PR") if t == 0 else v("PP"), v("EL"))
+            fp = v("FP", K * h + 1, K * h + K + 1)
+            scan(fp, al[h], al[h], (cf, cf2)[h], A.add, A.max)
+            scan(v("DF", K * h, K * h + K), fp, v("FP", K * h, K * h + K), 0.0, A.max, A.subtract)
+            act(v("JK%d" % h, 0, K), v("PB", K * h, K * h + K), F.Sign, bias=thr, scale=-1.0, acc=(n1, n2)[h])
+        scan(v("VV"), v("DF"), ios, -K * E, A.add, A.min)
+        ts(n1h, n1, 0.5, A.mult, float(K), A.add)
+        at = col("OL", 4)
+        ts(at, n2, 0.5, A.mult, n1h, A.add)
+        ts(v("EL"), ind(v("VV"), at), 1.0 / E, A.mult, float(K), A.add)
+        gather(v("PE"), v("PR") if t == 0 else v("PP"), v("EL", 0, 12))
         to_list(t, v("PEL"), v("PE"))
-        gather(v("Q1"), v("PJ"), v("EL"))
-        to_list(t, v("QL"), v("Q1"))
-        tt(v("Y1"), ind(a55, v("PEL")), v("NEG"), A.max)
-        tt(v("Y"), ind(large, v("QL")), v("Y1"), A.max)
         cs = []
         for j in range(4):
-            cs.append(act(v("VH", j, 4 * K, 4), ind(v(X), v("L64", 16 * j, 16 * j + 12)), F.Copy, scale=0.5))
-            copy(v("VH2", j, 4 * K, 4), v("VH", j, 4 * K, 4))
+            ts(v("L64", 16 * j, 16 * j + 16), ind(v("VV"), at), 4.0 / E, A.mult, float(4 * K + j), A.add)
+            src = ind(v(X), v("L64", 16 * j, 16 * j + 12))
+            if CP["vh"][j] == "s":
+                cs.append(act(v("VH", j, 4 * K, 4), src, F.Copy, scale=0.5))
+            else:
+                ts(v("VH", j, 4 * K, 4), src, 0.5, A.mult)
+            twin(CP["vh2"][j], v("VH2", j, 4 * K, 4), v("VH", j, 4 * K, 4))
         chain(cs)
         p1 = v("PP", 0, K)
-        act(p1, v("Y"), F.Abs)
-        scan(v("H4"), v("HOLD4"), p1, 0.0, A.add, A.min)
-        ts(v("L4"), v("H4", 3, K, 4), f4, A.add, 4.0, A.mult)
+        tt(p1, ind(found, v("PEL")), iop, A.min)
+        scan(v("H4"), hold4, p1, 0.0, A.add, A.min)
+        ts(v("L4"), v("H4", 3, K, 4), f4, A.add, 4.0 / E, A.mult)
         arr = T.sem["arr%d" % t]
         for i, (c0, c1, c2) in enumerate(PARTS):
             tt(v(Xn, 4 * c0, 4 * c1), ind(v("VH"), v("L4", c0 // 4, c1 // 4)), v("VH2", 4 * c0, 4 * c1), A.add)
@@ -383,7 +547,7 @@ def build(T, topo, core, par):
             quant(qc, qs, v(Xn, 4 * c0, 4 * c2))
             h0, g0, l0 = 1024 * t, 256 * t, K * t
             for b in range(4):
-                bank = "D%d" % b if i == 0 else ("PV1", "PS1", "PV0", "PS0")[b]
+                bank = "D%d" % b if i == 0 else ("PV1", "PS1", "D0", "D1")[b]
                 mm(bank, v("WC", 128 * b, 128 * b + 128), v("WS", 128 * b, 128 * b + 128), qc, qs)
                 o = v("H", h0 + 4 * c0 + b, h0 + 4 * c1, 4)
                 if CP["relu"][4 * i + b] == "s":
@@ -404,11 +568,11 @@ def build(T, topo, core, par):
         lc, ls = v("LC", K * t, K * t + K), v("LS", 256 * t, 256 * t + K)
         add("r", ("arr%d" % t, 2 * len(topo.engines(prv, core))), [], [lc, ls], T_BYT * 0.55, "arr", T_REM, after=[s1, s2])
         if t + 1 < R:
-            to_list(t + 1, jl(t + 1, 0), p1)
-            tables(t + 1)
+            blocks(p1)
+            scores(t + 1, 0)
             ranks(t + 1, 0)
         else:
-            ts(v("PL"), p1, -1.0, A.add)
+            ts(v("PL"), p1, 1.0 / E, A.mult, -1.0, A.add)
             dma("y", T.pl[:, 0:K], T["PL"][0:128:16, 0:K], [v("PL")], [], 6144)
         for b in range(4):
             mm("D%d" % b, v("QE", 128 * b, 128 * b + 128), v("SE", 128 * b, 128 * b + 128), lc, ls)
@@ -537,37 +701,78 @@ def order(ops, costs):
     near, eng = [o["near"] for o in ops], [o["e"] for o in ops]
     hard = [[(d, 0.0) for d in o["near"]] for o in ops]
     seq = by_key(best[1], hard, fwd)
-    base = [span(seq, near, eng, c) for c in costs]
-    wts = [2.0] + [1.0] * (len(costs) - 1)
+    names = sorted(set(eng))
+    queue = [names.index(e) for e in eng]
+    after = [[] for o in ops]
+    for o in ops:
+        for d in o["near"]:
+            after[d].append(o["k"])
+    gap = 24
 
-    def score(q):
-        return sum(w * span(q, near, eng, c) / b for w, c, b in zip(wts, costs, base)) / sum(wts)
+    def run(q, i0, old):
+        res = []
+        for c, (dur, lat, w) in enumerate(costs):
+            j0 = i0 // gap
+            if old is None:
+                en, free, snap = [0.0] * n, [0.0] * len(names), []
+            else:
+                en, snap = list(old[c][0]), old[c][1][:j0]
+                free = list(old[c][1][j0])
+            for i in range(j0 * gap, n):
+                if i % gap == 0:
+                    snap.append(list(free))
+                k = q[i]
+                e = queue[k]
+                t = free[e] - w
+                for j in near[k]:
+                    if en[j] > t:
+                        t = en[j]
+                t += w + dur[k]
+                free[e] = t
+                en[k] = t + lat[k]
+            res.append((en, snap))
+        return res
 
-    cur = top = score(seq)
-    now, pairs, key = seq, None, None
+    now = run(seq, 0, None)
+    base = [max(r[0]) for r in now]
+    wts = [WEIGHT[c] / base[c] / sum(WEIGHT) for c in range(len(costs))]
+    cur = top = 1.0
+    best_seq, pairs, pos = seq, None, None
     for it in range(STEPS):
         if pairs is None:
-            pairs = [tight(now, near, eng, c) for c in costs]
-            key = [0.0] * n
-            for j, k in enumerate(now):
-                key[k] = float(j)
-        pr = pairs[int(rng.integers(0, len(costs)))]
-        if not pr:
+            pairs = {}
+            pos = [0] * n
+            for j, k in enumerate(seq):
+                pos[k] = j
+        c = int(rng.integers(0, len(costs)))
+        if c not in pairs:
+            pairs[c] = tight(seq, near, eng, costs[c])
+        if not pairs[c]:
             continue
-        a, b = pr[int(rng.integers(0, len(pr)))]
-        k2 = list(key)
-        far = float(rng.integers(0, 2)) * float(rng.exponential(8.0))
+        a, b = pairs[c][int(rng.integers(0, len(pairs[c])))]
+        far = int(rng.integers(0, 2)) * int(rng.exponential(8.0))
         if rng.random() < 0.5:
-            k2[b] = key[a] - 0.5 - far
+            i0, i1 = max(0, pos[a] - far), pos[b] + 1
+            move = {b}
+            for k in reversed(seq[i0:i1]):
+                if k in move:
+                    move.update(near[k])
+            mid = [k for k in seq[i0:i1] if k in move] + [k for k in seq[i0:i1] if k not in move]
         else:
-            k2[a] = key[b] + 0.5 + far
-        q = by_key(k2, hard, fwd)
-        e = score(q)
+            i0, i1 = pos[a], min(n, pos[b] + 1 + far)
+            move = {a}
+            for k in seq[i0:i1]:
+                if k in move:
+                    move.update(after[k])
+            mid = [k for k in seq[i0:i1] if k not in move] + [k for k in seq[i0:i1] if k in move]
+        q = seq[:i0] + mid + seq[i1:]
+        res = run(q, i0, now)
+        e = sum(w * max(r[0]) for w, r in zip(wts, res))
         if e < cur or rng.random() < np.exp((cur - e) / (HEAT * (1.0 - it / STEPS) + 1e-6)):
-            cur, now, pairs = e, q, None
+            cur, seq, now, pairs = e, q, res, None
             if e < top:
-                top, seq = e, q
-    return seq
+                top, best_seq = e, q
+    return best_seq
 
 
 _ORDER = {}

@@ -1,6 +1,6 @@
 import numpy as np
 from concourse.bass import DstId, RemoteDMATransfer
-from concourse.mybir import dt, AluOpType, ActivationFunctionType, AxisListType
+from concourse.mybir import dt, AluOpType, ActivationFunctionType
 
 C, K, R = 384, 192, 3
 F32, BF, F16, I32, U16, U8, X4 = "float32", "bfloat16", "float16", "int32", "uint16", "uint8", "float8_e4m3fn_x4"
@@ -9,8 +9,7 @@ FIB = [1, 2, 3, 5, 8, 13, 21, 34, 55, 89]
 ZS = [(0, 208), (0, 240), (0, 304), (32, C)]
 E = 1.0 / 512
 W = 200
-B = 208
-NB = 12 * 17
+B, NB = 208, 204
 
 SCRATCH = {}
 
@@ -22,7 +21,6 @@ def _decl(name, n, d, where="sbuf"):
 for _t in range(R + 1):
     _decl("X%d" % _t, 4 * C, BF)
     _decl("QX%d" % _t, C, X4)
-    _decl("SX%d" % _t, C, U8)
 for _h in range(2):
     for _n, _w, _d in [("MK", K, F32), ("HD", K, F32), ("NEQ", 2 * K, BF), ("CMP", 12 * W, BF),
                        ("JK", 12 * W, BF), ("RK", 12 * 96, BF), ("AL", 24, F32), ("SC", K, F32),
@@ -34,41 +32,58 @@ for _b in range(4):
     _decl("D%d" % _b, 512, F32, "psum")
 for _n, _w, _d in [
     ("H", R * 1024, BF), ("QH", R * 256, X4), ("SH", R * 256, U8), ("LC", R * K, X4), ("LS", R * 256, U8),
-    ("U", 512, BF), ("QU", 128, X4), ("SU", 128, U8), ("QR", 128, X4), ("SR", 128, U8),
-    ("WC", 512, X4), ("WS", 512, U8), ("ONES", 512, BF), ("EB", 2048, BF), ("QE", 512, X4), ("SE", 512, U8),
+    ("SX", (R + 1) * C, U8), ("U", 512, BF), ("QU", 128, X4), ("SU", 128, U8), ("QR", 128, X4), ("SR", 128, U8),
+    ("WC", 512, X4), ("WS", 512, U8),
+    ("ONES", 512, BF), ("EB", 2048, BF), ("QE", 512, X4), ("SE", 512, U8),
     ("PTR", 24, I32), ("PI", 16, I32), ("UL", 8, U16),
-    ("COL", 40, F32), ("IOTA", K, F32), ("J16", K + 16, BF), ("NGB", 12, F32), ("IOC", C + K, BF),
-    ("CMIN", 2 * K, BF), ("R16", 2 * K, BF), ("T1", 96, BF), ("A16", 24, U16),
-    ("HOLD", 2 * C + 2 * K + B, BF), ("IOS", C + K, BF), ("TAB", 24, F32),
-    ("SREV", K, F32), ("RS", B, BF), ("SM", 256, F32), ("PIV", 12, F32), ("G16", 16, F32),
-    ("J48", 48, F32), ("OL", 6, U16), ("PB", C, BF), ("FP", C + 2, BF), ("DF", C, BF), ("VV", C, BF), ("PN", K, BF),
-    ("L64", 64, U16), ("EL", 16, U16), ("H4", K, BF), ("L4", 48, U16),
+    ("COL", 24, F32), ("IOTA", K, F32), ("J16", K, BF), ("NGB", 12, F32),
+    ("CMIN", 2 * K, BF), ("R16", 2 * K, BF), ("T1", 48, BF), ("A16", 24, U16),
+    ("HOLD", C + K, BF), ("IOS", C + K, BF), ("TAB", 8, F32),
+    ("SREV", K, F32), ("RS", K + 16, BF), ("IOQ", K, BF), ("BK", 6 * B, BF), ("KF", 2 * B, F32), ("KT", 104, F32),
+    ("KI", 26, I32), ("TH", B, BF), ("KM", 28, U16), ("SM", 256, F32), ("PIV", 24, F32), ("IOX", 224, F32),
+    ("CM2", K + 96, BF), ("J48", 64, F32), ("OL", 6, U16),
+    ("PB", C, BF), ("FP", C + 2, BF), ("DF", C, BF), ("VV", C, BF), ("PN", K, BF), ("L64", 64, U16), ("EL", 16, U16),
     ("VH", 4 * K, BF), ("VH2", 4 * K, BF), ("TR", len(FIB) * C, BF), ("ZR", 2 * C, BF), ("AP", C, BF),
-    ("PR", C, BF), ("PP", C, BF), ("PE", K, BF), ("PEL", 12, U16), ("J1", 60, U16), ("JL", len(FIB) * 24, U16),
+    ("PR", C, BF), ("PP", K, BF), ("PE", K, BF), ("PEL", 12, U16), ("J1", 60, U16), ("JL", len(FIB) * 24, U16),
     ("DA", C, F16), ("HSA", 3 * C, F16), ("HSB", 6 * K, BF), ("PL", K, F32), ("YB", C, F32),
-    ("KF", 9 * B, F32), ("KL", 3 * 14, U16), ("M0", 3 * K, BF), ("JR", 3 * K, BF), ("MR", 6 * K, BF), ("TB", 224, BF),
-    ("TP", 416, BF), ("PS", 2 * B, F32), ("BK", 10 * B, BF),
+    ("KS", 48, F32), ("KL", 12, U16), ("M0", 3 * K, BF), ("JR", 3 * K, BF), ("MR", 6 * K, BF),
+    ("TB", 224, BF), ("TP", 432, BF), ("TG", K, BF), ("PS", K + 96, F32), ("NB", 3 * K, F16),
 ]:
     _decl(_n, _w, _d)
 
 NDMA = 24
 SEMAPHORES = ["cv", "cs", "cp", "cg", "sent"] + ["arr%d" % _t for _t in range(R)] + ["d%d" % _k for _k in range(NDMA)]
 
-NS = {(0, 0): (0, 4), (0, 1): (0, 5), (1, 0): (0, 5), (1, 1): (0, 5), (2, 0): (0, 5), (2, 1): (0, 5)}
-CP = {"relu": "svssvsvs", "dec": "ssvs", "jump": "ssssvvvvs", "vh": "ssss", "vh2": "ggvv", "twin": "sss"}
-LOW = 128
-PARTS = [(0, 128, 128), (128, K, 256)]
+NS = {(0, 0): (0, 5), (0, 1): (0, 5), (1, 0): (0, 5), (1, 1): (0, 5), (2, 0): (0, 5), (2, 1): (0, 5)}
+CP = {"relu": "svssvsvs", "dec": "svss", "last": "svsv", "jump": "sssvsvsvsvv", "vh": "svss", "vh2": "vsvv",
+      "twin": "svs", "z": "g", "f0": "svs", "low": 160}
 
-SETS = [(0.83, 200, 1.55, 3.8, 150, 1500, 600, 900), (0.83, 120, 1.55, 3.8, 150, 3500, 800, 900),
-        (1.2, 200, 1.9, 5.0, 260, 1800, 800, 1300), (1.0, 150, 1.2, 2.5, 180, 2200, 500, 1200),
-        (0.9, 250, 1.3, 4.5, 200, 1500, 400, 700)]
-WEIGHT = [2.0, 1.0, 1.0, 1.0, 1.0]
-T_DMA, ROUNDS, STEPS, HEAT = 2000.0, 6, 40000, 0.0003
+SETS = [(0.83, 250, 1.4, 3.4, 110, 800, 400, 27, 6, 0, 64, 10, 64, 1300),
+        (0.83, 200, 1.55, 3.8, 150, 1300, 600, 20, 6, 0, 64, 30, 64, 2000),
+        (1.2, 260, 1.8, 4.5, 200, 1000, 500, 18, 9, 0, 64, 30, 64, 1500),
+        (1.0, 300, 1.2, 2.5, 130, 1500, 500, 20, 8, 0, 64, 10, 64, 1300),
+        (1.1, 200, 1.5, 4.0, 200, 1000, 400, 20, 5, 20, 50, 50, 30, 1500)]
+ORDER = (
+    "06020N000M03010R1f080v0w0x0y07090A0E0J0z1g0Y0C0B0m0S0X1h0G0W130T0O0H1i0L0Z0P151I0a0U1k1j0I1K1J0t1L1F0Q101l1P1Q0K1n1m0V"
+    "1s1N1o0D1R0n2w1p1O1M04051S2A0u1u2B1y1q2m2p0r281T2C271Y2a2s2g2j2n2D2q1W1U252t311V3d1E2W2Q222E2k1Z2f212d2F240p23342b2P2h"
+    "2u2K2Y2N2o2r2l303a2c2i2S261X202e3718293e322M2v38392G2J1z2V3b332x0f2T2H2L3f1b2O2X3c2y36351d3h2z2I2U2R2Z3g111t0e1v0o193i"
+    "0q1B3j0i121G1a3k3p0h3q3l3o3t4j4k0g3s3w3x0l4o4h4l3z3y4m0j3A4p4n0k3B3E3D3C4i0c4s3r3F3I3H4q1c3G3u3m3J3M3L143K4r4t3N3Q1A3P"
+    "0d3O4u3n3R3U3T3v3S1w4A3V3Y3X4v1e3W4y4B0b3Z421741164440431H4548474a494I464b4w4d4e4c0F4z4x4g4f4E4G4K4F1C4C4H1r4L4J1D4M1x"
+    "4D4P5k4O4Q5l534N5m5t5n4R54565u554S4W0s4U4Y5o4T574X4V4Z5p5v5J585q505a5e5c5L5K5w515f595b5d5r6q5M525g5x6g5h5N6d626m5T646j"
+    "5i5s5O6e615y5Q5Z6n695j656k676a5z6f6l5Y6c5P5V6h666b5W5A6o5B6B6i5S6z5R636F5X5C68606D5U6p6C6A6G6r5F6E6s6t6x6H5G6v5D6w6I5H"
+    "6J6u6M6K6W6N6L5E6X6O5I6y6P6Y6Q7i7r6S7o6Z6R7c7u6T7d7x7k7f7p6U737q7g70746V767w797l717H7z777E7s7D7t7h7I7n7a7F7m7G7v7J7e7y"
+    "7j72857K7S7b78757A867T82847B7L7U7C7V887M8387897W7N7Q8a7X7R8b8d8c7O7Y8e7P7Z808f8g818h8i8k8j8s8o8m8q8t8l8p8n8u8r928v8M8y"
+    "938x8w949b958z8O8N9c8L8A8E968C8G8B8P8F978D8H9d9r988Q8I8U8W8S9t9s8V8J8R8X9e8T9ua8998K8Y9va19f9Y8Z9V9G9S9H909w9Z9a9y9g9M"
+    "a49R9J919T9Ka29h9Ua59E9x9X9Pa39i9ja09B9La69Daj9W9N9z9kal9A9Ian9Q9Faha79l9O9C9nama9akaoai9oaaabapaf9mac9paeaqadar9qasau"
+    "aEatavaFawagaSaxaXayaUb3aVaAb6aGazbfaJaBaIb9aHbcaCaPbgb0b2aDaOb4aLbdaYaMb5bpbmb8blaZbabqbhaNb7bnbobbbraRbeaQb1bsbAaWaK"
+    "aTbibKbBbNbMbjbtbCbObPbkbDbubQbVbLbRbEbvbybSbTbzbFbwbUbWbGbxbYbXbHbIbJc2bZc0c1cac6c4c8cbc3c7c5ccc9cdcgcfcecuctchcvcwcK"
+    "cmcicockcxcncjclcpd1cAcyd0cCcXcEcLcqcBcVcYcZcDczcFcrcGcWcscHd2cIcJcQcOcMcScRcPcNcTcUd3d5d8d6d9d7d4da"
+)
 
 
 def build(T, topo, core, par):
     A, F = AluOpType, ActivationFunctionType
-    CYC, _lat, GATH, SCAT, T_MM, T_REM, T_ISS, T_BYT = par
+    CYC, _wake, GATH, SCAT, T_MM, T_REM, T_ISS, RATE, T_ROW, FV, MV, FS, MS, T_DMA = par
     rank = T.rank_of(core)
     nxt = T.cores[(rank + 1) % len(T.cores)]
     prv = T.cores[(rank - 1) % len(T.cores)]
@@ -108,12 +123,8 @@ def build(T, topo, core, par):
 
     def add(eng, fn, rd, wr, dur, kind="c", lat=0.0, after=()):
         ops.append({"e": eng, "fn": fn, "rd": flat(rd), "wr": flat(wr), "dur": dur, "kind": kind, "lat": lat,
-                    "after": list(after), "k": len(ops), "soft": []})
+                    "after": list(after), "k": len(ops)})
         return len(ops) - 1
-
-    def chain(ks):
-        for x, y in zip(ks, ks[1:]):
-            ops[y]["soft"].append(x)
 
     def vdur(out, ins, base=1.0, fast=True):
         if out[0] == "ind":
@@ -121,7 +132,7 @@ def build(T, topo, core, par):
         if ins[0][0] == "ind":
             return 50 + GATH * CYC * cnt(out)
         h = 0.5 if fast and all(two(w) for w in [out] + ins) else base
-        return CYC * max(64, h * cnt(out))
+        return FV + CYC * max(MV, h * cnt(out))
 
     def copy(out, in_):
         if out[0] == "ind":
@@ -150,10 +161,6 @@ def build(T, topo, core, par):
         return add("v", lambda q: q.tensor_tensor_scan(ap(out), ap(d0), ap(d1), ap(init), op0, op1), [d0, d1, init],
                    [out], vdur(out, [d0, d1]))
 
-    def reduce(out, in_, op):
-        return add("v", lambda q: q.tensor_reduce(ap(out), ap(in_), AxisListType.X, op), [in_], [out],
-                   CYC * max(64, cnt(in_)))
-
     def act(out, in_, func, bias=None, scale=None, acc=None):
         kw = {}
         if bias is not None:
@@ -162,7 +169,7 @@ def build(T, topo, core, par):
             kw["scale"] = scale
         if acc is not None:
             kw["accum_out"] = ap(acc)
-        d = (65 + GATH * CYC * cnt(out) if in_[0] == "ind" else CYC * max(64, cnt(out)) + 30) + (25 if acc else 0)
+        d = (65 + GATH * CYC * cnt(out) if in_[0] == "ind" else CYC * max(MS, cnt(out)) + FS) + (25 if acc else 0)
         return add("s", lambda q: q.activation(ap(out), ap(in_), func, **kw), [in_, bias], [out, acc], d)
 
     def gather(out, win, off):
@@ -202,31 +209,44 @@ def build(T, topo, core, par):
     def u8(w):
         return ap(w).bitcast(dt.uint8)
 
+    rid, pid, _e = topo.addr(nxt)
+    mask = topo.mask(core, nxt)
+    eng = topo.engines(core, nxt)
+    sends = []
+    halves = [sum(1 << e for e in eng[:len(eng) // 2]), sum(1 << e for e in eng[len(eng) // 2:])]
+
+    def send(pairs, sem, width):
+        if len(pairs) == 1:
+            fn = lambda q: q.remote_dma(pairs[0][1], pairs[0][0], T.sem[sem], T.sem["sent"], pid, rid, mask)
+        else:
+            fn = lambda q: q.remote_dma_fused(
+                [RemoteDMATransfer(dst_ids=[DstId(rid=rid, pnc=pid)], dma_engine_mask=m, remote_sem=T.sem[sem],
+                                   src=p[0], dst=p[1]) for m, p in zip(halves, pairs)], local_sem=T.sem["sent"])
+        k = add("g", fn, [p[2] for p in pairs], [], T_ISS, "rem", after=[x[0] for x in sends[-1:]])
+        w = add("r", None, [], [], 16 * len(pairs) * (T_ROW + width / RATE), "arr", after=[k] + [x[1] for x in sends[-1:]])
+        sends.append((k, w))
+
     dma("s", ap(v("U")), T.u[:], [], [v("U")], 131072)
     dma("s", ap(v("PTR")), T.ptr[:], [], [v("PTR")], 12288)
-    xa = dma("y", ap(v("X0", 0, 4 * K)), T.x[:, 0:4 * K], [], [v("X0", 0, 4 * K)], 196608)
-    xb = dma("y", ap(v("X0", 4 * K)), T.x[:, 4 * K:4 * C], [], [v("X0", 4 * K)], 393216)
+    xa = dma("y", ap(v("X0", 0, 4 * K)), T.x[:, 0:4 * K], [], [v("X0", 0, 4 * K)], 262144)
+    xb = dma("y", ap(v("X0", 4 * K)), T.x[:, 4 * K:4 * C], [], [v("X0", 4 * K)], 458752)
     dma("y", u8(v("WC")), T.wc[:], [], [v("WC")], 262144, after=[xa, xb])
     dma("y", ap(v("WS")), T.ws[:], [], [v("WS")], 65536, after=[xa, xb])
 
-    pc, ai, qi, gi, i16 = col("PI", 0), col("PI", 1), col("PI", 2), col("PI", 3), v("PI", 8, 16)
-    j16, j4 = v("J16", 0, K), v("J16", K, K + 16)
-    ioc, negi = v("IOC", 0, C), v("IOC", C, C + K)
+    pc, ai, gi, i16 = col("PI", 0), col("PI", 1), col("PI", 3), v("PI", 8, 16)
+    j16 = v("J16")
     ios, iop = v("IOS", 0, C), v("IOS", C, C + K)
     cmin, cm0, r16, keep = v("CMIN", 0, K), v("CMIN", K, 2 * K), v("R16", 0, K), v("R16", K, 2 * K)
-    holda, holdc, holdd = v("HOLD", 0, C), v("HOLD", C, 2 * C), v("HOLD", 2 * C, 2 * C + K)
-    hold4, holde = v("HOLD", 2 * C + K, 2 * C + 2 * K), v("HOLD", 2 * C + 2 * K)
+    holdc, holdd = v("HOLD", 0, C), v("HOLD", C, C + K)
     iota(pc, [[0, 1]], 0, 1)
     iota(i16, [[16, 8]], 0)
     iota(j16, [[0, 12], [1, 16]], 0)
     iota(v("IOTA"), [[1, K]], 0)
-    iota(j4, [[0, 4], [1, 4]], 0)
-    iota(ioc, [[1, C]], -K)
-    iota(negi, [[-1, K]], -1)
     iota(v("NGB"), [[-16, 12]], -16)
-    t01, t16, tbig = v("TAB", 0, 2), v("TAB", 8, 10), v("TAB", 16, 18)
+    t01 = v("TAB", 0, 2)
     iota(t01, [[1, 2]], 0)
-    iota(t16, [[-16, 2]], 0)
+    iota(v("IOX"), [[1, 224]], 0)
+    iota(v("SM", 0, 16), [[0, 16]], 0)
     for h in range(2):
         iota(col("ALV%d" % h, 0), [[0, 1]], 0)
     for t in range(R):
@@ -234,28 +254,23 @@ def build(T, topo, core, par):
         iota(v("H", 1024 * t + 4 * K, 1024 * t + 1024), [[0, 256]], 0)
     iota(v("ONES"), [[0, 512]], 1)
     for b in range(4):
-        select(v("EB", 512 * b, 512 * b + 512), v("ONES"), [[-1, 512]], A.is_equal, 0.0, b, 4)
-    quant(v("QE"), v("SE"), v("EB"))
-    (a0, a1, q0, q1, fe, f4, f5, f6, f7, f8, ns1, nb16, thr0, thr, cf, cfk, gam,
-     piv2, ns2, cst, pnc, cf2, up0, n1, n2, n1h, fc, fd) = [col("COL", j) for j in range(28)]
+        eb = v("EB", 512 * b, 512 * b + 512)
+        select(eb, v("ONES"), [[-1, 512]], A.is_equal, 0.0, b, 4)
+        quant(v("QE", 128 * b, 128 * b + 128), v("SE", 128 * b, 128 * b + 128), eb)
+    (a0, a1, f7, ns1, nb16, thr0, thr, cf, cfk, gam,
+     piv2, ns2, cst, pnc, cf2, up0, n1, n2, n1h, fc, fd, ns0, cj) = [col("COL", j) for j in range(23)]
     ts(ai, pc, 15, A.bitwise_and)
-    ts(qi, ai, 2, A.arith_shift_right)
     ts(gi, pc, 4, A.arith_shift_right, 1, A.bitwise_and)
     copy(a0, ai)
-    copy(q0, qi)
     copy(gam, gi)
     ts(a1, a0, 1.0, A.add)
-    ts(q1, q0, 1.0, A.add)
     ts(f7, a0, 15.0, A.is_lt, float(C), A.mult)
     ts(fc, f7, float(K), A.add, E, A.mult)
     ts(fd, f7, 0.5 * E, A.mult, -E, A.add)
-    ts(fe, f7, 2.0, A.mult)
-    ts(f5, q0, 3.0, A.is_lt, K * E, A.mult)
-    ts(f6, a0, 0.25, A.mult, q0, A.subtract)
-    ts(f8, f6, -1.0, A.add, E, A.mult)
-    ts(f4, f8, f5, A.add)
-    ts(ns1, a0, -16.0, A.mult, -15.0, A.add)
-    ts(nb16, a0, -0.0625, A.mult)
+    ts(ns1, a0, 4096.0, A.mult, 4096.0, A.add)
+    ts(ns0, a0, -4096.0, A.mult, 256.0, A.add)
+    ts(cj, a0, 16.0, A.mult, 31.0, A.add)
+    ts(nb16, a0, -0.0625, A.mult, 31.0 / 16, A.add)
     ts(thr0, a0, 16.0, A.mult, 15.5, A.add)
     ts(thr, thr0, K - 0.5, A.min)
     ts(cf, a0, -1.0, A.mult, 2071.5, A.add)
@@ -263,60 +278,69 @@ def build(T, topo, core, par):
     copy(col("FP", 0), cf)
     for h in range(2):
         fill(col("DB%d" % h, 0), -E)
-    act(ios, ioc, F.Copy, scale=E)
-    act(iop, negi, F.Copy, scale=-E)
-    act(v("PP", K, C), negi, F.Copy, scale=-E)
-    ts(tbig, t01, 0.5, A.subtract, 2.0 ** 97, A.mult)
-    fill(v("SM", K, 256), 2.0 ** 96)
+    act(sub(ios, 0, K), v("IOTA"), F.Copy, scale=E, bias=-K * E)
+    act(sub(ios, K, C), v("IOTA"), F.Copy, scale=E)
+    act(iop, v("IOTA"), F.Copy, scale=E, bias=E)
+    fill(v("SM", K + 16, 256), 2.0 ** 96)
     copy(v("UL"), i16)
     ts(cm0, j16, a0, A.is_equal, 0.5, A.subtract)
     ts(cmin, cm0, 2.0 ** 97, A.mult)
     ts(r16, j16, 0.5, A.subtract, 2.0 ** 97, A.mult)
     ts(keep, j16, 1.0, A.min)
     ts(v("A16"), v("J16", 0, 24), 0.0, A.mult, a0, A.add)
-    ts(v("T1", 0, 16), v("J16", 0, 16), a0, A.is_equal, 1024.0, A.mult)
-    ts(v("T1", 16, 32), v("J16", 0, 16), a1, A.is_equal, -float(C), A.mult)
+    ts(v("T1", 0, 16), v("J16", 0, 16), a0, A.is_equal, 1024.0 * E, A.mult)
+    ts(v("T1", 16, 32), v("J16", 0, 16), a1, A.is_equal, -C * E, A.mult)
     tt(v("T1", 32, 48), v("T1", 0, 16), v("T1", 16, 32), A.add)
-    gather(holda, v("T1", 32, 48), v("A16"))
-    act(holdc, holda, F.Copy, scale=E)
-    act(holdd, sub(holda, 0, K), F.Copy, scale=0.5 * E)
-    act(holde, sub(holda, 0, B), F.Copy, scale=2.0)
-    ts(v("T1", 48, 64), j4, q0, A.is_equal, 1.0, A.mult)
-    ts(v("T1", 64, 80), j4, q1, A.is_equal, -K * E, A.mult)
-    tt(v("T1", 80, 96), v("T1", 48, 64), v("T1", 64, 80), A.add)
-    gather(hold4, v("T1", 80, 96), v("A16", 0, 12))
+    gather(holdc, v("T1", 32, 48), v("A16"))
+    act(holdd, sub(holdc, 0, K), F.Copy, scale=0.5)
     dma("y", T.pl[:, K:C], T["IOTA"][0:128:16, 0:K], [v("IOTA")], [], 6144)
-    kf = [v("KF", B * j, B * j + B) for j in range(9)]
-    bk = [v("BK", B * j, B * j + B) for j in range(10)]
-    st1, st2, reset = kf[6], kf[7], bk[0]
-    in17 = [[0, 12], [1, 17]]
-    iota(v("KF", 0, 3 * B), [[0, 3 * B]], 0)
-    for j in (3, 5, 8):
-        iota(sub(kf[j], NB, B), [[0, B - NB]], 0)
-    iota(reset, [[0, B]], 0)
+    odd, kb, mk1, kc = v("KS", 0, 12), v("KS", 12, 24), v("KS", 24, 36), v("KS", 36, 48)
     iota(v("TB"), [[0, 224]], 0)
-    iota(v("RS", K, K + 2), [[-257, 2]], 256)
-    iota(sub(kf[3], 0, NB), [[16, 12], [1, 17]], 0)
-    iota(sub(kf[4], 0, NB), [[16, 12], [1, 17]], -1)
-    iota(sub(kf[5], 0, NB), [[0, 6], [1, 2], [0, 17]], 0)
-    iota(sub(kf[8], 0, NB), [[1008, 12], [-1, 17]], 1023)
-    iota(sub(st2, 0, 12), [[2, 12]], 2)
-    select(sub(kf[8], 0, NB), sub(kf[8], 0, NB), in17, A.not_equal, 100.0 / E, -16)
-    select(sub(reset, 0, NB), sub(reset, 0, NB), in17, A.not_equal, -100.0, 0)
-    select(sub(kf[0], 0, NB), sub(kf[3], 0, NB), in17, A.not_equal, float(K), -16)
-    select(sub(kf[1], 0, NB), sub(kf[4], 0, NB), in17, A.not_equal, float(K + 1), 0)
-    act(st1, kf[8], F.Copy, scale=E)
-    ts(kf[5], kf[5], gam, A.not_equal, float(B), A.mult)
-    tt(kf[2], kf[5], kf[3], A.add)
-    kl = [v("KL", 14 * j, 14 * j + 13) for j in range(3)]
-    for j in range(3):
-        scan(kf[3 + j], holde, kf[j], 0.0, A.add, A.min)
-        ts(kl[j], sub(kf[3 + j], 15, B, 16), fe, A.add)
+    act(v("IOQ"), v("IOTA"), F.Copy, scale=1.0 / 256)
+    iota(v("RS", K, K + 16), [[0, 16]], 1)
+    iota(v("TP", 416, 432), [[2, 16]], 4)
+    bk = [v("BK", B * j, B * j + B) for j in range(6)]
+    kf = [v("KF", B * j, B * j + B) for j in range(2)]
+    iota(kf[0], [[16, 13], [1, 16]], 0)
+    iota(sub(kf[0], 0, NB), [[16, 12], [1, 17]], 0)
+    act(bk[2], kf[0], F.Copy, scale=E)
+    iota(bk[0], [[0, B]], 29)
+    iota(sub(bk[0], 0, NB), [[2, 12], [0, 17]], 5)
+    iota(bk[1], [[0, B]], 1)
+    iota(sub(bk[1], 0, NB, 17), [[0, 12]], -1)
+    ii, bf, b17, z17, base, u0, p2, u1 = [v("KT", 13 * j, 13 * j + 13) for j in range(8)]
+    bi, pi_ = v("KI", 0, 13), v("KI", 13, 26)
+    km = [v("KM", 14 * j, 14 * j + 13) for j in range(2)]
+    iota(ii, [[16, 13]], 0)
+    ts(ii, ii, a0, A.add)
+    ts(bf, ii, 1.0 / 17, A.mult, -0.47, A.add)
+    copy(bi, bf)
+    copy(bf, bi)
+    ts(pi_, bi, 1, A.bitwise_and)
+    copy(p2, pi_)
+    tt(base, ii, bf, A.subtract)
+    ts(b17, bf, 17.0, A.mult)
+    tt(z17, b17, ii, A.is_equal)
+    ts(b17, z17, K + 1.0, A.mult)
+    tt(u0, base, b17, A.max)
+    ts(km[0], u0, -1.0, A.add)
+    ts(p2, p2, gam, A.not_equal, float(K + 16), A.mult)
+    tt(u1, base, p2, A.add)
+    ts(z17, z17, 417.0, A.mult)
+    tt(z17, z17, bf, A.add)
+    tt(u1, u1, z17, A.max)
+    ts(km[1], u1, -1.0, A.add)
+    iota(odd, [[0, 6], [1, 2]], 0)
+    iota(kb, [[16, 12]], 0)
+    iota(mk1, [[2, 12]], 4)
+    ts(odd, odd, gam, A.not_equal, float(K + 16), A.mult)
+    tt(kc, odd, kb, A.add)
+    ts(v("KL"), kc, a0, A.add)
     m0, m1, mb = [v("M0", K * j, K * j + K) for j in range(3)]
-    iota(mb, [[2, 12], [0, 16]], 2)
-    act(m1, cm0, F.Relu, scale=64.0)
+    iota(mb, [[2, 12], [0, 16]], 4)
+    act(m1, cm0, F.Copy, scale=31.0, bias=16.5)
     tt(m0, m1, mb, A.min)
-    act(m1, m0, F.Copy)
+    twin("g", m1, m0)
 
     quant(v("QU"), v("SU"), v("U"))
     add("v", lambda q: q.tensor_copy(ap(v("QR")).bitcast(dt.uint32), ap(v("QU")).bitcast(dt.uint32).indirect(ap(v("UL")))),
@@ -324,7 +348,8 @@ def build(T, topo, core, par):
     gather(v("SR"), v("SU"), v("UL"))
 
     def half(t, h):
-        return v("QX%d" % t, K * h, K * h + K), v("SX%d" % t, K * h, K * h + K), v("X%d" % t, 4 * K * h, 4 * K * h + 4 * K)
+        return (v("QX%d" % t, K * h, K * h + K), v("SX", C * t + K * h, C * t + K * h + K),
+                v("X%d" % t, 4 * K * h, 4 * K * h + 4 * K))
 
     def scores(t, h):
         qc, qs, _x = half(t, h)
@@ -340,31 +365,19 @@ def build(T, topo, core, par):
         tt(neq, pv, v("HD" + s), A.not_equal)
         scan(nqs, keep, neq, 0.0, A.mult, A.add)
         b0, b1 = NS[(t, h)]
-        cv, cs = [], []
-        mine = list(range(b0)) + list(range(b1, 12))
-        for j in range(len(mine) + 1):
-            if j < len(mine):
-                b = mine[j]
-                w, n, o = col("HD" + s, 16 * b + 15), 16 * b + 16, W * b
-                cv.append(ts(v("CMP" + s, o, o + n), v("PV" + s, 0, n), w, A.is_ge))
-                if n < K:
-                    cv.append(ts(v("CMP" + s, o + n, o + K), v("PV" + s, n, K), w, A.is_gt))
-            if j > 0:
-                b = mine[j - 1]
-                o = W * b
-                cv.append(scan(v("RK" + s, 96 * b, 96 * b + 96), v("CMP" + s, o, o + 96), v("CMP" + s, o + 96, o + K),
-                               sub(nqs, 16 * b + 15, 16 * b + 16), A.add, A.add))
+        for b in list(range(b0)) + list(range(b1, 12)):
+            w, n, o = col("HD" + s, 16 * b + 15), 16 * b + 16, W * b
+            ts(v("CMP" + s, o, o + n), v("PV" + s, 0, n), w, A.is_ge)
+            if n < K:
+                ts(v("CMP" + s, o + n, o + K), v("PV" + s, n, K), w, A.is_gt)
+            scan(v("RK" + s, 96 * b, 96 * b + 96), v("CMP" + s, o, o + 96), v("CMP" + s, o + 96, o + K),
+                 sub(nqs, 16 * b + 15, 16 * b + 16), A.add, A.add)
         tt(v("CMP" + s, K + W * b0, W * b1, W), v("NGB", b0, b1), sub(nqs, 16 * b0 + 15, 16 * b1, 16), A.subtract)
-        for b in range(b0, b1 + 1):
-            if b < b1:
-                cs.append(act(v("CMP" + s, W * b, W * b + K), ps, F.Sign, bias=col("HD" + s, 16 * b + 15), scale=-1.0))
-            if b > b0:
-                n, o = 16 * b, W * b - W
-                cs.append(act(v("JK" + s, o, o + n), v("CMP" + s, o, o + n), F.Relu, acc=col("AL" + s, b - 1)))
-                cs.append(act(v("JK" + s, o + n, o + K + 1), v("CMP" + s, o + n, o + K + 1), F.Relu, scale=-1.0,
-                              acc=col("AL" + s, 11 + b)))
-        chain(cv)
-        chain(cs)
+        for b in range(b0, b1):
+            n, o = 16 * b + 16, W * b
+            act(v("CMP" + s, o, o + K), ps, F.Sign, bias=col("HD" + s, 16 * b + 15), scale=-1.0)
+            act(v("JK" + s, o, o + n), v("CMP" + s, o, o + n), F.Relu, acc=col("AL" + s, b))
+            act(v("JK" + s, o + n, o + K + 1), v("CMP" + s, o + n, o + K + 1), F.Relu, scale=-1.0, acc=col("AL" + s, 12 + b))
         tt(v("RK" + s, 96 * b0 + 95, 96 * b1, 96), v("AL" + s, 12 + b0, 12 + b1), v("AL" + s, b0, b1), A.subtract)
         rk, off = v("RK" + s, 95, 12 * 96, 96), v("OFF" + s)
         if h == 0 or t == 0:
@@ -372,29 +385,31 @@ def build(T, topo, core, par):
         if h == 0:
             ts(off, rk, -1.0, A.mult, float(K - 1 + 16), A.add)
             copy(ind(v("SREV"), off), v("SC0"))
-            gather(v("RS", 0, K), v("IOTA"), off)
+            gather(v("RS", 0, K), v("IOQ" if t else "IOTA"), off)
             if t > 0:
-                scan(v("PIV"), sub(cmin, 0, 12), v("SREV", 15, K, 16), 0.0, A.max, A.min)
-                scan(v("SM", 0, K), cmin, v("SREV"), 0.0, A.max, A.min)
-                gather(bk[1], v("RS", 0, K + 2), kl[0])
-                gather(bk[2], v("RS", 0, K + 2), kl[1])
+                for j in range(2):
+                    scan(v("PIV", 12 * j, 12 * j + 12), sub(cmin, j, j + 12), v("SREV", 15, K, 16), 0.0, A.max, A.min)
+                scan(v("SM", 16, K + 16), cmin, v("SREV"), 0.0, A.max, A.min)
+                act(kf[1], ind(v("RS"), km[0]), F.Copy, bias=1.0)
+                scan(bk[4], kf[1], bk[3], 0.0, A.max, A.subtract)
         else:
             ts(off, rk, -16.0, A.add)
 
     def search():
         pv = v("PV1", 0, K)
-        for lv, (pivot, start) in enumerate(((col("PIV", 11), ns1), (piv2, ns2))):
-            cm, ol = "CM%d" % lv, col("OL", 2 * lv)
-            ts(v(cm, 0, K), pv, pivot, A.is_gt)
+        for cm, pivot, w, start in (("CM0", col("PIV", 11), -256.0, ns1), ("CM2", col("PIV", 23), 256.0, ns0)):
+            ts(v(cm, 0, K), pv, pivot, A.is_gt, w, A.mult)
             scan(v(cm, K, K + 96), v(cm, 0, 96), v(cm, 96, K), start, A.add, A.add)
-            ts(ol, col(cm, K + 95), 1.0, A.min)
-            if lv == 0:
-                tt(v("G16"), ind(tbig, ol), v("SM", 15, 256, 16), A.max)
-                reduce(piv2, v("G16"), A.min)
-                act(v("J48", 0, 16), ind(t16, ol), F.Identity, bias=nb16, acc=ns2)
-                act(v("J48", 16, 32), ind(t01, ol), F.Identity, acc=cst)
-            else:
-                act(v("J48", 32, 48), ind(t01, ol), F.Identity, bias=cst, acc=pnc)
+        ol = col("OL", 0)
+        ts(ol, cj, col("CM0", K + 95), A.min, col("CM2", K + 95), A.min)
+        act(v("J48", 0, 16), ind(v("SM"), ol), F.Identity, acc=piv2)
+        act(v("J48", 16, 32), ind(v("IOX"), ol), F.Identity, scale=-1.0, bias=nb16, acc=ns2)
+        act(v("J48", 48, 64), ind(v("IOX"), ol), F.Identity, scale=1.0 / 4096, bias=-31.0 / 65536, acc=cst)
+        ts(v("CM1", 0, K), pv, piv2, A.is_gt)
+        scan(v("CM1", K, K + 96), v("CM1", 0, 96), v("CM1", 96, K), ns2, A.add, A.add)
+        ol = col("OL", 2)
+        ts(ol, col("CM1", K + 95), 1.0, A.min)
+        act(v("J48", 32, 48), ind(t01, ol), F.Identity, scale=1.0 / 256, bias=cst, acc=pnc)
 
     turn = [0]
 
@@ -407,12 +422,13 @@ def build(T, topo, core, par):
 
     def climb():
         def both(out, win, k, c0, c1):
-            for e, a, b in (("v", c0, LOW), ("s", LOW, c1)):
+            for e, a, b in (("v", c0, CP["low"]), ("s", CP["low"], c1)):
                 take(e, sub(out, a, b), sub(win, 0, b), v("JL", 24 * k + a // 16, 24 * k + b // 16))
 
         tr = [v("TR", C * k, C * k + C) for k in range(len(FIB))]
         z = [v("ZR", 0, C), v("ZR", C, 2 * C)]
-        tt(tr[0], ind(ios, v("J1", 0, 24)), v("AP"), A.max)
+        for a in (K, 0):
+            tt(sub(tr[0], a, a + K), ind(ios, v("J1", a // 16, a // 16 + 12)), v("AP", a, a + K), A.max)
         tt(tr[1], ind(tr[0], v("J1", 0, 24)), v("AP"), A.max)
         n = len(FIB)
         for k in range(n + 2):
@@ -428,7 +444,6 @@ def build(T, topo, core, par):
     def blocks(p1):
         j = {d: v("J1", 12 * i, 12 * i + 12) for i, d in enumerate((1, 2, 4, 8))}
         p = {1: p1, 2: v("JR", 0, K), 4: v("JR", K, 2 * K), 8: v("JR", 2 * K, 3 * K)}
-        to_list(1, j[1], p1)
         for d in (2, 4, 8):
             gather(p[d], p[d // 2], j[d // 2])
             to_list(1, j[d], p[d])
@@ -441,34 +456,34 @@ def build(T, topo, core, par):
                 twin(CP["twin"][i], m[d][1], m[d][0])
         turn32(v("TP", 0, K), m[16][0])
         turn32(v("TP", K, 416), v("TB"))
-        gather(bk[4], v("PP"), kl[0])
-        gather(bk[5], v("TP"), kl[2])
-        tt(v("PS", 0, B), ind(v("TP"), kl[2]), bk[4], A.subtract)
-        scan(v("PS", B, B + NB), sub(reset, 0, NB), v("PS", 0, NB), -4.0, A.add, A.max)
-        scan(sub(bk[3], 0, NB), sub(bk[5], 0, NB), sub(st1, 0, NB), 0.0, A.max, A.subtract)
-        tt(sub(bk[3], 16, NB, 17), sub(st2, 0, 12), v("PS", B + 15, B + NB, 17), A.subtract)
+        gather(v("TG"), v("TP", 0, 416), v("KL"))
+        gather(v("TH"), v("TP"), km[1])
+        scan(bk[3], bk[0], v("TH"), 0.0, A.max, A.subtract)
+        scan(v("PS", 0, K), p1, v("TG"), 0.0, A.max, A.subtract)
+        scan(v("PS", K, K + 96), v("PS", 0, K, 2), v("PS", 1, K, 2), 0.0, A.min, A.min)
+        tt(sub(bk[2], 0, NB, 17), v("PS", K + 7, K + 96, 8), mk1, A.add)
+        scan(bk[5], bk[1], bk[2], 0.0, A.min, A.max)
 
     def jump(pn):
-        n0, n1_, dl, near = [sub(bk[j], 0, NB) for j in (6, 7, 8, 9)]
-        ts(n0, sub(bk[2], 0, NB), pn, A.is_ge, 2.0, A.add)
-        ts(n1_, sub(bk[1], 0, NB), pn, A.is_ge, 2.0, A.add)
-        scan(dl, n0, n1_, 0.0, A.max, A.subtract)
-        scan(near, dl, sub(bk[3], 0, NB), -4.0, A.add, A.max)
-        l = {d: v("JL", 12 * i, 12 * i + 12) for i, d in enumerate((1, 2, 3, 5))}
-        r = {1: v("TR", 0, K), 2: v("TR", K, 2 * K), 3: v("TR", 0, K), 5: v("TR", 2 * K, 3 * K)}
-        z = [v("ZR", 0, K), v("ZR", C, C + K)]
+        ts(v("NB", 0, B), bk[4], pn, A.is_ge)
+        scan(v("NB", B, 2 * B), v("NB", 0, B), bk[5], 0.0, A.add, A.min)
+        l = {d: v("JL", 12 * i, 12 * i + 12) for i, d in enumerate((1, 3))}
+        r = {d: v("TR", K * d, K * d + K) for d in (1, 2, 3)}
+        z = [v("ZR", K, C), v("ZR", C, C + K)]
         e = CP["jump"]
-        ts(l[1], sub(near, 16, NB, 17), 1.0 / E, A.mult, -1.0, A.add)
+        ts(l[1], v("NB", B + 16, B + NB, 17), 1.0 / E, A.mult, -1.0, A.add)
         take(e[0], r[1], iop, l[1])
         take(e[1], r[2], r[1], l[1])
-        to_list(1, l[2], r[2])
-        take(e[2], sub(r[3], 0, 160), r[2], sub(l[1], 0, 10))
-        to_list(1, sub(l[3], 2, 7), sub(r[3], 32, 112))
-        take(e[3], sub(r[5], 64, K), r[3], sub(l[2], 4, 12))
-        to_list(1, sub(l[5], 4, 12), sub(r[5], 64, K))
-        for i, (d, c0, c1) in enumerate(((1, 0, 1), (1, 0, 2), (2, 0, 4), (3, 2, 7), (5, 4, 12))):
-            take(e[4 + i], sub(z[1 - i % 2], 16 * c0, 16 * c1), z[i % 2], sub(l[d], c0, c1))
-        return z[1]
+        take(e[2], r[3], r[2], l[1])
+        take(CP["f0"][2], v("TR", 0, 64), r[3], v("J1", 8, 12))
+        to_list(1, v("JL", 24, 28), v("TR", 0, 64))
+        to_list(1, sub(l[3], 4, 12), sub(r[3], 64, K))
+        for i, (d, c0, c1) in enumerate(((1, 0, 1), (1, 0, 2), (1, 0, 3), (1, 2, 4), (1, 2, 5), (1, 4, 6),
+                                         (3, 4, 9), (3, 6, 12))):
+            take(e[3 + i], sub(z[1 - i % 2], 16 * c0, 16 * c1), z[i % 2], sub(l[d], c0, c1))
+        take(CP["f0"][0], v("ZR", 0, 128), z[1], v("J1", 0, 8))
+        take(CP["f0"][1], v("ZR", 128, K), z[1], v("JL", 24, 28))
+        return v("ZR", 0, C)
 
     quant(*half(0, 0))
     quant(*half(0, 1))
@@ -476,10 +491,6 @@ def build(T, topo, core, par):
     gather(v("PR"), ios, v("J1", 0, 24))
     scores(0, 0)
     ranks(0, 0)
-    rid, pid, _e = topo.addr(nxt)
-    mask = topo.mask(core, nxt)
-    eng = topo.engines(core, nxt)
-    halves = [sum(1 << e for e in eng[:len(eng) // 2]), sum(1 << e for e in eng[len(eng) // 2:])]
     for t in range(R):
         X, Xn = "X%d" % t, "X%d" % (t + 1)
         scores(t, 1)
@@ -493,12 +504,12 @@ def build(T, topo, core, par):
             search()
             ranks(t, 1)
             pn = pnc
-            ts(al[1], ind(v("IOTA"), v("OFF1")), pn, A.is_lt)
+            ts(al[1], ind(v("IOQ"), v("OFF1")), pn, A.is_lt)
         rs = v("RS", 0, K)
         ts(al[0], rs, pn, A.is_ge)
         ts(v("DA", 0, K), rs, pn, A.is_ge, 1.0 - E, A.mult)
-        for k in range(2):
-            scan(v("ZR", C * k, C * k + K), v("ALV0", 0, K), v("DA", 0, K), 1.0, A.add, A.subtract)
+        zo = K if t else 0
+        scan(v("ZR", zo, zo + K), v("ALV0", 0, K), v("DA", 0, K), 1.0, A.add, A.subtract)
         if t == 0:
             ts(v("DB0", 1, K + 1), rs, pn, A.is_ge, E, A.subtract)
             ts(v("DB1", 1, K + 1), al[1], E, A.subtract)
@@ -506,67 +517,65 @@ def build(T, topo, core, par):
             ts(up0, pn, -E, A.mult, K * E + 1.0, A.add)
             scan(v("AP", 0, K), al[0], v("DB0", 0, K), -1.0 - (K + 1) * E, A.add, A.subtract)
             scan(v("AP", K, C), al[1], v("DB1", 0, K), -1.0 - E, A.add, A.subtract)
-            for k in range(2):
-                scan(v("ZR", C * k + K, C * k + C), v("ALV1", 0, K), v("DA", K, C), up0, A.add, A.subtract)
+            scan(v("ZR", K, C), v("ALV1", 0, K), v("DA", K, C), up0, A.add, A.subtract)
+            twin(CP["z"], v("ZR", C, 2 * C), v("ZR", 0, C))
             found = climb()
         else:
+            scan(v("ZR", C, C + K), v("ALV0", 0, K), v("DA", 0, K), 1.0, A.add, A.subtract)
             found = jump(pn)
         scan(v("PB", 0, K), al[0], al[0], 0.0, A.add, A.max)
         scan(v("PB", K, C), al[1], al[1], col("PB", K - 1), A.add, A.max)
-        ts(cf2, pn, -1.0, A.mult, cfk, A.add)
+        ts(cf2, pn, -256.0 if t else -1.0, A.mult, cfk, A.add)
         for h in range(2):
             fp = v("FP", K * h + 1, K * h + K + 1)
             scan(fp, al[h], al[h], (cf, cf2)[h], A.add, A.max)
             scan(v("DF", K * h, K * h + K), fp, v("FP", K * h, K * h + K), 0.0, A.max, A.subtract)
             act(v("JK%d" % h, 0, K), v("PB", K * h, K * h + K), F.Sign, bias=thr, scale=-1.0, acc=(n1, n2)[h])
-        scan(v("VV"), v("DF"), ios, -K * E, A.add, A.min)
+            scan(v("VV", K * h, K * h + K), v("DF", K * h, K * h + K), sub(ios, K * h, K * h + K),
+                 (-K * E, col("VV", K - 1))[h], A.add, A.min)
         ts(n1h, n1, 0.5, A.mult, float(K), A.add)
         at = col("OL", 4)
         ts(at, n2, 0.5, A.mult, n1h, A.add)
         ts(v("EL"), ind(v("VV"), at), 1.0 / E, A.mult, float(K), A.add)
-        gather(v("PE"), v("PR") if t == 0 else v("PP"), v("EL", 0, 12))
-        to_list(t, v("PEL"), v("PE"))
-        cs = []
+        pel = v("EL", 0, 12)
+        if t == 0:
+            gather(v("PE"), v("PR"), pel)
+            to_list(t, v("PEL"), v("PE"))
+            pel = v("PEL")
+        ts(v("L64", 0, 16), ind(v("VV"), at), 4.0 / E, A.mult, float(4 * K), A.add)
+        for j in range(1, 4):
+            ts(v("L64", 16 * j, 16 * j + 12), v("EL", 0, 12), 4.0, A.mult, float(j), A.add)
         for j in range(4):
-            ts(v("L64", 16 * j, 16 * j + 16), ind(v("VV"), at), 4.0 / E, A.mult, float(4 * K + j), A.add)
-            src = ind(v(X), v("L64", 16 * j, 16 * j + 12))
+            src, o = ind(v(X), v("L64", 16 * j, 16 * j + 12)), v("VH", K * j, K * j + K)
             if CP["vh"][j] == "s":
-                cs.append(act(v("VH", j, 4 * K, 4), src, F.Copy, scale=0.5))
+                act(o, src, F.Copy, scale=0.5)
             else:
-                ts(v("VH", j, 4 * K, 4), src, 0.5, A.mult)
-            twin(CP["vh2"][j], v("VH2", j, 4 * K, 4), v("VH", j, 4 * K, 4))
-        chain(cs)
-        p1 = v("PP", 0, K)
-        tt(p1, ind(found, v("PEL")), iop, A.min)
-        scan(v("H4"), hold4, p1, 0.0, A.add, A.min)
-        ts(v("L4"), v("H4", 3, K, 4), f4, A.add, 4.0 / E, A.mult)
-        arr = T.sem["arr%d" % t]
-        for i, (c0, c1, c2) in enumerate(PARTS):
-            tt(v(Xn, 4 * c0, 4 * c1), ind(v("VH"), v("L4", c0 // 4, c1 // 4)), v("VH2", 4 * c0, 4 * c1), A.add)
-            qc, qs = v("QX%d" % (t + 1), c0, c2), v("SX%d" % (t + 1), c0, c2)
-            quant(qc, qs, v(Xn, 4 * c0, 4 * c2))
-            h0, g0, l0 = 1024 * t, 256 * t, K * t
+                ts(o, src, 0.5, A.mult)
+            twin(CP["vh2"][j], v("VH2", K * j, K * j + K), o)
+        p1 = v("PP")
+        tt(p1, ind(found, pel), iop, A.min)
+        to_list(1, v("J1", 0, 12), p1)
+        l0, g0, h0, arr = K * t, 256 * t, 1024 * t, "arr%d" % t
+        for i, (c0, c1) in enumerate(((0, 128), (128, K))):
+            for j in range(4):
+                tt(v(Xn, 4 * c0 + j, 4 * c1, 4), ind(v("VH", K * j, K * j + c1), v("J1", c0 // 16, c1 // 16)),
+                   v("VH2", K * j + c0, K * j + c1), A.add)
+            qc, qs = v("QX%d" % (t + 1), c0, c0 + 128), v("SX", C * (t + 1) + c0, C * (t + 1) + c0 + 128)
+            quant(qc, qs, v(Xn, 4 * c0, 4 * c0 + 512))
             for b in range(4):
                 bank = "D%d" % b if i == 0 else ("PV1", "PS1", "D0", "D1")[b]
                 mm(bank, v("WC", 128 * b, 128 * b + 128), v("WS", 128 * b, 128 * b + 128), qc, qs)
-                o = v("H", h0 + 4 * c0 + b, h0 + 4 * c1, 4)
+                o, src = v("H", h0 + 4 * c0 + b, h0 + 4 * c1, 4), v(bank, 0, c1 - c0)
                 if CP["relu"][4 * i + b] == "s":
-                    act(o, v(bank, 0, c1 - c0), F.Relu, scale=0.03125)
+                    act(o, src, F.Relu, scale=0.03125)
                 else:
-                    ts(o, v(bank, 0, c1 - c0), 0.0, A.max, 0.03125, A.mult)
-            quant(v("QH", g0 + c0, g0 + c2), v("SH", g0 + c0, g0 + c2), v("H", h0 + 4 * c0, h0 + 4 * c2))
-            qh, lc = v("QH", g0 + c0, g0 + c1), v("LC", l0 + c0, l0 + c1)
-            if i == 0:
-                s1 = add("g", lambda q, lc=lc, qh=qh, arr=arr:
-                         q.remote_dma(u8(lc), u8(qh), arr, T.sem["sent"], pid, rid, mask), [qh], [], T_ISS, "rem")
-            else:
-                sh, ls = v("SH", g0, g0 + 256), v("LS", g0, g0 + 256)
-                s2 = add("g", lambda q, lc=lc, qh=qh, ls=ls, sh=sh, arr=arr: q.remote_dma_fused(
-                    [RemoteDMATransfer(dst_ids=[DstId(rid=rid, pnc=pid)], dma_engine_mask=m, remote_sem=arr, src=a, dst=b)
-                     for m, a, b in ((halves[0], u8(qh), u8(lc)), (halves[1], ap(sh), ap(ls)))], local_sem=T.sem["sent"]),
-                    [qh, sh], [], T_ISS, "rem", after=[s1])
-        lc, ls = v("LC", K * t, K * t + K), v("LS", 256 * t, 256 * t + K)
-        add("r", ("arr%d" % t, 2 * len(topo.engines(prv, core))), [], [lc, ls], T_BYT * 0.55, "arr", T_REM, after=[s1, s2])
+                    ts(o, src, 0.0, A.max, 0.03125, A.mult)
+            quant(v("QH", g0 + c0, g0 + c0 + 128), v("SH", g0 + c0, g0 + c0 + 128), v("H", h0 + 4 * c0, h0 + 4 * c0 + 512))
+            qh, sh = v("QH", g0 + c0, g0 + c1), v("SH", g0, g0 + 256)
+            send([(u8(qh), u8(v("LC", l0 + c0, l0 + c1)), qh)] + ([(ap(sh), ap(v("LS", g0, g0 + 256)), sh)] if i else []),
+                 arr, 4 * (c1 - c0))
+        lc, ls = v("LC", l0, l0 + K), v("LS", g0, g0 + K)
+        add("a", (arr, 2 * len(topo.engines(prv, core))), [], [lc, ls], 0.0, "arr", T_REM, after=[sends[-1][1]])
         if t + 1 < R:
             blocks(p1)
             scores(t + 1, 0)
@@ -574,13 +583,14 @@ def build(T, topo, core, par):
         else:
             ts(v("PL"), p1, 1.0 / E, A.mult, -1.0, A.add)
             dma("y", T.pl[:, 0:K], T["PL"][0:128:16, 0:K], [v("PL")], [], 6144)
+        ed = CP["dec"] if t + 1 < R else CP["last"]
         for b in range(4):
             mm("D%d" % b, v("QE", 128 * b, 128 * b + 128), v("SE", 128 * b, 128 * b + 128), lc, ls)
-            o = v(Xn, 4 * K + b, 4 * C, 4)
-            if CP["dec"][b] == "s":
-                act(o, v("D%d" % b, 0, K), F.Copy)
+            o, src = v(Xn, 4 * K + b, 4 * C, 4), v("D%d" % b, 0, K)
+            if ed[b] == "s":
+                act(o, src, F.Copy)
             else:
-                copy(o, v("D%d" % b, 0, K))
+                copy(o, src)
         quant(*half(t + 1, 1))
 
     for h in range(2):
@@ -591,9 +601,9 @@ def build(T, topo, core, par):
         dma("y", T.oc[:, 4 * K * h:4 * K * h + 4 * K], u8(qc), [qc], [], 98304)
         for k in range(4):
             dma("y" if (h == 0 or k < 2) else "s", T.osc[4 * k:4 * k + 4, K * h:K * h + K],
-                T["SX%d" % R][32 * k:32 * k + 4, K * h:K * h + K], [qs], [], 768)
+                T["SX"][32 * k:32 * k + 4, C * R + K * h:C * R + K * h + K], [qs], [], 768)
         dma("y" if h == 0 else "s", T.y[:, K * h:K * h + K], ap(yb), [yb], [], 98304)
-    return ops, 2 * R * len(eng)
+    return ops, len(eng) * len(sends)
 
 
 def depend(ops):
@@ -619,181 +629,23 @@ def depend(ops):
         o["near"] = near
 
 
-def by_key(key, pre, seq):
-    k2 = list(key)
+def issue_order(ops):
+    ch = "0123456789abcdefghijklmnopqrstuvwxyzABCDEFGHIJKLMNOPQRSTUVWXYZ"
+    seq = [ch.index(ORDER[i]) * 62 + ch.index(ORDER[i + 1]) for i in range(0, len(ORDER), 2)]
+    done = set()
     for k in seq:
-        for d, _w in pre[k]:
-            if k2[k] <= k2[d]:
-                k2[k] = k2[d] + 1e-3
-    return [int(k) for k in np.argsort(k2, kind="stable")]
-
-
-def lay(ops, idx, pre, back):
-    st, en, busy = [0.0] * len(ops), [0.0] * len(ops), {}
-    for k in idx:
-        o = ops[k]
-        t0 = max([en[d] + w for d, w in pre[k]] + [0.0]) + (o["lat"] if back else 0.0)
-        iv = busy.setdefault(o["e"], [])
-        pos = len(iv)
-        for j, (s, e) in enumerate(iv):
-            if t0 + o["dur"] <= s:
-                pos = j
-                break
-            t0 = max(t0, e)
-        iv.insert(pos, (t0, t0 + o["dur"]))
-        st[k], en[k] = t0, t0 + o["dur"] + (0.0 if back else o["lat"])
-    return st, en
-
-
-def span(seq, near, eng, cost):
-    dur, lat, w = cost
-    en, free = [0.0] * len(dur), {}
-    for k in seq:
-        t = free.get(eng[k], 0.0)
-        for j in near[k]:
-            if en[j] + w > t:
-                t = en[j] + w
-        free[eng[k]] = t + dur[k]
-        en[k] = t + dur[k] + lat[k]
-    return max(en)
-
-
-def tight(seq, near, eng, cost):
-    dur, lat, w = cost
-    en, free, why, last = [0.0] * len(dur), {}, [None] * len(dur), {}
-    for k in seq:
-        e = eng[k]
-        t, y = free.get(e, 0.0), (last.get(e), True)
-        for j in near[k]:
-            if en[j] + w > t:
-                t, y = en[j] + w, (j, False)
-        free[e], en[k], why[k], last[e] = t + dur[k], t + dur[k] + lat[k], y, k
-    k, pairs = en.index(max(en)), []
-    while k is not None:
-        j, same = why[k]
-        if same and j is not None and j not in near[k]:
-            pairs.append((j, k))
-        k = j
-    return pairs
-
-
-def order(ops, costs):
-    n = len(ops)
-    lat = costs[0][2]
-    pre = [[(d, lat) for d in o["near"]] + [(d, 0.0) for d in o["soft"]] for o in ops]
-    suc = [[] for o in ops]
-    up = [0.0] * n
-    for o in reversed(ops):
-        up[o["k"]] += o["dur"] + o["lat"]
-        for d, w in pre[o["k"]]:
-            up[d] = max(up[d], up[o["k"]] + w)
-            suc[d].append((o["k"], w))
-    fwd, bwd = list(range(n)), list(range(n - 1, -1, -1))
-    st, en = lay(ops, by_key([-u for u in up], pre, fwd), pre, False)
-    best = (max(en), st)
-    rng = np.random.default_rng(0)
-    for it in range(ROUNDS):
-        nz = rng.normal(0.0, 200.0 if it % 2 else 1e-6, n)
-        _s, eb = lay(ops, by_key([-en[k] + nz[k] for k in range(n)], suc, bwd), suc, True)
-        st, en = lay(ops, by_key([-eb[k] for k in range(n)], pre, fwd), pre, False)
-        if max(en) < best[0]:
-            best = (max(en), st)
-    near, eng = [o["near"] for o in ops], [o["e"] for o in ops]
-    hard = [[(d, 0.0) for d in o["near"]] for o in ops]
-    seq = by_key(best[1], hard, fwd)
-    names = sorted(set(eng))
-    queue = [names.index(e) for e in eng]
-    after = [[] for o in ops]
-    for o in ops:
-        for d in o["near"]:
-            after[d].append(o["k"])
-    gap = 24
-
-    def run(q, i0, old):
-        res = []
-        for c, (dur, lat, w) in enumerate(costs):
-            j0 = i0 // gap
-            if old is None:
-                en, free, snap = [0.0] * n, [0.0] * len(names), []
-            else:
-                en, snap = list(old[c][0]), old[c][1][:j0]
-                free = list(old[c][1][j0])
-            for i in range(j0 * gap, n):
-                if i % gap == 0:
-                    snap.append(list(free))
-                k = q[i]
-                e = queue[k]
-                t = free[e] - w
-                for j in near[k]:
-                    if en[j] > t:
-                        t = en[j]
-                t += w + dur[k]
-                free[e] = t
-                en[k] = t + lat[k]
-            res.append((en, snap))
-        return res
-
-    now = run(seq, 0, None)
-    base = [max(r[0]) for r in now]
-    wts = [WEIGHT[c] / base[c] / sum(WEIGHT) for c in range(len(costs))]
-    cur = top = 1.0
-    best_seq, pairs, pos = seq, None, None
-    for it in range(STEPS):
-        if pairs is None:
-            pairs = {}
-            pos = [0] * n
-            for j, k in enumerate(seq):
-                pos[k] = j
-        c = int(rng.integers(0, len(costs)))
-        if c not in pairs:
-            pairs[c] = tight(seq, near, eng, costs[c])
-        if not pairs[c]:
-            continue
-        a, b = pairs[c][int(rng.integers(0, len(pairs[c])))]
-        far = int(rng.integers(0, 2)) * int(rng.exponential(8.0))
-        if rng.random() < 0.5:
-            i0, i1 = max(0, pos[a] - far), pos[b] + 1
-            move = {b}
-            for k in reversed(seq[i0:i1]):
-                if k in move:
-                    move.update(near[k])
-            mid = [k for k in seq[i0:i1] if k in move] + [k for k in seq[i0:i1] if k not in move]
-        else:
-            i0, i1 = pos[a], min(n, pos[b] + 1 + far)
-            move = {a}
-            for k in seq[i0:i1]:
-                if k in move:
-                    move.update(after[k])
-            mid = [k for k in seq[i0:i1] if k not in move] + [k for k in seq[i0:i1] if k in move]
-        q = seq[:i0] + mid + seq[i1:]
-        res = run(q, i0, now)
-        e = sum(w * max(r[0]) for w, r in zip(wts, res))
-        if e < cur or rng.random() < np.exp((cur - e) / (HEAT * (1.0 - it / STEPS) + 1e-6)):
-            cur, seq, now, pairs = e, q, res, None
-            if e < top:
-                top, best_seq = e, q
-    return best_seq
-
-
-_ORDER = {}
-
-
-def plan(T, topo, core):
-    ops, nsent = build(T, topo, core, SETS[0])
-    depend(ops)
-    if "seq" not in _ORDER:
-        costs = []
-        for par in SETS:
-            o2 = build(T, topo, core, par)[0]
-            costs.append(([o["dur"] for o in o2], [o["lat"] for o in o2], par[1]))
-        _ORDER["seq"], _ORDER["costs"] = order(ops, costs), costs
-    return ops, nsent, _ORDER["seq"]
+        assert all(d in done for d in ops[k]["dep"])
+        done.add(k)
+    assert len(done) == len(seq) == len(ops)
+    return seq
 
 
 def rank_program(g, core, T, topo):
     if T.rank_of(core) is None:
         return
-    ops, nsent, seq = plan(T, topo, core)
+    ops, nsent = build(T, topo, core, SETS[0])
+    depend(ops)
+    seq = issue_order(ops)
     queue = {"v": g.vector, "s": g.scalar, "p": g.tensor, "g": g, "y": g.sync}
     csem = {"v": "cv", "s": "cs", "p": "cp", "g": "cg"}
     count = {}
@@ -804,15 +656,17 @@ def rank_program(g, core, T, topo):
         o = ops[k]
         e = o["e"]
         if o["kind"] == "arr":
-            o["sig"], o["clock"] = o["fn"], {}
-            count[o["fn"][0]] = o["fn"][1]
+            if o["fn"] is not None:
+                o["sig"], o["clock"] = o["fn"], {}
+                count[o["fn"][0]] = o["fn"][1]
             continue
         q, kn = queue[e], known[e]
+        dep = [d for d in o["dep"] if ops[d]["kind"] != "rem"]
         need = {}
-        for d in o["dep"]:
+        for d in dep:
             s, n = ops[d]["sig"]
             need[s] = max(need.get(s, 0), n)
-        for d in sorted(o["dep"], key=lambda j: -pos[j]):
+        for d in sorted(dep, key=lambda j: -pos[j]):
             s, n = ops[d]["sig"]
             if kn.get(s, 0) < n:
                 q.wait_ge(T.sem[s], need[s])
@@ -821,15 +675,13 @@ def rank_program(g, core, T, topo):
                 kn[s2] = max(kn.get(s2, 0), n2)
         ins = o["fn"](q)
         o["clock"] = dict(kn)
-        if o["kind"] == "rem":
-            o["sig"] = ("sent", 0)
-        elif o["kind"] == "dma":
+        if o["kind"] == "dma":
             s = "d%d" % ndma
             ndma += 1
             ins.then_inc(T.sem[s], 16)
             o["sig"] = (s, 16)
             count[s] = 16
-        else:
+        elif o["kind"] != "rem":
             s = csem[e]
             count[s] = count.get(s, 0) + 1
             ins.then_inc(T.sem[s], 1)

import numpy as np
from concourse.bass import DstId, RemoteDMATransfer
from concourse.mybir import dt, AluOpType, ActivationFunctionType

C, K, R = 384, 192, 3
F32, BF, F16, I32, U16, U8, X4 = "float32", "bfloat16", "float16", "int32", "uint16", "uint8", "float8_e4m3fn_x4"

FIB = [1, 2, 3, 5, 8, 13, 21, 34, 55, 89]
ZS = [(0, 208), (0, 240), (0, 304), (32, C)]
E = 1.0 / 512
W = 200
B, NB = 208, 204

SCRATCH = {}


def _decl(name, n, d, where="sbuf"):
    SCRATCH[name] = (where, [128, n], d)


for _t in range(R + 1):
    _decl("X%d" % _t, 4 * C, BF)
    _decl("QX%d" % _t, C, X4)
for _h in range(2):
    for _n, _w, _d in [("MK", K, F32), ("HD", K, F32), ("NEQ", 2 * K, BF), ("CMP", 12 * W, BF),
                       ("JK", 12 * W, BF), ("RK", 12 * 96, BF), ("AL", 24, F32), ("SC", K, F32),
                       ("OFF", 12, U16), ("ALV", K + 2, BF), ("DB", K + 2, F16), ("CM", K + 96, BF)]:
        _decl(_n + str(_h), _w, _d)
    _decl("PV%d" % _h, 512, F32, "psum")
    _decl("PS%d" % _h, 512, F32, "psum")
for _b in range(4):
    _decl("D%d" % _b, 512, F32, "psum")
for _n, _w, _d in [
    ("H", R * 1024, BF), ("QH", R * 256, X4), ("SH", R * 256, U8), ("LC", R * K, X4), ("LS", R * 256, U8),
    ("SX", (R + 1) * C, U8), ("U", 512, BF), ("QU", 128, X4), ("SU", 128, U8), ("QR", 128, X4), ("SR", 128, U8),
    ("WC", 512, X4), ("WS", 512, U8),
    ("ONES", 512, BF), ("EB", 2048, BF), ("QE", 512, X4), ("SE", 512, U8),
    ("PTR", 24, I32), ("PI", 16, I32), ("UL", 8, U16),
    ("COL", 24, F32), ("IOTA", K, F32), ("J16", K, BF), ("NGB", 12, F32),
    ("CMIN", 2 * K, BF), ("R16", 2 * K, BF), ("T1", 48, BF), ("A16", 24, U16),
    ("HOLD", C + K, BF), ("IOS", C + K, BF), ("TAB", 8, F32),
    ("SREV", K, F32), ("RS", K + 16, BF), ("IOQ", K, BF), ("BK", 6 * B, BF), ("KF", 2 * B, F32), ("KT", 104, F32),
    ("KI", 26, I32), ("TH", B, BF), ("KM", 28, U16), ("SM", 256, F32), ("PIV", 24, F32), ("IOX", 224, F32),
    ("CM2", K + 96, BF), ("J48", 64, F32), ("OL", 6, U16),
    ("PB", C, BF), ("FP", C + 2, BF), ("DF", C, BF), ("VV", C, BF), ("PN", K, BF), ("L64", 64, U16), ("EL", 16, U16),
    ("VH", 4 * K, BF), ("VH2", 4 * K, BF), ("TR", len(FIB) * C, BF), ("ZR", 2 * C, BF), ("AP", C, BF),
    ("PR", C, BF), ("PP", K, BF), ("PE", K, BF), ("PEL", 12, U16), ("J1", 60, U16), ("JL", len(FIB) * 24, U16),
    ("DA", C, F16), ("HSA", 3 * C, F16), ("HSB", 6 * K, BF), ("PL", K, F32), ("YB", C, F32),
    ("KS", 48, F32), ("KL", 12, U16), ("M0", 3 * K, BF), ("JR", 3 * K, BF), ("MR", 6 * K, BF),
    ("TB", 224, BF), ("TP", 432, BF), ("TG", K, BF), ("PS", K + 96, F32), ("NB", 3 * K, F16),
]:
    _decl(_n, _w, _d)

NDMA = 24
SEMAPHORES = ["cv", "cs", "cp", "cg", "sent"] + ["arr%d" % _t for _t in range(R)] + ["d%d" % _k for _k in range(NDMA)]

NS = {(0, 0): (0, 5), (0, 1): (0, 5), (1, 0): (0, 5), (1, 1): (0, 5), (2, 0): (0, 5), (2, 1): (0, 5)}
CP = {"relu": "svssvsvs", "dec": "svss", "last": "svsv", "jump": "sssvsvsvsvv", "vh": "svss", "vh2": "vsvv",
      "twin": "svs", "z": "g", "f0": "svs", "low": 160}

SETS = [(0.83, 250, 1.4, 3.4, 110, 800, 400, 27, 6, 0, 64, 10, 64, 1300),
        (0.83, 200, 1.55, 3.8, 150, 1300, 600, 20, 6, 0, 64, 30, 64, 2000),
        (1.2, 260, 1.8, 4.5, 200, 1000, 500, 18, 9, 0, 64, 30, 64, 1500),
        (1.0, 300, 1.2, 2.5, 130, 1500, 500, 20, 8, 0, 64, 10, 64, 1300),
        (1.1, 200, 1.5, 4.0, 200, 1000, 400, 20, 5, 20, 50, 50, 30, 1500)]
ORDER = (
    "06020N000M03010R1f080v0w0x0y07090A0E0J0z1g0Y0C0B0m0S0X1h0G0W130T0O0H1i0L0Z0P151I0a0U1k1j0I1K1J0t1L1F0Q101l1P1Q0K1n1m0V"
    "1s1N1o0D1R0n2w1p1O1M04051S2A0u1u2B1y1q2m2p0r281T2C271Y2a2s2g2j2n2D2q1W1U252t311V3d1E2W2Q222E2k1Z2f212d2F240p23342b2P2h"
    "2u2K2Y2N2o2r2l303a2c2i2S261X202e3718293e322M2v38392G2J1z2V3b332x0f2T2H2L3f1b2O2X3c2y36351d3h2z2I2U2R2Z3g111t0e1v0o193i"
    "0q1B3j0i121G1a3k3p0h3q3l3o3t4j4k0g3s3w3x0l4o4h4l3z3y4m0j3A4p4n0k3B3E3D3C4i0c4s3r3F3I3H4q1c3G3u3m3J3M3L143K4r4t3N3Q1A3P"
    "0d3O4u3n3R3U3T3v3S1w4A3V3Y3X4v1e3W4y4B0b3Z421741164440431H4548474a494I464b4w4d4e4c0F4z4x4g4f4E4G4K4F1C4C4H1r4L4J1D4M1x"
    "4D4P5k4O4Q5l534N5m5t5n4R54565u554S4W0s4U4Y5o4T574X4V4Z5p5v5J585q505a5e5c5L5K5w515f595b5d5r6q5M525g5x6g5h5N6d626m5T646j"
    "5i5s5O6e615y5Q5Z6n695j656k676a5z6f6l5Y6c5P5V6h666b5W5A6o5B6B6i5S6z5R636F5X5C68606D5U6p6C6A6G6r5F6E6s6t6x6H5G6v5D6w6I5H"
    "6J6u6M6K6W6N6L5E6X6O5I6y6P6Y6Q7i7r6S7o6Z6R7c7u6T7d7x7k7f7p6U737q7g70746V767w797l717H7z777E7s7D7t7h7I7n7a7F7m7G7v7J7e7y"
    "7j72857K7S7b78757A867T82847B7L7U7C7V887M8387897W7N7Q8a7X7R8b8d8c7O7Y8e7P7Z808f8g818h8i8k8j8s8o8m8q8t8l8p8n8u8r928v8M8y"
    "938x8w949b958z8O8N9c8L8A8E968C8G8B8P8F978D8H9d9r988Q8I8U8W8S9t9s8V8J8R8X9e8T9ua8998K8Y9va19f9Y8Z9V9G9S9H909w9Z9a9y9g9M"
    "a49R9J919T9Ka29h9Ua59E9x9X9Pa39i9ja09B9La69Daj9W9N9z9kal9A9Ian9Q9Faha79l9O9C9nama9akaoai9oaaabapaf9mac9paeaqadar9qasau"
    "aEatavaFawagaSaxaXayaUb3aVaAb6aGazbfaJaBaIb9aHbcaCaPbgb0b2aDaOb4aLbdaYaMb5bpbmb8blaZbabqbhaNb7bnbobbbraRbeaQb1bsbAaWaK"
    "aTbibKbBbNbMbjbtbCbObPbkbDbubQbVbLbRbEbvbybSbTbzbFbwbUbWbGbxbYbXbHbIbJc2bZc0c1cac6c4c8cbc3c7c5ccc9cdcgcfcecuctchcvcwcK"
    "cmcicockcxcncjclcpd1cAcyd0cCcXcEcLcqcBcVcYcZcDczcFcrcGcWcscHd2cIcJcQcOcMcScRcPcNcTcUd3d5d8d6d9d7d4da"
)


def build(T, topo, core, par):
    A, F = AluOpType, ActivationFunctionType
    CYC, _wake, GATH, SCAT, T_MM, T_REM, T_ISS, RATE, T_ROW, FV, MV, FS, MS, T_DMA = par
    rank = T.rank_of(core)
    nxt = T.cores[(rank + 1) % len(T.cores)]
    prv = T.cores[(rank - 1) % len(T.cores)]
    ops = []

    def v(name, a=0, b=None, s=1):
        return (name, a, SCRATCH[name][1][1] if b is None else b, s)

    def col(name, j):
        return (name, j, j + 1, 1)

    def sub(w, a, b, s=1):
        return (w[0], w[1] + a, w[1] + b, s)

    def ap(w):
        if isinstance(w, tuple) and w[0] == "ind":
            return ap(w[1]).indirect(ap(w[2]))
        if isinstance(w, tuple):
            return T[w[0]][:, w[1]:w[2]] if w[3] == 1 else T[w[0]][:, w[1]:w[2]:w[3]]
        return w

    def ind(win, off):
        return ("ind", win, off)

    def flat(ws):
        r = []
        for w in ws:
            if isinstance(w, tuple):
                r += [w[1], w[2]] if w[0] == "ind" else [w]
        return r

    def cnt(w):
        return 16 * cnt(w[2]) if w[0] == "ind" else len(range(w[1], w[2], w[3]))

    def two(w):
        return SCRATCH[w[0]][2] in (BF, U16, F16)

    def add(eng, fn, rd, wr, dur, kind="c", lat=0.0, after=()):
        ops.append({"e": eng, "fn": fn, "rd": flat(rd), "wr": flat(wr), "dur": dur, "kind": kind, "lat": lat,
                    "after": list(after), "k": len(ops)})
        return len(ops) - 1

    def vdur(out, ins, base=1.0, fast=True):
        if out[0] == "ind":
            return 50 + SCAT * CYC * cnt(out)
        if ins[0][0] == "ind":
            return 50 + GATH * CYC * cnt(out)
        h = 0.5 if fast and all(two(w) for w in [out] + ins) else base
        return FV + CYC * max(MV, h * cnt(out))

    def copy(out, in_):
        if out[0] == "ind":
            return add("v", lambda q: q.tensor_copy(ap(out), ap(in_)), [in_, out[2]], [out[1]], vdur(out, [in_]))
        return add("v", lambda q: q.tensor_copy(ap(out), ap(in_)), [in_], [out], vdur(out, [in_]))

    def turn32(out, in_):
        return add("v", lambda q: q.transpose(ap(out), ap(in_)), [in_], [out], vdur(out, [in_]))

    def fill(out, c):
        return add("v", lambda q: q.memset(ap(out), c), [], [out], CYC * max(64, cnt(out)))

    def ts(out, in0, s1, op0, s2=None, op1=None):
        if op1 is None:
            fn = lambda q: q.tensor_scalar(ap(out), ap(in0), ap(s1), None, op0)
        else:
            fn = lambda q: q.tensor_scalar(ap(out), ap(in0), ap(s1), ap(s2), op0, op1)
        return add("v", fn, [in0, s1, s2], [out], vdur(out, [in0]))

    def tt(out, in0, in1, op):
        ps = any(w[0] != "ind" and SCRATCH[w[0]][0] == "psum" for w in (in0, in1))
        return add("v", lambda q: q.tensor_tensor(ap(out), ap(in0), ap(in1), op), [in0, in1], [out],
                   vdur(out, [in0, in1], 1.0 if ps else 2.0, False))

    def scan(out, d0, d1, init, op0, op1):
        return add("v", lambda q: q.tensor_tensor_scan(ap(out), ap(d0), ap(d1), ap(init), op0, op1), [d0, d1, init],
                   [out], vdur(out, [d0, d1]))

    def act(out, in_, func, bias=None, scale=None, acc=None):
        kw = {}
        if bias is not None:
            kw["bias"] = ap(bias)
        if scale is not None:
            kw["scale"] = scale
        if acc is not None:
            kw["accum_out"] = ap(acc)
        d = (65 + GATH * CYC * cnt(out) if in_[0] == "ind" else CYC * max(MS, cnt(out)) + FS) + (25 if acc else 0)
        return add("s", lambda q: q.activation(ap(out), ap(in_), func, **kw), [in_, bias], [out, acc], d)

    def gather(out, win, off):
        return act(out, ind(win, off), F.Copy)

    def take(e, out, win, off):
        return gather(out, win, off) if e == "s" else copy(out, ind(win, off))

    def quant(qc, qs, in_):
        return add("v", lambda q: q.quantize_mx(ap(qc), ap(qs), ap(in_)), [in_], [qc, qs],
                   CYC / 0.83 * (12 + 0.22 * cnt(in_)))

    def mm(bank, lc, ls, rc, rs):
        out = v(bank, 0, cnt(rc))
        return add("p", lambda q: q.matmul_mx(ap(out), ap(lc), ap(ls), ap(rc), ap(rs), True, True), [lc, ls, rc, rs],
                   [out], T_MM * (cnt(rc) + 16) / 208.0)

    def iota(out, pattern, base, cm=0):
        if SCRATCH[out[0]][2] == I32:
            fn = lambda q: q.iota(ap(out), pattern, base, cm)
        else:
            fn = lambda q: q.iota(ap(out), pattern, base, cm, allow_small_or_imprecise_dtypes=True)
        return add("g", fn, [], [out], 160 + 2 * CYC * cnt(out))

    def select(out, in_, pattern, op, c, base, cm=0):
        return add("g", lambda q: q.affine_select(ap(out), ap(in_), pattern, op, c, base, cm), [in_], [out],
                   200 + 2 * CYC * cnt(out))

    def twin(e, out, in_):
        if e == "g":
            return select(out, in_, [[0, cnt(out)]], A.is_ge, 0.0, 0)
        return act(out, in_, F.Copy) if e == "s" else copy(out, in_)

    def dma(eng, out, in_, rd, wr, nbytes, after=()):
        return add(eng, lambda q: q.dma_start(out, in_), rd, wr, 100.0, "dma", T_DMA + nbytes / 200.0, after)

    def u8(w):
        return ap(w).bitcast(dt.uint8)

    rid, pid, _e = topo.addr(nxt)
    mask = topo.mask(core, nxt)
    eng = topo.engines(core, nxt)
    sends = []
    halves = [sum(1 << e for e in eng[:len(eng) // 2]), sum(1 << e for e in eng[len(eng) // 2:])]

    def send(pairs, sem, width):
        if len(pairs) == 1:
            fn = lambda q: q.remote_dma(pairs[0][1], pairs[0][0], T.sem[sem], T.sem["sent"], pid, rid, mask)
        else:
            fn = lambda q: q.remote_dma_fused(
                [RemoteDMATransfer(dst_ids=[DstId(rid=rid, pnc=pid)], dma_engine_mask=m, remote_sem=T.sem[sem],
                                   src=p[0], dst=p[1]) for m, p in zip(halves, pairs)], local_sem=T.sem["sent"])
        k = add("g", fn, [p[2] for p in pairs], [], T_ISS, "rem", after=[x[0] for x in sends[-1:]])
        w = add("r", None, [], [], 16 * len(pairs) * (T_ROW + width / RATE), "arr", after=[k] + [x[1] for x in sends[-1:]])
        sends.append((k, w))

    dma("s", ap(v("U")), T.u[:], [], [v("U")], 131072)
    dma("s", ap(v("PTR")), T.ptr[:], [], [v("PTR")], 12288)
    xa = dma("y", ap(v("X0", 0, 4 * K)), T.x[:, 0:4 * K], [], [v("X0", 0, 4 * K)], 262144)
    xb = dma("y", ap(v("X0", 4 * K)), T.x[:, 4 * K:4 * C], [], [v("X0", 4 * K)], 458752)
    dma("y", u8(v("WC")), T.wc[:], [], [v("WC")], 262144, after=[xa, xb])
    dma("y", ap(v("WS")), T.ws[:], [], [v("WS")], 65536, after=[xa, xb])

    pc, ai, gi, i16 = col("PI", 0), col("PI", 1), col("PI", 3), v("PI", 8, 16)
    j16 = v("J16")
    ios, iop = v("IOS", 0, C), v("IOS", C, C + K)
    cmin, cm0, r16, keep = v("CMIN", 0, K), v("CMIN", K, 2 * K), v("R16", 0, K), v("R16", K, 2 * K)
    holdc, holdd = v("HOLD", 0, C), v("HOLD", C, C + K)
    iota(pc, [[0, 1]], 0, 1)
    iota(i16, [[16, 8]], 0)
    iota(j16, [[0, 12], [1, 16]], 0)
    iota(v("IOTA"), [[1, K]], 0)
    iota(v("NGB"), [[-16, 12]], -16)
    t01 = v("TAB", 0, 2)
    iota(t01, [[1, 2]], 0)
    iota(v("IOX"), [[1, 224]], 0)
    iota(v("SM", 0, 16), [[0, 16]], 0)
    for h in range(2):
        iota(col("ALV%d" % h, 0), [[0, 1]], 0)
    for t in range(R):
        iota(v("X%d" % (t + 1), 4 * K, 1024), [[0, 256]], 0)
        iota(v("H", 1024 * t + 4 * K, 1024 * t + 1024), [[0, 256]], 0)
    iota(v("ONES"), [[0, 512]], 1)
    for b in range(4):
        eb = v("EB", 512 * b, 512 * b + 512)
        select(eb, v("ONES"), [[-1, 512]], A.is_equal, 0.0, b, 4)
        quant(v("QE", 128 * b, 128 * b + 128), v("SE", 128 * b, 128 * b + 128), eb)
    (a0, a1, f7, ns1, nb16, thr0, thr, cf, cfk, gam,
     piv2, ns2, cst, pnc, cf2, up0, n1, n2, n1h, fc, fd, ns0, cj) = [col("COL", j) for j in range(23)]
    ts(ai, pc, 15, A.bitwise_and)
    ts(gi, pc, 4, A.arith_shift_right, 1, A.bitwise_and)
    copy(a0, ai)
    copy(gam, gi)
    ts(a1, a0, 1.0, A.add)
    ts(f7, a0, 15.0, A.is_lt, float(C), A.mult)
    ts(fc, f7, float(K), A.add, E, A.mult)
    ts(fd, f7, 0.5 * E, A.mult, -E, A.add)
    ts(ns1, a0, 4096.0, A.mult, 4096.0, A.add)
    ts(ns0, a0, -4096.0, A.mult, 256.0, A.add)
    ts(cj, a0, 16.0, A.mult, 31.0, A.add)
    ts(nb16, a0, -0.0625, A.mult, 31.0 / 16, A.add)
    ts(thr0, a0, 16.0, A.mult, 15.5, A.add)
    ts(thr, thr0, K - 0.5, A.min)
    ts(cf, a0, -1.0, A.mult, 2071.5, A.add)
    ts(cfk, cf, float(K), A.add)
    copy(col("FP", 0), cf)
    for h in range(2):
        fill(col("DB%d" % h, 0), -E)
    act(sub(ios, 0, K), v("IOTA"), F.Copy, scale=E, bias=-K * E)
    act(sub(ios, K, C), v("IOTA"), F.Copy, scale=E)
    act(iop, v("IOTA"), F.Copy, scale=E, bias=E)
    fill(v("SM", K + 16, 256), 2.0 ** 96)
    copy(v("UL"), i16)
    ts(cm0, j16, a0, A.is_equal, 0.5, A.subtract)
    ts(cmin, cm0, 2.0 ** 97, A.mult)
    ts(r16, j16, 0.5, A.subtract, 2.0 ** 97, A.mult)
    ts(keep, j16, 1.0, A.min)
    ts(v("A16"), v("J16", 0, 24), 0.0, A.mult, a0, A.add)
    ts(v("T1", 0, 16), v("J16", 0, 16), a0, A.is_equal, 1024.0 * E, A.mult)
    ts(v("T1", 16, 32), v("J16", 0, 16), a1, A.is_equal, -C * E, A.mult)
    tt(v("T1", 32, 48), v("T1", 0, 16), v("T1", 16, 32), A.add)
    gather(holdc, v("T1", 32, 48), v("A16"))
    act(holdd, sub(holdc, 0, K), F.Copy, scale=0.5)
    dma("y", T.pl[:, K:C], T["IOTA"][0:128:16, 0:K], [v("IOTA")], [], 6144)
    odd, kb, mk1, kc = v("KS", 0, 12), v("KS", 12, 24), v("KS", 24, 36), v("KS", 36, 48)
    iota(v("TB"), [[0, 224]], 0)
    act(v("IOQ"), v("IOTA"), F.Copy, scale=1.0 / 256)
    iota(v("RS", K, K + 16), [[0, 16]], 1)
    iota(v("TP", 416, 432), [[2, 16]], 4)
    bk = [v("BK", B * j, B * j + B) for j in range(6)]
    kf = [v("KF", B * j, B * j + B) for j in range(2)]
    iota(kf[0], [[16, 13], [1, 16]], 0)
    iota(sub(kf[0], 0, NB), [[16, 12], [1, 17]], 0)
    act(bk[2], kf[0], F.Copy, scale=E)
    iota(bk[0], [[0, B]], 29)
    iota(sub(bk[0], 0, NB), [[2, 12], [0, 17]], 5)
    iota(bk[1], [[0, B]], 1)
    iota(sub(bk[1], 0, NB, 17), [[0, 12]], -1)
    ii, bf, b17, z17, base, u0, p2, u1 = [v("KT", 13 * j, 13 * j + 13) for j in range(8)]
    bi, pi_ = v("KI", 0, 13), v("KI", 13, 26)
    km = [v("KM", 14 * j, 14 * j + 13) for j in range(2)]
    iota(ii, [[16, 13]], 0)
    ts(ii, ii, a0, A.add)
    ts(bf, ii, 1.0 / 17, A.mult, -0.47, A.add)
    copy(bi, bf)
    copy(bf, bi)
    ts(pi_, bi, 1, A.bitwise_and)
    copy(p2, pi_)
    tt(base, ii, bf, A.subtract)
    ts(b17, bf, 17.0, A.mult)
    tt(z17, b17, ii, A.is_equal)
    ts(b17, z17, K + 1.0, A.mult)
    tt(u0, base, b17, A.max)
    ts(km[0], u0, -1.0, A.add)
    ts(p2, p2, gam, A.not_equal, float(K + 16), A.mult)
    tt(u1, base, p2, A.add)
    ts(z17, z17, 417.0, A.mult)
    tt(z17, z17, bf, A.add)
    tt(u1, u1, z17, A.max)
    ts(km[1], u1, -1.0, A.add)
    iota(odd, [[0, 6], [1, 2]], 0)
    iota(kb, [[16, 12]], 0)
    iota(mk1, [[2, 12]], 4)
    ts(odd, odd, gam, A.not_equal, float(K + 16), A.mult)
    tt(kc, odd, kb, A.add)
    ts(v("KL"), kc, a0, A.add)
    m0, m1, mb = [v("M0", K * j, K * j + K) for j in range(3)]
    iota(mb, [[2, 12], [0, 16]], 4)
    act(m1, cm0, F.Copy, scale=31.0, bias=16.5)
    tt(m0, m1, mb, A.min)
    twin("g", m1, m0)

    quant(v("QU"), v("SU"), v("U"))
    add("v", lambda q: q.tensor_copy(ap(v("QR")).bitcast(dt.uint32), ap(v("QU")).bitcast(dt.uint32).indirect(ap(v("UL")))),
        [v("QU"), v("UL")], [v("QR")], 50 + GATH * CYC * 128)
    gather(v("SR"), v("SU"), v("UL"))

    def half(t, h):
        return (v("QX%d" % t, K * h, K * h + K), v("SX", C * t + K * h, C * t + K * h + K),
                v("X%d" % t, 4 * K * h, 4 * K * h + 4 * K))

    def scores(t, h):
        qc, qs, _x = half(t, h)
        mm("PV%d" % h, v("QR"), v("SR"), qc, qs)
        mm("PS%d" % h, v("QR"), v("SR"), qc, qs)

    def ranks(t, h):
        s = str(h)
        pv, ps = v("PV" + s, 0, K), v("PS" + s, 0, K)
        neq, nqs = v("NEQ" + s, 0, K), v("NEQ" + s, K, 2 * K)
        tt(v("MK" + s), pv, cmin, A.min)
        scan(v("HD" + s), r16, v("MK" + s), 0.0, A.min, A.max)
        tt(neq, pv, v("HD" + s), A.not_equal)
        scan(nqs, keep, neq, 0.0, A.mult, A.add)
        b0, b1 = NS[(t, h)]
        for b in list(range(b0)) + list(range(b1, 12)):
            w, n, o = col("HD" + s, 16 * b + 15), 16 * b + 16, W * b
            ts(v("CMP" + s, o, o + n), v("PV" + s, 0, n), w, A.is_ge)
            if n < K:
                ts(v("CMP" + s, o + n, o + K), v("PV" + s, n, K), w, A.is_gt)
            scan(v("RK" + s, 96 * b, 96 * b + 96), v("CMP" + s, o, o + 96), v("CMP" + s, o + 96, o + K),
                 sub(nqs, 16 * b + 15, 16 * b + 16), A.add, A.add)
        tt(v("CMP" + s, K + W * b0, W * b1, W), v("NGB", b0, b1), sub(nqs, 16 * b0 + 15, 16 * b1, 16), A.subtract)
        for b in range(b0, b1):
            n, o = 16 * b + 16, W * b
            act(v("CMP" + s, o, o + K), ps, F.Sign, bias=col("HD" + s, 16 * b + 15), scale=-1.0)
            act(v("JK" + s, o, o + n), v("CMP" + s, o, o + n), F.Relu, acc=col("AL" + s, b))
            act(v("JK" + s, o + n, o + K + 1), v("CMP" + s, o + n, o + K + 1), F.Relu, scale=-1.0, acc=col("AL" + s, 12 + b))
        tt(v("RK" + s, 96 * b0 + 95, 96 * b1, 96), v("AL" + s, 12 + b0, 12 + b1), v("AL" + s, b0, b1), A.subtract)
        rk, off = v("RK" + s, 95, 12 * 96, 96), v("OFF" + s)
        if h == 0 or t == 0:
            act(v("SC" + s), ps, F.Copy)
        if h == 0:
            ts(off, rk, -1.0, A.mult, float(K - 1 + 16), A.add)
            copy(ind(v("SREV"), off), v("SC0"))
            gather(v("RS", 0, K), v("IOQ" if t else "IOTA"), off)
            if t > 0:
                for j in range(2):
                    scan(v("PIV", 12 * j, 12 * j + 12), sub(cmin, j, j + 12), v("SREV", 15, K, 16), 0.0, A.max, A.min)
                scan(v("SM", 16, K + 16), cmin, v("SREV"), 0.0, A.max, A.min)
                act(kf[1], ind(v("RS"), km[0]), F.Copy, bias=1.0)
                scan(bk[4], kf[1], bk[3], 0.0, A.max, A.subtract)
        else:
            ts(off, rk, -16.0, A.add)

    def search():
        pv = v("PV1", 0, K)
        for cm, pivot, w, start in (("CM0", col("PIV", 11), -256.0, ns1), ("CM2", col("PIV", 23), 256.0, ns0)):
            ts(v(cm, 0, K), pv, pivot, A.is_gt, w, A.mult)
            scan(v(cm, K, K + 96), v(cm, 0, 96), v(cm, 96, K), start, A.add, A.add)
        ol = col("OL", 0)
        ts(ol, cj, col("CM0", K + 95), A.min, col("CM2", K + 95), A.min)
        act(v("J48", 0, 16), ind(v("SM"), ol), F.Identity, acc=piv2)
        act(v("J48", 16, 32), ind(v("IOX"), ol), F.Identity, scale=-1.0, bias=nb16, acc=ns2)
        act(v("J48", 48, 64), ind(v("IOX"), ol), F.Identity, scale=1.0 / 4096, bias=-31.0 / 65536, acc=cst)
        ts(v("CM1", 0, K), pv, piv2, A.is_gt)
        scan(v("CM1", K, K + 96), v("CM1", 0, 96), v("CM1", 96, K), ns2, A.add, A.add)
        ol = col("OL", 2)
        ts(ol, col("CM1", K + 95), 1.0, A.min)
        act(v("J48", 32, 48), ind(t01, ol), F.Identity, scale=1.0 / 256, bias=cst, acc=pnc)

    turn = [0]

    def to_list(t, out, rep):
        turn[0] = (turn[0] + 1) % 6
        n = cnt(rep)
        buf, o, hold, f = ("HSA", C * (turn[0] % 3), holdc, fc) if t == 0 else ("HSB", K * turn[0], holdd, fd)
        scan(v(buf, o, o + n), sub(hold, 0, n), rep, 0.0, A.add, A.min)
        ts(out, v(buf, o + 15, o + n, 16), f, A.add, 1.0 / E, A.mult)

    def climb():
        def both(out, win, k, c0, c1):
            for e, a, b in (("v", c0, CP["low"]), ("s", CP["low"], c1)):
                take(e, sub(out, a, b), sub(win, 0, b), v("JL", 24 * k + a // 16, 24 * k + b // 16))

        tr = [v("TR", C * k, C * k + C) for k in range(len(FIB))]
        z = [v("ZR", 0, C), v("ZR", C, 2 * C)]
        for a in (K, 0):
            tt(sub(tr[0], a, a + K), ind(ios, v("J1", a // 16, a // 16 + 12)), v("AP", a, a + K), A.max)
        tt(tr[1], ind(tr[0], v("J1", 0, 24)), v("AP"), A.max)
        n = len(FIB)
        for k in range(n + 2):
            if 2 <= k < n:
                both(tr[k], tr[k - 1], k - 2, 0, C)
            i = k - (n + 2 - len(ZS))
            if i >= 0:
                both(z[1 - i % 2], z[i % 2], k - 2, *ZS[i])
            if k < n:
                to_list(0, v("JL", 24 * k, 24 * k + 24), tr[k])
        return z[0]

    def blocks(p1):
        j = {d: v("J1", 12 * i, 12 * i + 12) for i, d in enumerate((1, 2, 4, 8))}
        p = {1: p1, 2: v("JR", 0, K), 4: v("JR", K, 2 * K), 8: v("JR", 2 * K, 3 * K)}
        for d in (2, 4, 8):
            gather(p[d], p[d // 2], j[d // 2])
            to_list(1, j[d], p[d])
        m = {1: (m0, m1), 16: (v("TB", 16, 16 + K), None)}
        for i, d in enumerate((2, 4, 8, 16)):
            if d < 16:
                m[d] = (v("MR", 2 * K * i, 2 * K * i + K), v("MR", 2 * K * i + K, 2 * K * i + 2 * K))
            tt(m[d][0], ind(m[d // 2][0], j[d // 2]), m[d // 2][1], A.max)
            if d < 16:
                twin(CP["twin"][i], m[d][1], m[d][0])
        turn32(v("TP", 0, K), m[16][0])
        turn32(v("TP", K, 416), v("TB"))
        gather(v("TG"), v("TP", 0, 416), v("KL"))
        gather(v("TH"), v("TP"), km[1])
        scan(bk[3], bk[0], v("TH"), 0.0, A.max, A.subtract)
        scan(v("PS", 0, K), p1, v("TG"), 0.0, A.max, A.subtract)
        scan(v("PS", K, K + 96), v("PS", 0, K, 2), v("PS", 1, K, 2), 0.0, A.min, A.min)
        tt(sub(bk[2], 0, NB, 17), v("PS", K + 7, K + 96, 8), mk1, A.add)
        scan(bk[5], bk[1], bk[2], 0.0, A.min, A.max)

    def jump(pn):
        ts(v("NB", 0, B), bk[4], pn, A.is_ge)
        scan(v("NB", B, 2 * B), v("NB", 0, B), bk[5], 0.0, A.add, A.min)
        l = {d: v("JL", 12 * i, 12 * i + 12) for i, d in enumerate((1, 3))}
        r = {d: v("TR", K * d, K * d + K) for d in (1, 2, 3)}
        z = [v("ZR", K, C), v("ZR", C, C + K)]
        e = CP["jump"]
        ts(l[1], v("NB", B + 16, B + NB, 17), 1.0 / E, A.mult, -1.0, A.add)
        take(e[0], r[1], iop, l[1])
        take(e[1], r[2], r[1], l[1])
        take(e[2], r[3], r[2], l[1])
        take(CP["f0"][2], v("TR", 0, 64), r[3], v("J1", 8, 12))
        to_list(1, v("JL", 24, 28), v("TR", 0, 64))
        to_list(1, sub(l[3], 4, 12), sub(r[3], 64, K))
        for i, (d, c0, c1) in enumerate(((1, 0, 1), (1, 0, 2), (1, 0, 3), (1, 2, 4), (1, 2, 5), (1, 4, 6),
                                         (3, 4, 9), (3, 6, 12))):
            take(e[3 + i], sub(z[1 - i % 2], 16 * c0, 16 * c1), z[i % 2], sub(l[d], c0, c1))
        take(CP["f0"][0], v("ZR", 0, 128), z[1], v("J1", 0, 8))
        take(CP["f0"][1], v("ZR", 128, K), z[1], v("JL", 24, 28))
        return v("ZR", 0, C)

    quant(*half(0, 0))
    quant(*half(0, 1))
    copy(v("J1", 0, 24), v("PTR"))
    gather(v("PR"), ios, v("J1", 0, 24))
    scores(0, 0)
    ranks(0, 0)
    for t in range(R):
        X, Xn = "X%d" % t, "X%d" % (t + 1)
        scores(t, 1)
        al = [v("ALV%d" % h, 1, K + 1) for h in range(2)]
        if t == 0:
            ranks(t, 1)
            tt(al[1], ind(v("SREV"), v("OFF1")), v("SC1"), A.is_lt)
            scan(v("PN"), al[1], al[1], 0.0, A.add, A.max)
            pn = col("PN", K - 1)
        else:
            search()
            ranks(t, 1)
            pn = pnc
            ts(al[1], ind(v("IOQ"), v("OFF1")), pn, A.is_lt)
        rs = v("RS", 0, K)
        ts(al[0], rs, pn, A.is_ge)
        ts(v("DA", 0, K), rs, pn, A.is_ge, 1.0 - E, A.mult)
        zo = K if t else 0
        scan(v("ZR", zo, zo + K), v("ALV0", 0, K), v("DA", 0, K), 1.0, A.add, A.subtract)
        if t == 0:
            ts(v("DB0", 1, K + 1), rs, pn, A.is_ge, E, A.subtract)
            ts(v("DB1", 1, K + 1), al[1], E, A.subtract)
            ts(v("DA", K, C), al[1], 1.0 - E, A.mult)
            ts(up0, pn, -E, A.mult, K * E + 1.0, A.add)
            scan(v("AP", 0, K), al[0], v("DB0", 0, K), -1.0 - (K + 1) * E, A.add, A.subtract)
            scan(v("AP", K, C), al[1], v("DB1", 0, K), -1.0 - E, A.add, A.subtract)
            scan(v("ZR", K, C), v("ALV1", 0, K), v("DA", K, C), up0, A.add, A.subtract)
            twin(CP["z"], v("ZR", C, 2 * C), v("ZR", 0, C))
            found = climb()
        else:
            scan(v("ZR", C, C + K), v("ALV0", 0, K), v("DA", 0, K), 1.0, A.add, A.subtract)
            found = jump(pn)
        scan(v("PB", 0, K), al[0], al[0], 0.0, A.add, A.max)
        scan(v("PB", K, C), al[1], al[1], col("PB", K - 1), A.add, A.max)
        ts(cf2, pn, -256.0 if t else -1.0, A.mult, cfk, A.add)
        for h in range(2):
            fp = v("FP", K * h + 1, K * h + K + 1)
            scan(fp, al[h], al[h], (cf, cf2)[h], A.add, A.max)
            scan(v("DF", K * h, K * h + K), fp, v("FP", K * h, K * h + K), 0.0, A.max, A.subtract)
            act(v("JK%d" % h, 0, K), v("PB", K * h, K * h + K), F.Sign, bias=thr, scale=-1.0, acc=(n1, n2)[h])
            scan(v("VV", K * h, K * h + K), v("DF", K * h, K * h + K), sub(ios, K * h, K * h + K),
                 (-K * E, col("VV", K - 1))[h], A.add, A.min)
        ts(n1h, n1, 0.5, A.mult, float(K), A.add)
        at = col("OL", 4)
        ts(at, n2, 0.5, A.mult, n1h, A.add)
        ts(v("EL"), ind(v("VV"), at), 1.0 / E, A.mult, float(K), A.add)
        pel = v("EL", 0, 12)
        if t == 0:
            gather(v("PE"), v("PR"), pel)
            to_list(t, v("PEL"), v("PE"))
            pel = v("PEL")
        ts(v("L64", 0, 16), ind(v("VV"), at), 4.0 / E, A.mult, float(4 * K), A.add)
        for j in range(1, 4):
            ts(v("L64", 16 * j, 16 * j + 12), v("EL", 0, 12), 4.0, A.mult, float(j), A.add)
        for j in range(4):
            src, o = ind(v(X), v("L64", 16 * j, 16 * j + 12)), v("VH", K * j, K * j + K)
            if CP["vh"][j] == "s":
                act(o, src, F.Copy, scale=0.5)
            else:
                ts(o, src, 0.5, A.mult)
            twin(CP["vh2"][j], v("VH2", K * j, K * j + K), o)
        p1 = v("PP")
        tt(p1, ind(found, pel), iop, A.min)
        to_list(1, v("J1", 0, 12), p1)
        l0, g0, h0, arr = K * t, 256 * t, 1024 * t, "arr%d" % t
        for i, (c0, c1) in enumerate(((0, 128), (128, K))):
            for j in range(4):
                tt(v(Xn, 4 * c0 + j, 4 * c1, 4), ind(v("VH", K * j, K * j + c1), v("J1", c0 // 16, c1 // 16)),
                   v("VH2", K * j + c0, K * j + c1), A.add)
            qc, qs = v("QX%d" % (t + 1), c0, c0 + 128), v("SX", C * (t + 1) + c0, C * (t + 1) + c0 + 128)
            quant(qc, qs, v(Xn, 4 * c0, 4 * c0 + 512))
            for b in range(4):
                bank = "D%d" % b if i == 0 else ("PV1", "PS1", "D0", "D1")[b]
                mm(bank, v("WC", 128 * b, 128 * b + 128), v("WS", 128 * b, 128 * b + 128), qc, qs)
                o, src = v("H", h0 + 4 * c0 + b, h0 + 4 * c1, 4), v(bank, 0, c1 - c0)
                if CP["relu"][4 * i + b] == "s":
                    act(o, src, F.Relu, scale=0.03125)
                else:
                    ts(o, src, 0.0, A.max, 0.03125, A.mult)
            quant(v("QH", g0 + c0, g0 + c0 + 128), v("SH", g0 + c0, g0 + c0 + 128), v("H", h0 + 4 * c0, h0 + 4 * c0 + 512))
            qh, sh = v("QH", g0 + c0, g0 + c1), v("SH", g0, g0 + 256)
            send([(u8(qh), u8(v("LC", l0 + c0, l0 + c1)), qh)] + ([(ap(sh), ap(v("LS", g0, g0 + 256)), sh)] if i else []),
                 arr, 4 * (c1 - c0))
        lc, ls = v("LC", l0, l0 + K), v("LS", g0, g0 + K)
        add("a", (arr, 2 * len(topo.engines(prv, core))), [], [lc, ls], 0.0, "arr", T_REM, after=[sends[-1][1]])
        if t + 1 < R:
            blocks(p1)
            scores(t + 1, 0)
            ranks(t + 1, 0)
        else:
            ts(v("PL"), p1, 1.0 / E, A.mult, -1.0, A.add)
            dma("y", T.pl[:, 0:K], T["PL"][0:128:16, 0:K], [v("PL")], [], 6144)
        ed = CP["dec"] if t + 1 < R else CP["last"]
        for b in range(4):
            mm("D%d" % b, v("QE", 128 * b, 128 * b + 128), v("SE", 128 * b, 128 * b + 128), lc, ls)
            o, src = v(Xn, 4 * K + b, 4 * C, 4), v("D%d" % b, 0, K)
            if ed[b] == "s":
                act(o, src, F.Copy)
            else:
                copy(o, src)
        quant(*half(t + 1, 1))

    for h in range(2):
        qc, qs, _x = half(R, h)
        mm("PV%d" % h, v("QU"), v("SU"), qc, qs)
        yb = v("YB", K * h, K * h + K)
        copy(yb, v("PV%d" % h, 0, K))
        dma("y", T.oc[:, 4 * K * h:4 * K * h + 4 * K], u8(qc), [qc], [], 98304)
        for k in range(4):
            dma("y" if (h == 0 or k < 2) else "s", T.osc[4 * k:4 * k + 4, K * h:K * h + K],
                T["SX"][32 * k:32 * k + 4, C * R + K * h:C * R + K * h + K], [qs], [], 768)
        dma("y" if h == 0 else "s", T.y[:, K * h:K * h + K], ap(yb), [yb], [], 98304)
    return ops, len(eng) * len(sends)


def depend(ops):
    seen, anc = {}, []
    for o in ops:
        dep = set(o["after"])
        for isw, ws in ((False, o["rd"]), (True, o["wr"])):
            for w in ws:
                psum = SCRATCH[w[0]][0] == "psum"
                m = np.zeros(SCRATCH[w[0]][1][1], bool)
                m[w[1]:w[2]:w[3]] = True
                for (k, pw, pm, pe) in seen.get(w[0], []):
                    if k != o["k"] and ((psum and pe != o["e"]) or ((isw or pw) and bool((m & pm).any()))):
                        dep.add(k)
                seen.setdefault(w[0], []).append((o["k"], isw, m, o["e"]))
        o["dep"] = sorted(dep)
        near, m = [], 0
        for d in reversed(o["dep"]):
            if not (m >> d) & 1:
                near.append(d)
                m |= anc[d] | (1 << d)
        anc.append(m)
        o["near"] = near


def issue_order(ops):
    ch = "0123456789abcdefghijklmnopqrstuvwxyzABCDEFGHIJKLMNOPQRSTUVWXYZ"
    seq = [ch.index(ORDER[i]) * 62 + ch.index(ORDER[i + 1]) for i in range(0, len(ORDER), 2)]
    done = set()
    for k in seq:
        assert all(d in done for d in ops[k]["dep"])
        done.add(k)
    assert len(done) == len(seq) == len(ops)
    return seq


def rank_program(g, core, T, topo):
    if T.rank_of(core) is None:
        return
    ops, nsent = build(T, topo, core, SETS[0])
    depend(ops)
    seq = issue_order(ops)
    queue = {"v": g.vector, "s": g.scalar, "p": g.tensor, "g": g, "y": g.sync}
    csem = {"v": "cv", "s": "cs", "p": "cp", "g": "cg"}
    count = {}
    known = {e: {} for e in queue}
    pos = {k: j for j, k in enumerate(seq)}
    ndma = 0
    for k in seq:
        o = ops[k]
        e = o["e"]
        if o["kind"] == "arr":
            if o["fn"] is not None:
                o["sig"], o["clock"] = o["fn"], {}
                count[o["fn"][0]] = o["fn"][1]
            continue
        q, kn = queue[e], known[e]
        dep = [d for d in o["dep"] if ops[d]["kind"] != "rem"]
        need = {}
        for d in dep:
            s, n = ops[d]["sig"]
            need[s] = max(need.get(s, 0), n)
        for d in sorted(dep, key=lambda j: -pos[j]):
            s, n = ops[d]["sig"]
            if kn.get(s, 0) < n:
                q.wait_ge(T.sem[s], need[s])
                kn[s] = need[s]
            for s2, n2 in ops[d]["clock"].items():
                kn[s2] = max(kn.get(s2, 0), n2)
        ins = o["fn"](q)
        o["clock"] = dict(kn)
        if o["kind"] == "dma":
            s = "d%d" % ndma
            ndma += 1
            ins.then_inc(T.sem[s], 16)
            o["sig"] = (s, 16)
            count[s] = 16
        elif o["kind"] != "rem":
            s = csem[e]
            count[s] = count.get(s, 0) + 1
            ins.then_inc(T.sem[s], 1)
            o["sig"] = (s, count[s])
    g.wait_ge(T.sem["sent"], nsent)
    for s, n in count.items():
        if max(known[e].get(s, 0) for e in queue) < n:
            g.sync.wait_ge(T.sem[s], n)
